import numpy as np, ml_dtypes
CORES = [36,164,52,180,100,228,116,244]
N = 8
import mx_ref
BF = ml_dtypes.bfloat16
def cut(t, i, w=512):
    return t[:, w * i:w * i + w]
def pick(q, e):
    c = np.concatenate([q[0].reshape(128, -1, 4), np.zeros((128, 1, 4), np.uint8)], axis=1); s = np.concatenate([q[1], np.ones((16, 1), np.uint8)], axis=1)
    return (np.ascontiguousarray(c[:, e].reshape(128, -1)), np.ascontiguousarray(s[:, e]))
def join(*qs):
    return (np.concatenate([q[0] for q in qs], axis=1), np.concatenate([q[1] for q in qs], axis=1))
def put(q, e, v):
    c, s = q[0].reshape(128, -1, 4).copy(), q[1].copy(); c[:, e] = v[0].reshape(128, -1, 4); s[:, e] = v[1]
    return (c.reshape(128, -1), s)
def pk(c, s):
    return (np.ascontiguousarray(c), mx_ref.live(s))
def emit(q):
    return q[0], q[1]
def decode(q):
    o = []
    for b in range(4):
        e = np.zeros((128, 128, 4), np.float32); e[np.arange(128), np.arange(128), b] = 1
        o.append(mx_ref.matmul(mx_ref.quantize(e.reshape(128, 512).astype(BF)), q))
    return np.stack(o, axis=2).reshape(128, -1)
def f(rng, *shape):
    return mx_ref.flush((rng.standard_normal(shape, dtype=np.float32) * np.exp2(rng.integers(-2, 3, shape[:-1] + (1,)))).astype(BF))
def wide(rng, *shape, cols=0):
    v = rng.standard_normal(shape, dtype=np.float32) * np.exp2(rng.integers(-12, 13, shape)).astype(np.float32)
    if cols: v *= np.repeat(np.exp2(rng.integers(-cols, cols + 1, shape[:-2] + (1, shape[-1] // 4))) * (rng.random(shape[:-2] + (1, shape[-1] // 4)) > 0.0625), 4, axis=-1).astype(np.float32)
    return mx_ref.flush(v.astype(BF))
P, K, O = 128, 32, 1
def places(t, j):
    return (j + t * np.arange(N)[:, None]) % P
def checks(tab, u):
    return np.stack([mx_ref.matmul(mx_ref.quantize(np.ascontiguousarray(u[r])), tab[r])[:2] for r in range(N)], axis=1)
def judge(c, g, t):
    j = np.arange(P)
    p = (j + t) % N
    at = places(t, j)
    c, a = c[np.arange(N)[:, None], at], np.abs(g[np.arange(N)[:, None], at])
    s = c[p, j]
    for r in range(N):
        s = np.where(p == r, s, s - c[r])
    bad = np.argsort(-np.abs(s), kind="stable")[:K]
    a[p, j] = -1
    return bad, np.argmax(a, axis=0)[bad]
def rebuilt(tab, bad, lost, t):
    at = places(t, bad)
    v = decode(join(*[pick(tab[r], at[r]) for r in range(N)])).reshape(128, N, K, 4)
    new = np.zeros((128, K, 4), np.float32)
    for k in range(K):
        p = (bad[k] + t) % N
        x = v[:, p, k]
        for r in range(N):
            if r != p and r != lost[k]: x = x - v[:, r, k]
        new[:, k] = x
    return mx_ref.quantize(np.ascontiguousarray(new.reshape(128, -1).astype(BF)))
def data(rng):
    return f(rng, N, 128, 4 * P).astype(np.float32).reshape(N, 128, P, 4)
def striped(v):
    v = v.copy()
    for r in range(N):
        j = np.arange(r, P, N)
        v[r][:, j] = 0
        v[r][:, j] = np.sum(v[:, :, j], axis=0)
    return v
def harm(rng, v, stripes, size):
    for j in stripes:
        v[(j + rng.integers(1, N)) % N][:, j] = size * rng.standard_normal((128, 4))
def queries(rng):
    q = np.array(f(rng, 1, 128, 512))
    q[:, :, 8:] = 0
    return np.concatenate([q] * N)
def draw(rng, v, q=None):
    v = v.astype(np.float32).reshape(N, 128, 4 * P)
    v[np.abs(v) < np.float32(2.0 ** -16)] = 0
    return {"tb": v.astype(BF), "u": queries(rng) if q is None else q, "w": f(rng, N, 128, 512 * O)}
def setup_inputs(rng):
    v = striped(data(rng))
    harm(rng, v, rng.permutation(P)[:K + 6], 8)
    return draw(rng, v)
def setup_inputs_again(rng):
    v, q = striped(data(rng) * np.float32(2.0 ** -8)), queries(rng)
    s = np.where(q[0, :, 4:8].astype(np.float32) < 0, -1.0, 1.0)
    q[:, :, :4] = (np.abs(q[:, :, :4].astype(np.float32)) * s).astype(BF)
    q[:, :32, :4] = 0
    on = (np.arange(128) < 32)[:, None]
    at = N * rng.permutation(P // N)[:K // 2] + 2 * rng.integers(0, N // 2, K // 2) + np.arange(K // 2) % 2
    for j in at:
        p = int(j) % N
        m = (p + int(rng.integers(1, N))) % N
        if p % 2:
            m = ((p + 1) // 2 + N // 2 * int(rng.integers(0, 2))) % N
            if m == p: m = (m + N // 2) % N
        v[m][:, j] = 2.0 ** -4 * (1 + rng.random((128, 4))) * s * on
        v[p][:, j] = (2.0 ** 5 if p % 2 else -2.0 ** 5) * (1 + rng.random((128, 4))) * s
    return draw(rng, v, q)
def setup_inputs_one(rng):
    v, q = striped(data(rng)), queries(rng)
    s = np.where(q[0, :, :4].astype(np.float32) < 0, -1.0, 1.0)
    q[:, :, 4:8] = (np.abs(q[:, :, 4:8].astype(np.float32)) * s).astype(BF)
    m, i = int(rng.integers(0, N)), np.arange(P)
    at = rng.permutation(np.flatnonzero((i % N != m) & ((i - m + 1) % N != m)))[:2 * K]
    size = np.repeat([2.0 ** 16, 2.0 ** 11], K)
    v[m][:, at] = (1 + rng.random((128, 2 * K, 4))) * s[:, None] * size[:, None]
    return draw(rng, v, q)
def setup_inputs_spread(rng):
    q = (queries(rng).astype(np.float32) * np.float32(2.0 ** 20)).astype(BF)
    return draw(rng, wide(rng, N, 128, 4 * P, cols=6), q)
def setup_inputs_ties(rng):
    v, q = np.zeros((N, 128, P, 4), np.float32), queries(rng)
    s = np.where(q[0, :, 4:8].astype(np.float32) < 0, -1.0, 1.0)
    q[:, :32, :4] = 0
    on = (np.arange(128) < 32)[:, None]
    for p in range(N):
        at = p + N * rng.permutation(P // N)
        for g in range(P // N // 3):
            x = 2.0 ** -2 * rng.standard_normal((N, 128, 1, 4))
            a, b, m = (p + 1 + rng.permutation(N - 1)[:3]) % N
            x[p] *= 2.0 ** 22
            x[m] = x[p]
            x[a, :, 0] = np.where(on, 2.0 ** 23 * (1 + rng.random((128, 4))) * s, x[a, :, 0])
            x[b] = x[a] * rng.choice([-1.0, 1.0])
            v[:, :, at[3 * g:3 * g + 3]] = x * rng.choice([-1.0, 1.0], (3, 1))
    return draw(rng, v, q)
def setup_inputs_zero(rng):
    v = striped(data(rng))
    lo, hi = int(rng.integers(0, K // 4 + 1)), int(rng.integers(K // 2, P - K // 4 + 1))
    v[:, :, :hi] = 0
    v[:, :, hi + K // 4:] = 0
    for j in range(lo, lo + K // 4):
        m, n = (j + 1 + rng.permutation(N - 1)[:2]) % N
        v[m][:, j] = 4 * rng.standard_normal((128, 4))
        v[n][:, j] = -v[m][:, j]
    harm(rng, v, np.arange(hi, hi + K // 4), 8)
    return draw(rng, v)
def check_inputs(d):
    b = []
    for k, lo, hi in (("tb", -16, 24), ("u", -30, 30), ("w", -30, 30)):
        v = np.abs(d[k].astype(np.float32))
        if not (np.isfinite(v).all() and ((v == 0) | (v >= 2.0 ** lo) & (v <= 2.0 ** hi)).all()): b.append("a value of " + k)
    q = d["u"].astype(np.float32)
    if (q[:, :, 8:] != 0).any(): b.append("u has numbers behind its first 2 columns")
    if (q != q[:1]).any(): b.append("u isn't the same on all ranks")
    return b
def reference(tb, u, w):
    tab = [mx_ref.quantize(np.ascontiguousarray(tb[r])) for r in range(N)]
    bs = np.zeros((N, 4, K), np.float32)
    for t in range(2):
        c, g = checks(tab, u)
        bad, lost = judge(c, g, t)
        new = rebuilt(tab, bad, lost, t)
        at = places(t, bad)
        for r in range(N):
            e = np.flatnonzero(lost == r)
            tab[r] = put(tab[r], at[r, e], pick(new, e))
        bs[:, 2 * t] = bad
        bs[:, 2 * t + 1] = lost
    oc, osc, y = np.zeros((N, 128, 4 * P), np.uint8), np.zeros((N, 16, P), np.uint8), np.zeros((N, 128, O * P), np.float32)
    for r in range(N):
        oc[r], osc[r] = emit(tab[r])
        for o in range(O):
            y[r, :, o * P:o * P + P] = mx_ref.matmul(mx_ref.quantize(np.ascontiguousarray(cut(w[r], o))), tab[r])
    return {"oc": oc, "osc": osc, "bs": bs, "y": y}

@@ -1,0 +1,597 @@
+import numpy as np
+from concourse.bass import DstId, RemoteDMATransfer
+from concourse.mybir import dt, AluOpType as Op, AxisListType, ActivationFunctionType as AF
+
+N, P, K = 8, 128, 32
+REB = ((0, 2, 4, 6), (1, 3, 5, 7))
+NK = K // 4
+TINY = 2.0 ** -121
+X4, U8, F32, I32, U16, BF = "float8_e4m3fn_x4", "uint8", "float32", "int32", "uint16", "bfloat16"
+
+
+def _sb(n, d):
+    return ("sbuf", [128, n], d)
+
+
+SCRATCH = {
+    "tbt": _sb(544, BF), "ut": _sb(512, BF), "wt": _sb(512, BF), "hz": _sb(512, BF), "eb": _sb(2048, BF),
+    "t0": _sb(128, X4), "t0s": _sb(128, U8), "tr": _sb(128, X4), "trs": _sb(128, U8),
+    "uq": _sb(128, X4), "uqs": _sb(128, U8), "wq": _sb(128, X4), "wqs": _sb(128, U8),
+    "eq": _sb(512, X4), "eqs": _sb(512, U8),
+    "ur": _sb(256, X4), "urs": _sb(256, U8),
+    "t1": _sb(128, X4), "t1s": _sb(128, U8), "t2": _sb(128, X4), "t2s": _sb(128, U8),
+    "ones": _sb(256, F32), "ident": _sb(128, F32), "ck": _sb(576, F32), "dz": _sb(361, F32),
+    "pi": _sb(2, I32), "pj": _sb(4, I32), "cf": _sb(8, F32), "mk": _sb(4, F32), "rr": _sb(8, F32), "irow": _sb(32, F32),
+    "pr": _sb(8, I32), "prb": _sb(8, I32), "xr": _sb(16, F32), "xi": _sb(16, I32), "xj": _sb(16, I32), "kw": _sb(256, F32), "pf": _sb(1, F32),
+    "wr": _sb(8, F32), "w32": _sb(8, F32), "w0": _sb(8, F32), "dm": _sb(8, F32), "pm": _sb(8, F32), "c1": _sb(24, F32),
+    "src": _sb(16, F32), "tgt": _sb(16, F32), "lc": _sb(8, F32), "rm": _sb(8, F32), "kb": _sb(8, F32), "fac": _sb(128, F32), "seg": _sb(256, F32),
+    "d0": _sb(64, F32), "oz": _sb(16, U16),
+    "ag": _sb(16, F32), "agn": _sb(32, F32), "so": _sb(72, F32), "xo": _sb(361, F32), "xs": _sb(361, F32), "msk": _sb(288, F32),
+    "rep": _sb(9, F32), "junk": _sb(288, F32), "hit": _sb(192, F32), "hiti": _sb(64, I32), "gv": _sb(40, F32), "w40": _sb(40, F32), "gt": _sb(96, F32),
+    "lw": _sb(96, F32), "ysb": _sb(128, F32),
+    "ps": ("psum", [128, 512], F32), "da": ("psum", [128, 2048], F32), "db": ("psum", [128, 1536], F32),
+}
+for _t in "01":
+    SCRATCH.update({
+        "sc" + _t: _sb(32, X4), "ss" + _t: _sb(32, U8), "la" + _t: _sb(192, X4), "ls" + _t: _sb(192, U8),
+        "or" + _t: _sb(128, X4), "os" + _t: _sb(128, U8), "h" + _t: _sb(512, BF), "nq" + _t: _sb(128, X4), "ns" + _t: _sb(128, U8),
+        "tw" + _t: _sb(256, X4), "tws" + _t: _sb(256, U8), "sb" + _t: _sb(256, F32),
+        "sr" + _t: _sb(64, F32), "ar" + _t: _sb(128, F32), "thr" + _t: _sb(128, F32), "g" + _t: _sb(193, F32), "yo" + _t: _sb(193, F32),
+        "yb" + _t: _sb(64, F32), "sm" + _t: _sb(32, F32), "of" + _t: _sb(2, U16), "vx" + _t: _sb(128, F32), "vr" + _t: _sb(96, F32), "vi" + _t: _sb(96, I32),
+        "bsb" + _t: _sb(64, F32), "rl" + _t: _sb(96, F32), "ol" + _t: _sb(4, U16), "ei" + _t: _sb(784, F32), "oi" + _t: _sb(8, U16),
+    })
+SEMAPHORES = ["v", "a", "sl", "s_ck", "s_la0", "s_la1", "s_nw0", "s_nw1"] + ["e%d" % _i for _i in range(135)]
+
+
+def rank_program(g, core, T, topo):
+    rank = T.rank_of(core)
+    if rank is None:
+        return
+    V, A, PE, SY = g.vector, g.scalar, g.tensor, g.sync
+    X = AxisListType.X
+    used, nv, na, nsl, fin = [0], [0], [0], [0], []
+
+    def ev(ins, n=1):
+        s = T.sem["e%d" % used[0]]
+        used[0] += 1
+        ins.then_inc(s, n)
+        return (s, n)
+
+    def wait(q, *evs):
+        for s, n in evs:
+            q.wait_ge(s, n)
+
+    def v(ins):
+        ins.then_inc(T.sem.v, 1)
+        nv[0] += 1
+
+    def vw():
+        V.wait_ge(T.sem.v, nv[0])
+
+    def a(ins):
+        ins.then_inc(T.sem.a, 1)
+        na[0] += 1
+
+    def aw():
+        A.wait_ge(T.sem.a, na[0])
+
+    def ts(out, i0, s1, op0, s2=None, op1=None):
+        if op1 is None:
+            return V.tensor_scalar(out, i0, s1, None, op0)
+        return V.tensor_scalar(out, i0, s1, s2, op0, op1)
+
+    def tt(out, i0, i1, op):
+        return V.tensor_tensor(out, i0, i1, op)
+
+    def u8(view):
+        return view.bitcast(dt.uint8)
+
+    def u32(view):
+        return view.bitcast(dt.uint32)
+
+    others = [r for r in range(N) if r != rank]
+    EW = len(topo.engines(core, T.cores[others[0]]))
+
+    def dst(r):
+        rid, pid = topo.addr(T.cores[r], core)
+        return DstId(rid=int(rid), pnc=int(pid))
+
+    def to_all(src, out, sem):
+        m = int(topo.mask(core, T.cores[others[0]]))
+        g.remote_dma_fused([RemoteDMATransfer(dst_ids=[dst(r) for r in others], dma_engine_mask=m, remote_sem=sem, srcs=[src], dsts=[out for r in others])], local_sem=T.sem.sl)
+        nsl[0] += EW
+
+    def to_rebuilders(pairs, sem):
+        tr = []
+        for i, (r, s, d) in enumerate(pairs):
+            es = topo.engines(core, T.cores[r])
+            w = len(es) // 4
+            m = 0
+            for e in es[w * i:w * i + w]:
+                m |= 1 << e
+            tr.append(RemoteDMATransfer(dst_ids=[dst(r)], dma_engine_mask=m, remote_sem=sem, srcs=[s], dsts=[d]))
+            nsl[0] += w
+        g.remote_dma_fused(tr, local_sem=T.sem.sl)
+
+    mine = [t for t in range(2) if rank in REB[t]][0]
+
+    e_tb = ev(SY.dma_start(T.tbt[:, 0:512], T.tb[:, 0:512]), 16)
+    e_tb2 = ev(A.dma_start(T.tbt[:, 512:544], T.tb[:, 0:32]), 16)
+    e_u0 = ev(A.dma_start(T.ut[:, 0:4], T.u[:, 0:4]), 16)
+    e_u1 = ev(A.dma_start(T.ut[:, 4:16], T.u[:, 0:12]), 16)
+
+    def iota(out, pat, base, cm, f=True):
+        if f:
+            return ev(g.iota(out, pat, base, cm, allow_small_or_imprecise_dtypes=True))
+        return ev(g.iota(out, pat, base, cm))
+    i_pi = iota(T.pi[:, 0:2], [[1, 2]], 0, 1, False)
+    i_rr = iota(T.rr[:, 0:8], [[1, 8]], 0, 0)
+    i_ir = iota(T.irow[:, 0:32], [[1, 32]], 0, 0)
+    i_pf = iota(T.pf[:, 0:1], [[0, 1]], 0, 1)
+    i_pr = iota(T.pr[:, 0:8], [[1, 8]], 0, 1, False)
+    i_x0 = iota(T.xr[:, 0:8], [[16, 8]], rank, 0)
+    i_x1 = iota(T.xr[:, 8:16], [[16, 8]], P - rank, 0)
+
+    v(V.memset(T.ut[:, 16:512], 0.0))
+    e_hz = ev(V.memset(T.hz[:], 0.0))
+    e_ones = ev(V.memset(T.ones[:], 1.0))
+    wait(g, e_ones)
+    e_id = ev(g.affine_select(T.ident[:], T.ones[:, 0:128], [[-1, 128]], Op.is_equal, 0.0, 0, 1))
+    i_kw = iota(T.kw[:, 0:256], [[0, 8], [1, 32]], P, 0)
+    wait(V, i_pi)
+    v(ts(T.pj[:, 2:3], T.pi[:, 0:1], 7, Op.bitwise_and))
+    v(ts(T.pj[:, 0:1], T.pi[:, 0:1], 15, Op.bitwise_and))
+    v(ts(T.pj[:, 1:2], T.pi[:, 0:1], 31, Op.bitwise_and))
+    v(ts(T.pj[:, 3:4], T.pi[:, 1:2], 7, Op.bitwise_and))
+    vw()
+    v(ts(T.mk[:, 0:1], T.pj[:, 2:3], float(rank), Op.is_equal))
+    v(ts(T.mk[:, 1:2], T.pj[:, 2:3], float(rank), Op.not_equal))
+    v(ts(T.mk[:, 2:3], T.pj[:, 2:3], float(rank), Op.not_equal))
+    v(V.tensor_copy(T.cf[:, 0:4], T.pj[:, 0:4]))
+    vw()
+    p16, p32, p8, q1 = (T.cf[:, i:i + 1] for i in range(4))
+    wait(V, e_u0, e_u1)
+    e_uq = ev(V.quantize_mx(T.uq[:], T.uqs[:], T.ut[:]))
+    wait(V, e_tb)
+    e_t0 = ev(V.quantize_mx(T.t0[:], T.t0s[:], T.tbt[:, 0:512]))
+    wait(V, e_tb2)
+    e_tr = ev(V.quantize_mx(T.tr[:], T.trs[:], T.tbt[:, 4 * rank:4 * rank + 512]))
+    wait(PE, e_uq, e_t0)
+    e_m0 = ev(PE.matmul_mx(T.ps[:, 0:128], T.t0[:], T.t0s[:], T.uq[:], T.uqs[:], True, True))
+    wait(PE, e_tr)
+    e_m1 = ev(PE.matmul_mx(T.db[:, 0:128], T.tr[:], T.trs[:], T.uq[:], T.uqs[:], True, True))
+    o = 8 * rank
+    wait(V, e_m0)
+    e_c0 = ev(tt(T.ck[:, o:o + 3], T.ps[:, 0:3], T.mk[:, 0:3], Op.mult))
+    wait(V, e_m1)
+    e_c1 = ev(V.tensor_copy(T.ck[:, o + 3:o + 5], T.db[:, 1:3]))
+    wait(g, e_c0, e_c1)
+    to_all(T.ck[:, o:o + 5], T.ck[:, o:o + 5], T.sem.s_ck)
+    wait(SY, e_t0)
+    e_tw0 = [ev(SY.dma_start(u8(T.tw0[:, 0:128]), u8(T.t0[:])), 16), ev(SY.dma_start(T.tws0[:, 0:128], T.t0s[:]), 16)]
+    e_w = ev(SY.dma_start(T.wt[:], T.w[:, 0:512]), 16)
+
+    wait(A, e_hz, e_ones)
+    e_k0 = ev(A.activation(T.ck[:, 72:576], T.hz[:, 0:504], AF.Copy))
+    e_k1 = ev(A.activation(T.dz[:, 0:256], T.ones[:], AF.Copy))
+    e_k2 = ev(A.activation(T.dz[:, 256:361], T.ones[:, 0:105], AF.Copy))
+    for b in range(4):
+        a(A.activation(T.eb[:, 512 * b:512 * b + 512], T.hz[:], AF.Copy))
+    e_k3 = ev(A.activation(T.d0[:], T.ones[:, 0:64], AF.Copy))
+    wait(A, e_id)
+    aw()
+    for b in range(4):
+        a(A.activation(T.eb[:, 512 * b + b:512 * b + 512:4], T.ident[:], AF.Copy))
+    a(A.activation(T.seg[:], T.ones[:], AF.Copy))
+    aw()
+    e_seg = ev(A.activation(T.seg[:, 0:256:32], T.hz[:, 0:8], AF.Copy))
+    e_eb = ev(A.activation(T["h%d" % mine][:], T.hz[:], AF.Copy))
+
+    wait(V, e_hz, e_ones, e_uq, e_t0, e_tr, e_c0, e_c1)
+    wait(V, i_rr, i_ir, i_pr, i_x0, i_x1, i_pf, i_kw)
+    v(ts(T.fac[:, 0:32], T.irow[:], p32, Op.is_lt, -2.0 ** -24, Op.mult))
+    v(V.memset(T.fac[:, 32:128], 1.0))
+    v(V.memset(T.ck[:, 64:72], -TINY))
+    v(V.memset(T.xs[:, 297:298], -TINY))
+    v(V.memset(T.xs[:, 298:361], 0.0))
+    v(V.memset(T.g0[:, 130:193], -1.0))
+    v(V.memset(T.g1[:, 130:193], -1.0))
+    v(ts(T.wr[:], T.rr[:], -1.0 / 8192, Op.mult, 8.0 / 8192, Op.add))
+    v(ts(T.w32[:], T.rr[:], -1.0 / 32, Op.mult, 8.0 / 32, Op.add))
+    v(ts(T.gt[:, 0:8], T.rr[:], p8, Op.not_equal))
+    v(ts(T.prb[:], T.pr[:], 127, Op.bitwise_and))
+    v(ts(T.xi[:], T.xr[:], p16, Op.add))
+    v(ts(T.lc[:, 6:7], p16, 8.0, Op.is_ge, -1000.0, Op.mult))
+    v(ts(T.lc[:, 7:8], p16, 8.0, Op.is_lt, -1000.0, Op.mult))
+    v(ts(T.dm[:], T.rr[:], q1, Op.not_equal))
+    v(ts(T.pm[:], T.rr[:], q1, Op.is_equal))
+    vw()
+    wait(V, e_k0, e_k1, e_k2)
+    v(ts(T.fac[:, 0:32], T.fac[:, 0:32], 1.0, Op.add))
+    for b in range(1, 4):
+        v(V.memset(T.fac[32 * b:32 * b + 32, 128 - 32 * b:128], 1.0 - 2.0 ** -24))
+    for gg in (T.g0, T.g1):
+        v(V.memset(gg[:, 145:146], 15.0))
+        v(V.memset(gg[:, 177:178], 15.0))
+        v(ts(gg[:, 128:129], T.pf[:], 1.0 / 256, Op.mult))
+    v(V.memset(T.dz[:, 329:330], -1.0))
+    v(tt(T.w0[:], T.gt[:, 0:8], T.wr[:], Op.mult))
+    v(ts(T.rm[:, 0:8:2], T.rr[:, 0:8:2], T.lc[:, 6:7], Op.add))
+    v(ts(T.rm[:, 1:8:2], T.rr[:, 1:8:2], T.lc[:, 7:8], Op.add))
+    v(ts(T.lc[:, 0:1], p8, -1.0, Op.add))
+    v(ts(T.lc[:, 1:2], p8, 0.0, Op.is_equal, 8.0, Op.mult))
+    v(ts(T.lc[:, 2:3], p16, 8.0, Op.is_lt, 64.0, Op.mult))
+    v(ts(T.lc[:, 3:4], p16, 8.0, Op.is_ge, 64.0, Op.mult))
+    v(ts(T.lc[:, 4:5], p8, -1.0, Op.add, 8.0, Op.mult))
+    v(V.tensor_copy(T.c1[:, 0:8], T.prb[:]))
+    v(ts(T.xj[:], T.xi[:], 127, Op.bitwise_and))
+    v(V.memset(T.oz[:, 0:8], 0))
+    v(V.memset(T.oz[:, 8:16], 2))
+    e_fac = ev(V.quantize_mx(T.tw0[:, 128:256], T.tws0[:, 128:256], T.hz[:]))
+    vw()
+    wait(V, e_fac, e_k3)
+    v(ts(T.kb[:], T.rm[:], T.lc[:, 4:5], Op.add))
+    v(V.memset(T.d0[:, 0:64:8], 0.0))
+    v(V.memset(T.d0[:, 1:64:8], -1.0))
+    v(V.tensor_copy(T.src[:], T.xj[:]))
+    e_oz = ev(tt(T.c1[:, 8:16], T.c1[:, 0:8], T.w32[:], Op.add))
+    v(V.quantize_mx(T["la%d" % mine][:, 64:192], T["ls%d" % mine][:, 64:192], T.hz[:]))
+    v(V.quantize_mx(T["or%d" % mine][:], T["os%d" % mine][:], T.hz[:]))
+    vw()
+    wait(V, e_oz)
+    v(ts(T.tgt[:], T.src[:], (8 - rank) / 32.0, Op.add))
+    v(tt(T.c1[:, 16:24], T.c1[:, 8:16], T.pm[:], Op.mult))
+    im1, is08, lo64, hi64 = (T.lc[:, i:i + 1] for i in range(4))
+
+    def unpacker():
+        wait(V, e_eb)
+        return ev(V.quantize_mx(T.eq[:], T.eqs[:], T.eb[:]))
+
+    def turn(buf, o, w, n, k):
+        m = (n + k) % 4
+        return buf[32 * n:32 * n + 32, o + k * w:o + k * w + w], buf[32 * m:32 * m + 32, o:o + w]
+
+    def half(buf, o, w, n):
+        return buf[64 * n:64 * n + 64, o + 2 * w:o + 3 * w], buf[64 - 64 * n:128 - 64 * n, o:o + w]
+
+    def order(t, so, e_s, lost, e_tab):
+        sr, ar, thr, gg, yo, yb, sm = (T["%s%d" % (n, t)] for n in ("sr", "ar", "thr", "g", "yo", "yb", "sm"))
+        lost[0]()
+        wait(A, e_s, e_fac)
+        e_th = ev(A.activation(thr[:], T.fac[:], AF.Abs, scale=so[0]))
+        wait(V, e_s)
+        e_tp = ev(V.transpose(sr[:], so[1]))
+        vw()
+        lost[1]()
+        wait(V, e_tp)
+        wait(A, e_tp)
+        vw()
+
+        def size(p0, p1, c, q0, q1):
+            v(tt(ar[p0:p1, c:c + 32], sr[q0:q1, 0:32], sr[q0:q1, 32:64], Op.max))
+        size(0, 128, 0, 0, 128)
+        size(0, 64, 64, 64, 128)
+        size(64, 128, 64, 0, 64)
+        for n in range(3):
+            size(32 * n, 32 * n + 32, 32, 32 * n + 32, 32 * n + 64)
+        for n in range(4):
+            m = (n + 3) % 4
+            a(A.activation(ar[32 * n:32 * n + 32, 96:128], sr[32 * m:32 * m + 32, 0:32], AF.Abs))
+        e_tn = ev(A.activation(ar[96:128, 32:64], sr[0:32, 0:32], AF.Abs))
+        lost[2]()
+        vw()
+        wait(V, e_th, e_tn)
+        V.wait_ge(T.sem.a, na[0])
+        v(tt(gg[:, 0:128], ar[:], thr[:], Op.is_gt))
+        lost[3]()
+        vw()
+        v(V.tensor_tensor_scan(yo[:], T.dz[:, 0:193], gg[:], 0.0, Op.mult, Op.add))
+        vw()
+        v(V.transpose(yb[:], yo[:, 129:193]))
+        vw()
+        e_z0 = ev(V.tensor_reduce(sm[:, 8:9], yb[:, 0:32], X, Op.min, apply_absolute_value=True))
+        e_z1 = ev(V.tensor_reduce(sm[:, 9:10], yb[:, 32:64], X, Op.min, apply_absolute_value=True))
+        wait(A, e_z0, e_z1)
+        wait(V, e_z0, e_z1)
+        for n in range(4):
+            v(V.tensor_copy(*turn(sm, 8, 2, n, 1)))
+        v(V.tensor_copy(*half(sm, 8, 2, 0)))
+        for n in range(4):
+            a(A.activation(*turn(sm, 8, 2, n, 3), AF.Copy))
+        e_zn = ev(A.activation(*half(sm, 8, 2, 1), AF.Copy))
+        vw()
+        wait(V, e_zn)
+        V.wait_ge(T.sem.a, na[0])
+        v(V.tensor_reduce(sm[:, 16:17], sm[:, 8:16:2], X, Op.min))
+        v(V.tensor_reduce(sm[:, 17:18], sm[:, 9:16:2], X, Op.min))
+        vw()
+        of = T["of%d" % t]
+        e_of = ev(ts(of[:], sm[:, 16:18], 256.0, Op.mult))
+        tab, tabs = (T.t0, T.t0s) if t == 0 else (T.t1, T.t1s)
+        sc, ss, la, ls = (T["%s%d" % (n, t)] for n in ("sc", "ss", "la", "ls"))
+        wait(V, *e_tab)
+        wait(A, *e_tab)
+        wait(V, e_of)
+        wait(A, e_of)
+        e_sc = ev(V.tensor_copy(u32(sc[:]), u32(tab[:, 0:128]).indirect(of[:])))
+        e_ss = ev(A.activation(ss[:], tabs[:, 0:128].indirect(of[:]), AF.Copy))
+        sl = slice(NK * rank, NK * rank + NK)
+        wait(g, e_sc)
+        to_rebuilders([(r, u8(sc[:, NK * i:NK * i + NK]), u8(la[:, sl])) for i, r in enumerate(REB[t]) if r != rank], T.sem["s_la%d" % t])
+        wait(g, e_ss)
+        to_rebuilders([(r, ss[:, NK * i:NK * i + NK], ls[:, sl]) for i, r in enumerate(REB[t]) if r != rank], T.sem["s_la%d" % t])
+        own = []
+        if rank in REB[t]:
+            i = REB[t].index(rank)
+            wait(SY, e_sc)
+            own.append(ev(SY.dma_start(u8(la[:, sl]), u8(sc[:, NK * i:NK * i + NK])), 16))
+            wait(SY, e_ss)
+            own.append(ev(SY.dma_start(ls[:, sl], ss[:, NK * i:NK * i + NK]), 16))
+        vx, vr, vi, bsb = T["vx%d" % t], T["vr%d" % t], T["vi%d" % t], T["bsb%d" % t]
+        for h in range(2):
+            v(ts(vx[:, 32 * h:32 * h + 32], T.ones[:, 0:32], sm[:, 16 + h:17 + h], Op.mult, 256.0, Op.mult))
+        vw()
+        v(V.transpose(vx[:, 64:128], vx[:, 0:64]))
+        vw()
+        for h in range(2):
+            s = vx[:, 64 + 32 * h:80 + 32 * h]
+            v(V.tensor_copy(vi[:, 16 * h:16 * h + 16], s))
+            if t:
+                v(ts(vi[:, 32 + 16 * h:48 + 16 * h], s, float(t), Op.add))
+            v(V.tensor_copy(vr[:, 16 * h:16 * h + 16], s))
+        vw()
+        v(V.tensor_copy(bsb[:, 0:32], vi[:, 0:32]))
+        v(ts(vi[:, 64:96], vi[:, 32 * t:32 * t + 32], 7, Op.bitwise_and))
+        vw()
+        v(tt(vr[:, 32:64], vr[:, 0:32], bsb[:, 0:32], Op.subtract))
+        v(V.tensor_copy(vr[:, 64:96], vi[:, 64:96]))
+        vw()
+        e_b = ev(ts(bsb[:, 32:64], vr[:, 32:64], -32.0, Op.mult, 8.0, Op.add))
+        wait(SY, e_b)
+        fin.append(ev(SY.dma_start(T.bs[2 * t:2 * t + 2, 0:32], bsb[0:1, 0:64]), 16))
+        return own, e_b
+
+    def rebuild_list(t, e_b):
+        s = NK * REB[t].index(rank)
+        vr, bsb, rl, ol = T["vr%d" % t], T["bsb%d" % t], T["rl%d" % t], T["ol%d" % t]
+        q, lost = vr[:, 64 + s:72 + s], bsb[:, 32 + s:40 + s]
+        v(ts(rl[:, 0:8], q, im1, Op.is_le, float(NK), Op.mult))
+        v(ts(rl[:, 8:16], q, im1, Op.is_le))
+        v(ts(rl[:, 16:24], q, is08, Op.mult))
+        vw()
+        wait(V, e_b)
+        v(tt(rl[:, 24:32], lost, rl[:, 8:16], Op.subtract))
+        v(tt(rl[:, 32:40], rl[:, 0:8], T.kb[:], Op.add))
+        v(tt(rl[:, 40:48], rl[:, 16:24], T.rm[:], Op.add))
+        vw()
+        v(ts(rl[:, 48:56:2], rl[:, 24:32:2], im1, Op.is_equal, lo64, Op.mult))
+        v(ts(rl[:, 49:56:2], rl[:, 25:32:2], im1, Op.is_equal, hi64, Op.mult))
+        v(tt(rl[:, 56:64], rl[:, 32:40], rl[:, 40:48], Op.max))
+        vw()
+        v(tt(rl[:, 64:72], rl[:, 48:56], rl[:, 56:64], Op.max))
+        vw()
+        v(tt(rl[:, 72:76], rl[:, 64:72:2], rl[:, 65:72:2], Op.max))
+        vw()
+        return ev(V.tensor_copy(ol[:], rl[:, 72:76]))
+
+    def rebuild(t, own, e_ol, e_eq, e_free):
+        la, ls, od, os_, h, nq, ns, sb, ol = (T["%s%d" % (n, t)] for n in ("la", "ls", "or", "os", "h", "nq", "ns", "sb", "ol"))
+        D, banks = (T.da, 4) if t == 0 else (T.db, 3)
+        arr = (T.sem["s_la%d" % t], 7 * 2 * (EW // 4))
+        wait(V, e_ol, e_eq, *own)
+        wait(V, arr)
+        e_oc = ev(V.tensor_copy(u32(od[:, 0:64]), u32(la[:, 0:96]).indirect(ol[:])))
+        wait(A, e_ol, *own)
+        wait(A, arr)
+        e_os = ev(A.activation(os_[:, 0:64], ls[:, 0:96].indirect(ol[:]), AF.Copy))
+        wait(PE, *e_free)
+        wait(PE, e_eq, e_oc, e_os)
+        scans, cps = [], []
+        for b in range(4):
+            k = 512 * (b % banks)
+            if b >= banks:
+                wait(PE, scans[b - banks])
+            e_d = ev(PE.matmul_mx(D[:, k:k + 128], T.eq[:, 128 * b:128 * b + 128], T.eqs[:, 128 * b:128 * b + 128], od[:], os_[:], True, True))
+            wait(V, e_d)
+            scans.append(ev(V.tensor_tensor_scan(sb[:, 64 * b:64 * b + 64], T.d0[:], D[:, k:k + 64], 0.0, Op.mult, Op.subtract)))
+        for b in range(3):
+            wait(A, scans[b])
+            cps.append(ev(A.activation(h[:, b:4 * NK:4], sb[:, 64 * b + 7:64 * b + 64:8], AF.Copy)))
+        wait(V, scans[3])
+        cps.append(ev(V.tensor_copy(h[:, 3:4 * NK:4], sb[:, 199:256:8])))
+        wait(V, e_eb, *scans)
+        wait(V, *cps)
+        e_nq = ev(V.quantize_mx(nq[:], ns[:], h[:]))
+        i = REB[t].index(rank)
+        sl = slice(P + NK * i, P + NK * i + NK)
+        tw, tws = T["tw%d" % t], T["tws%d" % t]
+        wait(g, e_nq)
+        to_all(u8(nq[:, 0:NK]), u8(tw[:, sl]), T.sem["s_nw%d" % t])
+        to_all(ns[:, 0:NK], tws[:, sl], T.sem["s_nw%d" % t])
+        wait(SY, e_nq)
+        return [ev(SY.dma_start(u8(tw[:, sl]), u8(nq[:, 0:NK])), 16), ev(SY.dma_start(tws[:, sl], ns[:, 0:NK]), 16)]
+
+    def table0(t):
+        for c in range(8):
+            v(ts(T["ei%d" % t][:, 32 * c:32 * c + 32], T["vr%d" % t][:, 0:32], T.tgt[:, 8 * t + c:8 * t + c + 1], Op.is_equal))
+
+    def table1(t):
+        ei = T["ei%d" % t]
+        v(tt(ei[:, 256:512], ei[:, 0:256], T.kw[:], Op.mult))
+
+    def table2(t):
+        ei = T["ei%d" % t]
+        v(V.tensor_tensor_scan(ei[:, 512:768], T.seg[:], ei[:, 256:512], 0.0, Op.mult, Op.max))
+
+    def table3(t):
+        ei = T["ei%d" % t]
+        v(tt(ei[:, 768:776], ei[:, 543:768:32], T.src[:, 8 * t:8 * t + 8], Op.max))
+
+    def table4(t):
+        return ev(V.tensor_copy(T["oi%d" % t][:], T["ei%d" % t][:, 768:776]))
+
+    def arrived(t):
+        return (T.sem["s_nw%d" % t], EW * (6 if mine == t else 8))
+
+    s_ck = (T.sem.s_ck, 7 * EW)
+    wait(A, e_c0, e_c1)
+    wait(A, s_ck)
+    e_ag0 = ev(A.activation(T.ag[:, 0:8], T.ck[:, 2:64:8], AF.Abs))
+    e_ag1 = ev(A.activation(T.ag[:, 8:16], T.ck[:, 4:64:8], AF.Abs))
+    vw()
+    wait(V, s_ck)
+    v(V.tensor_reduce(T.cf[:, 5:6], T.ck[:, 0:64:8], X, Op.add))
+    vw()
+    e_s = ev(V.tensor_tensor_scan(T.so[:], T.dz[:, 289:361], T.ck[:, 1:576:8], T.cf[:, 5:6], Op.mult, Op.subtract))
+
+    def l0a():
+        wait(V, e_ag0)
+        v(V.tensor_reduce(T.cf[:, 6:7], T.ag[:, 0:8], X, Op.max))
+
+    def l0b():
+        v(ts(T.gt[:, 8:16], T.ag[:, 0:8], T.cf[:, 6:7], Op.is_equal))
+
+    def l0c():
+        v(tt(T.gt[:, 16:24], T.gt[:, 8:16], T.w0[:], Op.mult))
+
+    def l0d():
+        v(V.tensor_reduce(T.g0[:, 129:130], T.gt[:, 16:24], X, Op.max))
+
+    own, e_b = order(0, (T.so[:, 8:9], T.so[:, 8:72]), e_s, (l0a, l0b, l0c, l0d), [e_t0])
+    new_own = []
+    if mine == 0:
+        e_ol = rebuild_list(0, e_b)
+        e_eq = unpacker()
+        new_own = rebuild(0, own, e_ol, e_eq, [])
+    vr, bsb = T.vr0, T.bsb0
+    hit, hi = T.hit, T.hiti
+    wait(V, e_b)
+    e_ms = []
+    for r in range(N):
+        e_ms.append(ev(ts(T.msk[:, 32 * r:32 * r + 32], vr[:, 0:32], T.c1[:, 8 + r:9 + r], Op.is_equal, T.dm[:, r:r + 1], Op.mult)))
+    v(V.tensor_reduce(T.cf[:, 4:5], T.c1[:, 16:24], X, Op.add))
+    table0(0)
+    v(tt(hit[:, 0:32], bsb[:, 0:32], bsb[:, 32:64], Op.subtract))
+    v(tt(T.gt[:, 24:32], T.ck[:, 3:64:8], T.pm[:], Op.mult))
+    v(ts(hit[:, 32:64], bsb[:, 32:64], q1, Op.not_equal))
+    v(ts(hit[:, 160:192], vr[:, 32:64], 1.0 / 256, Op.mult))
+    vw()
+    e_ms.append(ev(ts(T.msk[:, 256:288], vr[:, 0:32], T.cf[:, 4:5], Op.is_equal, -1.0, Op.mult)))
+    for r in range(N + 1):
+        wait(A, e_ms[r])
+        a(A.activation(T.junk[:, 32 * r:32 * r + 32], T.msk[:, 32 * r:32 * r + 32], AF.Copy, accum_out=T.rep[:, r:r + 1]))
+    aw()
+    e_rep = ev(A.activation(T.gt[:, 64:73], T.rep[:], AF.Copy))
+    v(ts(hi[:, 0:32], hit[:, 0:32], 128.0, Op.add))
+    v(V.tensor_reduce(T.cf[:, 7:8], T.gt[:, 24:32], X, Op.add))
+    table1(0)
+    vw()
+    v(ts(hi[:, 32:64], hi[:, 0:32], 127, Op.bitwise_and))
+    wait(V, e_seg)
+    table2(0)
+    vw()
+    v(V.tensor_copy(hit[:, 64:96], hi[:, 32:64]))
+    table3(0)
+    e_ur0 = ev(V.tensor_copy(u32(T.ur[:, 0:128]), u32(T.uq[:]).indirect(T.oz[:, 0:8])))
+    vw()
+    e_oi = table4(0)
+    v(ts(hit[:, 96:128], hit[:, 64:96], T.pf[:, 0:1], Op.is_equal))
+    wait(V, e_rep, *e_ms)
+    v(tt(T.gt[:, 32:40], T.dm[:], T.gt[:, 64:72], Op.subtract))
+    v(ts(T.gt[:, 40:41], T.gt[:, 72:73], 1.0, Op.add, -1.0, Op.mult))
+    vw()
+    v(tt(hit[:, 128:160], hit[:, 96:128], hit[:, 32:64], Op.mult))
+    v(tt(T.xs[:, 65:297:33], T.ck[:, 3:64:8], T.gt[:, 32:40], Op.mult))
+    v(tt(T.xs[:, 32:33], T.cf[:, 7:8], T.gt[:, 40:41], Op.mult))
+    v(tt(T.w40[:, 0:8], T.gt[:, 32:40], T.wr[:], Op.mult))
+    wait(V, e_ag1)
+    v(tt(T.gv[:, 0:8], T.gt[:, 32:40], T.ag[:, 8:16], Op.mult))
+    e_ur1 = ev(V.tensor_copy(u32(T.ur[:, 128:256]), u32(T.uq[:]).indirect(T.oz[:, 8:16])))
+    vw()
+    v(tt(T.w40[:, 8:40], hit[:, 128:160], hit[:, 160:192], Op.mult))
+    wait(A, e_uq, e_oz, e_ur0, e_ur1)
+    e_us0 = ev(A.activation(T.urs[:, 0:128], T.uqs[:].indirect(T.oz[:, 0:8]), AF.Copy))
+    e_us1 = ev(A.activation(T.urs[:, 128:256], T.uqs[:].indirect(T.oz[:, 8:16]), AF.Copy))
+    wait(V, e_oi)
+
+    nw = arrived(0)
+    wait(PE, e_us0, e_us1, e_ur0, e_ur1)
+    wait(PE, e_c0, e_c1, *new_own)
+    wait(PE, nw)
+    e_cn = ev(PE.matmul_mx(T.ps[:, 0:128], T.ur[:, 0:128], T.urs[:, 0:128], T.tw0[:, 128:256], T.tws0[:, 128:256], True, True))
+    e_gn = ev(PE.matmul_mx(T.db[:, 0:128], T.ur[:, 128:256], T.urs[:, 128:256], T.tw0[:, 128:256], T.tws0[:, 128:256], True, True))
+    wait(V, *e_tw0)
+    wait(V, *new_own)
+    vw()
+    wait(V, nw)
+    p1 = ev(V.tensor_copy(u32(T.t1[:]), u32(T.tw0[:, 0:160]).indirect(T.oi0[:])))
+    wait(A, e_gn)
+    e_agn = ev(A.activation(T.agn[:], T.db[:, 0:32], AF.Abs))
+    wait(A, e_oi, *e_tw0)
+    wait(A, *new_own)
+    wait(A, nw)
+    p2 = ev(A.activation(T.t1s[:], T.tws0[:, 0:160].indirect(T.oi0[:]), AF.Copy))
+    wait(SY, p1, p2)
+    e_tw1 = [ev(SY.dma_start(u8(T.tw1[:, 0:128]), u8(T.t1[:])), 16), ev(SY.dma_start(T.tws1[:, 0:128], T.t1s[:]), 16)]
+    wait(V, e_cn)
+    for r in range(N):
+        v(tt(T.xs[:, 33 + 33 * r:65 + 33 * r], T.msk[:, 32 * r:32 * r + 32], T.ps[:, 0:32], Op.mult))
+    e_xp = ev(tt(T.xs[:, 0:32], T.msk[:, 256:288], T.ps[:, 0:32], Op.mult))
+    wait(V, e_agn)
+    v(tt(T.gv[:, 8:40], T.agn[:], hit[:, 128:160], Op.mult))
+    wait(V, e_xp)
+    vw()
+    e_s = ev(V.tensor_tensor_scan(T.xo[:], T.dz[:], T.xs[:], 0.0, Op.mult, Op.subtract))
+
+    def l1a():
+        v(V.tensor_reduce(T.gt[:, 42:43], T.gv[:], X, Op.max))
+
+    def l1b():
+        v(ts(T.lw[:, 0:40], T.gv[:], T.gt[:, 42:43], Op.is_equal))
+
+    def l1c():
+        v(tt(T.lw[:, 40:80], T.lw[:, 0:40], T.w40[:], Op.mult))
+
+    def l1d():
+        v(V.tensor_reduce(T.g1[:, 129:130], T.lw[:, 40:80], X, Op.max))
+
+    own, e_b = order(1, (T.xo[:, 297:298], T.xo[:, 297:361]), e_s, (l1a, l1b, l1c, l1d), [p1, p2])
+    new_own = []
+    if mine == 1:
+        e_ol = rebuild_list(1, e_b)
+        e_eq = unpacker()
+        new_own = rebuild(1, own, e_ol, e_eq, [e_agn])
+    wait(V, e_b)
+    table0(1)
+    wait(V, e_w, e_eb)
+    e_wq = ev(V.quantize_mx(T.wq[:], T.wqs[:], T.wt[:]))
+    vw()
+    table1(1)
+    vw()
+    table2(1)
+    vw()
+    table3(1)
+    vw()
+    e_oi = table4(1)
+    nw = arrived(1)
+    wait(V, e_oi, *e_tw1)
+    wait(V, *new_own)
+    wait(V, nw)
+    p1 = ev(V.tensor_copy(u32(T.t2[:]), u32(T.tw1[:, 0:160]).indirect(T.oi1[:])))
+    wait(A, e_oi, *e_tw1)
+    wait(A, *new_own)
+    wait(A, nw)
+    p2 = ev(A.activation(T.t2s[:], T.tws1[:, 0:160].indirect(T.oi1[:]), AF.Copy))
+    wait(SY, p1)
+    fin.append(ev(SY.dma_start(T.oc[:, 0:512], u8(T.t2[:])), 16))
+    wait(A, p2)
+    for k in range(4):
+        fin.append(ev(A.dma_start(T.osc[4 * k:4 * k + 4, 0:128], T.t2s[32 * k:32 * k + 4, 0:128]), 16))
+    wait(PE, e_wq, e_xp, p1, p2)
+    e_y = ev(PE.matmul_mx(T.ps[:, 0:128], T.wq[:], T.wqs[:], T.t2[:], T.t2s[:], True, True))
+    wait(V, e_y)
+    e_yc = ev(V.tensor_copy(T.ysb[:], T.ps[:, 0:128]))
+    wait(SY, e_yc)
+    fin.append(ev(SY.dma_start(T.y[:, 0:128], T.ysb[:]), 16))
+    wait(g, *fin)
+    g.wait_ge(T.sem.sl, nsl[0])

@@ -1,4 +1,3 @@
-import numpy as np
 from concourse.bass import DstId, RemoteDMATransfer
 from concourse.mybir import dt, AluOpType as Op, AxisListType, ActivationFunctionType as AF
 
@@ -6,6 +5,8 @@ N, P, K = 8, 128, 32
 REB = ((0, 2, 4, 6), (1, 3, 5, 7))
 NK = K // 4
 TINY = 2.0 ** -121
+PITCH = 512.0
+RND = 1.5 * 2.0 ** 23
 X4, U8, F32, I32, U16, BF = "float8_e4m3fn_x4", "uint8", "float32", "int32", "uint16", "bfloat16"
 
 
@@ -14,33 +15,30 @@ def _sb(n, d):
 
 
 SCRATCH = {
-    "tbt": _sb(544, BF), "ut": _sb(512, BF), "wt": _sb(512, BF), "hz": _sb(512, BF), "eb": _sb(2048, BF),
+    "tbt": _sb(544, BF), "ut": _sb(512, BF), "ut2": _sb(512, BF), "wt": _sb(512, BF), "hz": _sb(512, BF), "eb": _sb(516, BF),
     "t0": _sb(128, X4), "t0s": _sb(128, U8), "tr": _sb(128, X4), "trs": _sb(128, U8),
-    "uq": _sb(128, X4), "uqs": _sb(128, U8), "wq": _sb(128, X4), "wqs": _sb(128, U8),
-    "eq": _sb(512, X4), "eqs": _sb(512, U8),
-    "ur": _sb(256, X4), "urs": _sb(256, U8),
-    "t1": _sb(128, X4), "t1s": _sb(128, U8), "t2": _sb(128, X4), "t2s": _sb(128, U8),
-    "ones": _sb(256, F32), "ident": _sb(128, F32), "ck": _sb(576, F32), "dz": _sb(361, F32),
-    "pi": _sb(2, I32), "pj": _sb(4, I32), "cf": _sb(8, F32), "mk": _sb(4, F32), "rr": _sb(8, F32), "irow": _sb(32, F32),
-    "pr": _sb(8, I32), "prb": _sb(8, I32), "xr": _sb(16, F32), "xi": _sb(16, I32), "xj": _sb(16, I32), "kw": _sb(256, F32), "pf": _sb(1, F32),
-    "wr": _sb(8, F32), "w32": _sb(8, F32), "w0": _sb(8, F32), "dm": _sb(8, F32), "pm": _sb(8, F32), "c1": _sb(24, F32),
-    "src": _sb(16, F32), "tgt": _sb(16, F32), "lc": _sb(8, F32), "rm": _sb(8, F32), "kb": _sb(8, F32), "fac": _sb(128, F32), "seg": _sb(256, F32),
-    "d0": _sb(64, F32), "oz": _sb(16, U16),
-    "ag": _sb(16, F32), "agn": _sb(32, F32), "so": _sb(72, F32), "xo": _sb(361, F32), "xs": _sb(361, F32), "msk": _sb(288, F32),
-    "rep": _sb(9, F32), "junk": _sb(288, F32), "hit": _sb(192, F32), "hiti": _sb(64, I32), "gv": _sb(40, F32), "w40": _sb(40, F32), "gt": _sb(96, F32),
-    "lw": _sb(96, F32), "ysb": _sb(128, F32),
-    "ps": ("psum", [128, 512], F32), "da": ("psum", [128, 2048], F32), "db": ("psum", [128, 1536], F32),
+    "uq": _sb(128, X4), "uqs": _sb(128, U8), "u2": _sb(128, X4), "u2s": _sb(128, U8), "wq": _sb(128, X4), "wqs": _sb(128, U8),
+    "eq": _sb(512, X4), "eqs": _sb(512, U8), "tw": _sb(320, X4), "tws": _sb(320, U8), "t2": _sb(128, X4), "t2s": _sb(128, U8),
+    "sn": _sb(16, X4), "sns": _sb(16, U8),
+    "dz": _sb(657, BF), "ck": _sb(96, F32), "xs": _sb(192, F32), "so": _sb(192, F32), "fac": _sb(128, F32), "gg": _sb(193, F32),
+    "pi": _sb(4, I32), "pj": _sb(8, I32), "cf": _sb(16, F32), "irow": _sb(128, F32), "i16": _sb(128, F32), "dg": _sb(128, F32),
+    "m32": _sb(32, F32), "w16": _sb(24, F32), "co": _sb(16, U16), "tl": _sb(64, F32), "tq": _sb(64, F32), "to": _sb(320, F32),
+    "mk": _sb(64, F32), "val": _sb(64, F32), "sa": _sb(1024, BF), "sz": _sb(1024, BF), "rp": _sb(48, F32), "ki": _sb(48, I32), "ku": _sb(24, U16),
+    "ag": _sb(32, F32), "gv": _sb(40, F32), "w40": _sb(40, F32), "lw": _sb(96, F32), "hit": _sb(192, F32), "gs": _sb(768, F32),
+    "o1": _sb(8, U16), "ofx": _sb(48, F32), "oi": _sb(8, U16), "na": _sb(16, F32), "tk": _sb(32, F32), "rc": _sb(128, F32), "ng": _sb(64, F32),
+    "st": _sb(64, F32), "sub": _sb(128, F32), "sb": _sb(256, F32), "ysb": _sb(128, F32),
+    "ps": ("psum", [128, 2048], F32), "da": ("psum", [128, 2048], F32),
 }
 for _t in "01":
     SCRATCH.update({
-        "sc" + _t: _sb(32, X4), "ss" + _t: _sb(32, U8), "la" + _t: _sb(192, X4), "ls" + _t: _sb(192, U8),
+        "sc" + _t: _sb(32, X4), "ss" + _t: _sb(32, U8), "la" + _t: _sb(224, X4), "ls" + _t: _sb(224, U8),
         "or" + _t: _sb(128, X4), "os" + _t: _sb(128, U8), "h" + _t: _sb(512, BF), "nq" + _t: _sb(128, X4), "ns" + _t: _sb(128, U8),
-        "tw" + _t: _sb(256, X4), "tws" + _t: _sb(256, U8), "sb" + _t: _sb(256, F32),
-        "sr" + _t: _sb(64, F32), "ar" + _t: _sb(128, F32), "thr" + _t: _sb(128, F32), "g" + _t: _sb(193, F32), "yo" + _t: _sb(193, F32),
-        "yb" + _t: _sb(64, F32), "sm" + _t: _sb(32, F32), "of" + _t: _sb(2, U16), "vx" + _t: _sb(128, F32), "vr" + _t: _sb(96, F32), "vi" + _t: _sb(96, I32),
-        "bsb" + _t: _sb(64, F32), "rl" + _t: _sb(96, F32), "ol" + _t: _sb(4, U16), "ei" + _t: _sb(784, F32), "oi" + _t: _sb(8, U16),
+        "sr" + _t: _sb(64, F32), "ar" + _t: _sb(128, F32), "thr" + _t: _sb(128, F32), "yo" + _t: _sb(193, F32),
+        "yb" + _t: _sb(64, F32), "sm" + _t: _sb(8, F32), "of" + _t: _sb(6, U16), "ci" + _t: _sb(4, I32),
+        "bsb" + _t: _sb(64, F32), "rl" + _t: _sb(96, F32), "ol" + _t: _sb(4, U16),
     })
-SEMAPHORES = ["v", "a", "sl", "s_ck", "s_la0", "s_la1", "s_nw0", "s_nw1"] + ["e%d" % _i for _i in range(135)]
+NE, ND = 110, 28
+SEMAPHORES = ["sl", "s_ck", "s_la0", "s_la1", "s_na", "s_nb", "s_nw"] + ["e%d" % _i for _i in range(NE)] + ["d%d" % _i for _i in range(ND)]
 
 
 def rank_program(g, core, T, topo):
@@ -49,39 +47,96 @@ def rank_program(g, core, T, topo):
         return
     V, A, PE, SY = g.vector, g.scalar, g.tensor, g.sync
     X = AxisListType.X
-    used, nv, na, nsl, fin = [0], [0], [0], [0], []
+    QS = {"g": g, "V": V, "A": A, "P": PE, "S": SY}
 
-    def ev(ins, n=1):
-        s = T.sem["e%d" % used[0]]
-        used[0] += 1
-        ins.then_inc(s, n)
-        return (s, n)
+    ops = []
 
-    def wait(q, *evs):
-        for s, n in evs:
-            q.wait_ge(s, n)
+    def step(dma=False):
+        return {"n": 0, "used": False, "dma": dma, "ids": 0, "know": 0}
 
-    def v(ins):
-        ins.then_inc(T.sem.v, 1)
-        nv[0] += 1
+    def flatten(deps):
+        return [x for d in deps for x in (flatten(d) if isinstance(d, list) else [d])]
 
-    def vw():
-        V.wait_ge(T.sem.v, nv[0])
+    def op(q, fn, deps, s=None, dma=False):
+        s = step(dma) if s is None else s
+        s["n"] += 1
+        flat = flatten(deps)
+        for d in flat:
+            if isinstance(d, dict):
+                d["used"] = True
+        ops.append((q, fn, flat, s))
+        return s
 
-    def a(ins):
-        ins.then_inc(T.sem.a, 1)
-        na[0] += 1
+    def emit():
+        know = {q: 0 for q in QS}
+        pool = {False: [["e%d" % i, 0, 0] for i in range(NE)], True: [["d%d" % i, 0, 0] for i in range(ND)]}
+        for i, (q, fn, deps, s) in enumerate(ops):
+            for d in deps:
+                if not isinstance(d, dict):
+                    QS[q].wait_ge(d[0], d[1])
+                elif d["ids"] & ~know[q] or not d["waited"]:
+                    QS[q].wait_ge(T.sem[d["sem"]], d["top"])
+                    know[q] |= d["know"]
+                    d["waited"] = True
+            if fn is None:
+                continue
+            ins = fn()
+            if s["used"]:
+                w = 16 if s["dma"] else 1
+                if "sem" not in s:
+                    e = [x for x in pool[s["dma"]] if x[2] >= 0 and not x[2] & ~know[q]][0]
+                    pool[s["dma"]].remove(e)
+                    pool[s["dma"]].append(e)
+                    s.update(sem=e[0], top=e[1] + w * s["n"], left=s["n"], slot=e, waited=False)
+                    e[1], e[2] = s["top"], -1
+                ins.then_inc(T.sem[s["sem"]], w)
+                s["ids"] |= 1 << i
+                s["know"] |= know[q] | 1 << i
+                s["left"] -= 1
+                if not s["left"]:
+                    s["slot"][2] = s["ids"]
 
-    def aw():
-        A.wait_ge(T.sem.a, na[0])
-
-    def ts(out, i0, s1, op0, s2=None, op1=None):
+    def ts(out, i0, s1, op0, s2=None, op1=None, d=(), s=None):
         if op1 is None:
-            return V.tensor_scalar(out, i0, s1, None, op0)
-        return V.tensor_scalar(out, i0, s1, s2, op0, op1)
+            return op("V", lambda: V.tensor_scalar(out, i0, s1, None, op0), d, s)
+        return op("V", lambda: V.tensor_scalar(out, i0, s1, s2, op0, op1), d, s)
 
-    def tt(out, i0, i1, op):
-        return V.tensor_tensor(out, i0, i1, op)
+    def tt(out, i0, i1, o, d=(), s=None):
+        return op("V", lambda: V.tensor_tensor(out, i0, i1, o), d, s)
+
+    def cp(out, i0, d=(), s=None):
+        return op("V", lambda: V.tensor_copy(out, i0), d, s)
+
+    def ms(out, c, d=(), s=None):
+        return op("V", lambda: V.memset(out, c), d, s)
+
+    def red(out, i0, o, d=(), s=None, ab=False):
+        if ab:
+            return op("V", lambda: V.tensor_reduce(out, i0, X, o, apply_absolute_value=True), d, s)
+        return op("V", lambda: V.tensor_reduce(out, i0, X, o), d, s)
+
+    def scan(out, d0, d1, o1, d=(), s=None):
+        return op("V", lambda: V.tensor_tensor_scan(out, d0, d1, 0.0, Op.mult, o1), d, s)
+
+    def tp(out, i0, d=(), s=None):
+        return op("V", lambda: V.transpose(out, i0), d, s)
+
+    def qz(q, sc, i0, d=(), s=None):
+        return op("V", lambda: V.quantize_mx(q, sc, i0), d, s)
+
+    def act(out, i0, f=AF.Copy, d=(), s=None, **kw):
+        return op("A", lambda: A.activation(out, i0, f, **kw), d, s)
+
+    def mm(out, w, ws, x, xs_, d=()):
+        return op("P", lambda: PE.matmul_mx(out, w, ws, x, xs_, True, True), d)
+
+    def dma(q, out, i0, d=(), s=None):
+        return op(q, lambda: QS[q].dma_start(out, i0), d, s, True)
+
+    def iota(out, pat, base, cm, f=True):
+        if f:
+            return op("g", lambda: g.iota(out, pat, base, cm, allow_small_or_imprecise_dtypes=True), ())
+        return op("g", lambda: g.iota(out, pat, base, cm), ())
 
     def u8(view):
         return view.bitcast(dt.uint8)
@@ -91,507 +146,365 @@ def rank_program(g, core, T, topo):
 
     others = [r for r in range(N) if r != rank]
     EW = len(topo.engines(core, T.cores[others[0]]))
+    nsl, fin = [0], []
 
     def dst(r):
         rid, pid = topo.addr(T.cores[r], core)
         return DstId(rid=int(rid), pnc=int(pid))
 
-    def to_all(src, out, sem):
-        m = int(topo.mask(core, T.cores[others[0]]))
-        g.remote_dma_fused([RemoteDMATransfer(dst_ids=[dst(r) for r in others], dma_engine_mask=m, remote_sem=sem, srcs=[src], dsts=[out for r in others])], local_sem=T.sem.sl)
+    def to_many(rs, src, out, sem, d):
+        m = int(topo.mask(core, T.cores[rs[0]]))
         nsl[0] += EW
+        op("g", lambda: g.remote_dma_fused([RemoteDMATransfer(dst_ids=[dst(r) for r in rs], dma_engine_mask=m, remote_sem=sem, srcs=[src], dsts=[out for r in rs])], local_sem=T.sem.sl), d)
 
-    def to_rebuilders(pairs, sem):
-        tr = []
-        for i, (r, s, d) in enumerate(pairs):
-            es = topo.engines(core, T.cores[r])
-            w = len(es) // 4
-            m = 0
-            for e in es[w * i:w * i + w]:
-                m |= 1 << e
-            tr.append(RemoteDMATransfer(dst_ids=[dst(r)], dma_engine_mask=m, remote_sem=sem, srcs=[s], dsts=[d]))
-            nsl[0] += w
-        g.remote_dma_fused(tr, local_sem=T.sem.sl)
+    def to_each(pairs, sem, d, wide):
+        tr, w, e0 = [], EW // 4, 0
+        for i, (r, s, o) in enumerate(pairs):
+            n = 2 * w if len(pairs) == 3 and i == wide else w
+            m = sum(1 << e for e in topo.engines(core, T.cores[r])[e0:e0 + n])
+            tr.append(RemoteDMATransfer(dst_ids=[dst(r)], dma_engine_mask=m, remote_sem=sem, srcs=[s], dsts=[o]))
+            nsl[0] += n
+            e0 += n
+        op("g", lambda: g.remote_dma_fused(tr, local_sem=T.sem.sl), d)
 
     mine = [t for t in range(2) if rank in REB[t]][0]
+    I = REB[mine].index(rank)
+    la, ls, od, os_, h, nq, ns = (T["%s%d" % (n, mine)] for n in ("la", "ls", "or", "os", "h", "nq", "ns"))
+    x0 = 64 * (I & 1) if mine == 0 else 0
+    ones, dzc, dz0, dz1, dzr, seg = T.dz[:, 0:128], T.dz[:, 0:193], T.dz[:, 193:273], T.dz[:, 273:465], T.dz[:, 465:529], T.dz[:, 529:657]
+    rr = T.irow[:, 0:8]
+    p8, p16, p32, q1, pf = (T.cf[:, i:i + 1] for i in range(5))
+    hp = T.cf[:, 5:7]
 
-    e_tb = ev(SY.dma_start(T.tbt[:, 0:512], T.tb[:, 0:512]), 16)
-    e_tb2 = ev(A.dma_start(T.tbt[:, 512:544], T.tb[:, 0:32]), 16)
-    e_u0 = ev(A.dma_start(T.ut[:, 0:4], T.u[:, 0:4]), 16)
-    e_u1 = ev(A.dma_start(T.ut[:, 4:16], T.u[:, 0:12]), 16)
+    e_tb = dma("S", T.tbt[:, 0:512], T.tb[:, 0:512])
+    e_u = dma("A", T.ut[:, 0:8], T.u[:, 0:8])
+    e_tb2 = dma("A", T.tbt[:, 512:544], T.tb[:, 0:32])
+    i_pi = iota(T.pi[:], [[1, 2], [0, 2]], 0, 1, False)
+    i_ir = iota(T.irow[:], [[1, P]], 0, 0)
+    i_tl = iota(T.tl[:], [[0, 8], [-1, 8]], 7, 0)
+    i_tq = iota(T.tq[:], [[1, 8], [0, 8]], 0, 0)
+    i_16 = iota(T.i16[:], [[0, 8], [1, 16]], 0, 0)
+    z_ut = ms(T.ut[:, 8:512], 0.0)
+    z_hz = ms(T.hz[:], 0.0)
+    z_dz = ms(T.dz[:], 1.0)
+    z_na = ms(T.na[:], 0.0)
+    e_uq = qz(T.uq[:], T.uqs[:], T.ut[:], [z_ut, e_u])
+    e_t0 = qz(T.t0[:], T.t0s[:], T.tbt[:, 0:512], [e_tb])
+    e_tr = qz(T.tr[:], T.trs[:], T.tbt[:, 4 * rank:4 * rank + 512], [e_tb2])
+    m0 = mm(T.ps[:, 0:128], T.t0[:], T.t0s[:], T.uq[:], T.uqs[:], [e_uq, e_t0])
+    m1 = mm(T.ps[:, 512:640], T.tr[:], T.trs[:], T.uq[:], T.uqs[:], [e_tr])
+    o = 4 * rank
+    e_c = cp(T.ck[:, o:o + 2], T.ps[:, 0:2], [m0, z_na])
+    cp(T.ck[:, o + 2:o + 4], T.ps[:, 512:514], [m1], e_c)
+    to_many(sorted(others, key=lambda r: r in REB[0]), T.ck[:, o:o + 4], T.ck[:, o:o + 4], T.sem.s_ck, [e_c])
+    e_w = dma("S", T.wt[:], T.w[:, 0:512], [e_c])
+    z_eb = ms(T.eb[:], 0.0)
+    i_eb = op("g", lambda: g.affine_select(T.eb[:, 3:515:4], ones, [[-1, P]], Op.is_equal, 0.0, 0, 1), [z_eb, z_dz])
+    i_v0 = iota(T.val[:, 0:32], [[2, K]], 33, 0)
+    i_v1 = iota(T.val[:, 32:64], [[1, K]], 160, 0)
+    i_p8 = iota(T.cf[:, 8:9], [[0, 1]], 7, 8)
+    i_pn = iota(T.cf[:, 9:10], [[0, 1]], 64, -1)
 
-    def iota(out, pat, base, cm, f=True):
-        if f:
-            return ev(g.iota(out, pat, base, cm, allow_small_or_imprecise_dtypes=True))
-        return ev(g.iota(out, pat, base, cm))
-    i_pi = iota(T.pi[:, 0:2], [[1, 2]], 0, 1, False)
-    i_rr = iota(T.rr[:, 0:8], [[1, 8]], 0, 0)
-    i_ir = iota(T.irow[:, 0:32], [[1, 32]], 0, 0)
-    i_pf = iota(T.pf[:, 0:1], [[0, 1]], 0, 1)
-    i_pr = iota(T.pr[:, 0:8], [[1, 8]], 0, 1, False)
-    i_x0 = iota(T.xr[:, 0:8], [[16, 8]], rank, 0)
-    i_x1 = iota(T.xr[:, 8:16], [[16, 8]], P - rank, 0)
+    k_a = act(T.xs[:, 128:129], T.dz[:, 0:1], d=[z_dz, z_hz], scale=-TINY)
+    act(T.xs[:, 129:192], T.hz[:, 0:63], s=k_a)
+    for a, b in ((130, 145), (146, 177), (178, 193)):
+        act(T.gg[:, a:b], T.dz[:, 0:b - a], s=k_a, scale=-PITCH)
+    act(T.gg[:, 145:178:32], T.dz[:, 0:2], s=k_a, scale=15 * PITCH)
+    act(T.dz[:, 128:129], T.dz[:, 0:1], s=k_a, scale=PITCH)
+    act(T.dz[:, 201:242:40], T.dz[:, 0:2], s=k_a, scale=-1.0)
+    k_b = act(T.dz[:, 289:434:144], T.dz[:, 0:2], scale=-1.0)
+    act(T.dz[:, 465:529:8], T.hz[:, 0:8], s=k_b)
+    act(T.dz[:, 466:529:8], T.dz[:, 0:8], s=k_b, scale=-1.0)
+    act(T.dz[:, 529:657:16], T.hz[:, 0:8], s=k_b)
+    k_h = act(h[:], T.hz[:])
+    k_s = act(T.sa[:, 0:512], T.hz[:])
+    act(T.sa[:, 512:1024], T.hz[:], s=k_s)
+    if mine == 0:
+        k_u = act(T.ut2[:], T.hz[:])
+        k_u2 = step()
+        for n in range(4):
+            act(T.ut2[:, 128 * n:128 * n + 8], T.ut[:, 0:8], d=[k_u, e_u], s=k_u2)
 
-    v(V.memset(T.ut[:, 16:512], 0.0))
-    e_hz = ev(V.memset(T.hz[:], 0.0))
-    e_ones = ev(V.memset(T.ones[:], 1.0))
-    wait(g, e_ones)
-    e_id = ev(g.affine_select(T.ident[:], T.ones[:, 0:128], [[-1, 128]], Op.is_equal, 0.0, 0, 1))
-    i_kw = iota(T.kw[:, 0:256], [[0, 8], [1, 32]], P, 0)
-    wait(V, i_pi)
-    v(ts(T.pj[:, 2:3], T.pi[:, 0:1], 7, Op.bitwise_and))
-    v(ts(T.pj[:, 0:1], T.pi[:, 0:1], 15, Op.bitwise_and))
-    v(ts(T.pj[:, 1:2], T.pi[:, 0:1], 31, Op.bitwise_and))
-    v(ts(T.pj[:, 3:4], T.pi[:, 1:2], 7, Op.bitwise_and))
-    vw()
-    v(ts(T.mk[:, 0:1], T.pj[:, 2:3], float(rank), Op.is_equal))
-    v(ts(T.mk[:, 1:2], T.pj[:, 2:3], float(rank), Op.not_equal))
-    v(ts(T.mk[:, 2:3], T.pj[:, 2:3], float(rank), Op.not_equal))
-    v(V.tensor_copy(T.cf[:, 0:4], T.pj[:, 0:4]))
-    vw()
-    p16, p32, p8, q1 = (T.cf[:, i:i + 1] for i in range(4))
-    wait(V, e_u0, e_u1)
-    e_uq = ev(V.quantize_mx(T.uq[:], T.uqs[:], T.ut[:]))
-    wait(V, e_tb)
-    e_t0 = ev(V.quantize_mx(T.t0[:], T.t0s[:], T.tbt[:, 0:512]))
-    wait(V, e_tb2)
-    e_tr = ev(V.quantize_mx(T.tr[:], T.trs[:], T.tbt[:, 4 * rank:4 * rank + 512]))
-    wait(PE, e_uq, e_t0)
-    e_m0 = ev(PE.matmul_mx(T.ps[:, 0:128], T.t0[:], T.t0s[:], T.uq[:], T.uqs[:], True, True))
-    wait(PE, e_tr)
-    e_m1 = ev(PE.matmul_mx(T.db[:, 0:128], T.tr[:], T.trs[:], T.uq[:], T.uqs[:], True, True))
-    o = 8 * rank
-    wait(V, e_m0)
-    e_c0 = ev(tt(T.ck[:, o:o + 3], T.ps[:, 0:3], T.mk[:, 0:3], Op.mult))
-    wait(V, e_m1)
-    e_c1 = ev(V.tensor_copy(T.ck[:, o + 3:o + 5], T.db[:, 1:3]))
-    wait(g, e_c0, e_c1)
-    to_all(T.ck[:, o:o + 5], T.ck[:, o:o + 5], T.sem.s_ck)
-    wait(SY, e_t0)
-    e_tw0 = [ev(SY.dma_start(u8(T.tw0[:, 0:128]), u8(T.t0[:])), 16), ev(SY.dma_start(T.tws0[:, 0:128], T.t0s[:]), 16)]
-    e_w = ev(SY.dma_start(T.wt[:], T.w[:, 0:512]), 16)
+    k1 = ts(T.pj[:, 0:1], T.pi[:, 0:1], 7, Op.bitwise_and, d=[i_pi])
+    ts(T.pj[:, 1:2], T.pi[:, 0:1], 15, Op.bitwise_and, s=k1)
+    ts(T.pj[:, 2:3], T.pi[:, 0:1], 31, Op.bitwise_and, s=k1)
+    ts(T.pj[:, 3:4], T.pi[:, 2:3], 7, Op.bitwise_and, s=k1)
+    ts(T.pj[:, 5:7], T.pi[:, 0:2], 4, Op.arith_shift_right, 1, Op.bitwise_and, s=k1)
+    cp(T.pj[:, 4:5], T.pi[:, 0:1], s=k1)
+    k3 = ts(T.w16[:, 16:24], rr, -0.125, Op.mult, 1.0, Op.add, d=[i_ir])
+    k2 = cp(T.cf[:, 0:7], T.pj[:, 0:7], [k1])
+    e_la = qz(la[:, 96:224], ls[:, 96:224], T.hz[:], [z_hz])
+    ts(T.m32[:, 0:8], rr, p8, Op.not_equal, d=[k2], s=k3)
+    ts(T.cf[:, 7:8], p32, pf, Op.subtract, float(P), Op.add, s=k3)
+    k4 = ts(T.m32[:, 8:16], rr, p8, Op.not_equal, -1.0, Op.mult)
+    ts(T.m32[:, 16:24], rr, p8, Op.is_equal, s=k4)
+    ts(T.m32[:, 24:32], rr, p8, Op.not_equal, s=k4)
+    ts(T.co[:, 0:1], p8, 4.0, Op.mult, 1.0, Op.add, s=k4)
+    ts(T.co[:, 1:2], p8, 4.0, Op.mult, s=k4)
+    ts(T.fac[:, 0:32], T.irow[:, 0:32], p32, Op.is_ge, 1.0 - 2.0 ** -24, Op.max, s=k4)
+    ts(T.gg[:, 128:129], pf, 1.0 - 4.5 / 8, Op.add, s=k4)
+    tt(T.w16[:, 0:8], T.w16[:, 16:24], T.m32[:, 0:8], Op.mult, [k3], k4)
+    tt(T.w16[:, 8:16], T.w16[:, 16:24], T.m32[:, 0:8], Op.mult, s=k4)
+    ts(T.fac[:, 32:128], T.irow[:, 32:128], T.cf[:, 7:8], Op.is_lt, 1.0 - 2.0 ** -24, Op.max, s=k4)
 
-    wait(A, e_hz, e_ones)
-    e_k0 = ev(A.activation(T.ck[:, 72:576], T.hz[:, 0:504], AF.Copy))
-    e_k1 = ev(A.activation(T.dz[:, 0:256], T.ones[:], AF.Copy))
-    e_k2 = ev(A.activation(T.dz[:, 256:361], T.ones[:, 0:105], AF.Copy))
-    for b in range(4):
-        a(A.activation(T.eb[:, 512 * b:512 * b + 512], T.hz[:], AF.Copy))
-    e_k3 = ev(A.activation(T.d0[:], T.ones[:, 0:64], AF.Copy))
-    wait(A, e_id)
-    aw()
-    for b in range(4):
-        a(A.activation(T.eb[:, 512 * b + b:512 * b + 512:4], T.ident[:], AF.Copy))
-    a(A.activation(T.seg[:], T.ones[:], AF.Copy))
-    aw()
-    e_seg = ev(A.activation(T.seg[:, 0:256:32], T.hz[:, 0:8], AF.Copy))
-    e_eb = ev(A.activation(T["h%d" % mine][:], T.hz[:], AF.Copy))
-
-    wait(V, e_hz, e_ones, e_uq, e_t0, e_tr, e_c0, e_c1)
-    wait(V, i_rr, i_ir, i_pr, i_x0, i_x1, i_pf, i_kw)
-    v(ts(T.fac[:, 0:32], T.irow[:], p32, Op.is_lt, -2.0 ** -24, Op.mult))
-    v(V.memset(T.fac[:, 32:128], 1.0))
-    v(V.memset(T.ck[:, 64:72], -TINY))
-    v(V.memset(T.xs[:, 297:298], -TINY))
-    v(V.memset(T.xs[:, 298:361], 0.0))
-    v(V.memset(T.g0[:, 130:193], -1.0))
-    v(V.memset(T.g1[:, 130:193], -1.0))
-    v(ts(T.wr[:], T.rr[:], -1.0 / 8192, Op.mult, 8.0 / 8192, Op.add))
-    v(ts(T.w32[:], T.rr[:], -1.0 / 32, Op.mult, 8.0 / 32, Op.add))
-    v(ts(T.gt[:, 0:8], T.rr[:], p8, Op.not_equal))
-    v(ts(T.prb[:], T.pr[:], 127, Op.bitwise_and))
-    v(ts(T.xi[:], T.xr[:], p16, Op.add))
-    v(ts(T.lc[:, 6:7], p16, 8.0, Op.is_ge, -1000.0, Op.mult))
-    v(ts(T.lc[:, 7:8], p16, 8.0, Op.is_lt, -1000.0, Op.mult))
-    v(ts(T.dm[:], T.rr[:], q1, Op.not_equal))
-    v(ts(T.pm[:], T.rr[:], q1, Op.is_equal))
-    vw()
-    wait(V, e_k0, e_k1, e_k2)
-    v(ts(T.fac[:, 0:32], T.fac[:, 0:32], 1.0, Op.add))
-    for b in range(1, 4):
-        v(V.memset(T.fac[32 * b:32 * b + 32, 128 - 32 * b:128], 1.0 - 2.0 ** -24))
-    for gg in (T.g0, T.g1):
-        v(V.memset(gg[:, 145:146], 15.0))
-        v(V.memset(gg[:, 177:178], 15.0))
-        v(ts(gg[:, 128:129], T.pf[:], 1.0 / 256, Op.mult))
-    v(V.memset(T.dz[:, 329:330], -1.0))
-    v(tt(T.w0[:], T.gt[:, 0:8], T.wr[:], Op.mult))
-    v(ts(T.rm[:, 0:8:2], T.rr[:, 0:8:2], T.lc[:, 6:7], Op.add))
-    v(ts(T.rm[:, 1:8:2], T.rr[:, 1:8:2], T.lc[:, 7:8], Op.add))
-    v(ts(T.lc[:, 0:1], p8, -1.0, Op.add))
-    v(ts(T.lc[:, 1:2], p8, 0.0, Op.is_equal, 8.0, Op.mult))
-    v(ts(T.lc[:, 2:3], p16, 8.0, Op.is_lt, 64.0, Op.mult))
-    v(ts(T.lc[:, 3:4], p16, 8.0, Op.is_ge, 64.0, Op.mult))
-    v(ts(T.lc[:, 4:5], p8, -1.0, Op.add, 8.0, Op.mult))
-    v(V.tensor_copy(T.c1[:, 0:8], T.prb[:]))
-    v(ts(T.xj[:], T.xi[:], 127, Op.bitwise_and))
-    v(V.memset(T.oz[:, 0:8], 0))
-    v(V.memset(T.oz[:, 8:16], 2))
-    e_fac = ev(V.quantize_mx(T.tw0[:, 128:256], T.tws0[:, 128:256], T.hz[:]))
-    vw()
-    wait(V, e_fac, e_k3)
-    v(ts(T.kb[:], T.rm[:], T.lc[:, 4:5], Op.add))
-    v(V.memset(T.d0[:, 0:64:8], 0.0))
-    v(V.memset(T.d0[:, 1:64:8], -1.0))
-    v(V.tensor_copy(T.src[:], T.xj[:]))
-    e_oz = ev(tt(T.c1[:, 8:16], T.c1[:, 0:8], T.w32[:], Op.add))
-    v(V.quantize_mx(T["la%d" % mine][:, 64:192], T["ls%d" % mine][:, 64:192], T.hz[:]))
-    v(V.quantize_mx(T["or%d" % mine][:], T["os%d" % mine][:], T.hz[:]))
-    vw()
-    wait(V, e_oz)
-    v(ts(T.tgt[:], T.src[:], (8 - rank) / 32.0, Op.add))
-    v(tt(T.c1[:, 16:24], T.c1[:, 8:16], T.pm[:], Op.mult))
-    im1, is08, lo64, hi64 = (T.lc[:, i:i + 1] for i in range(4))
+    def rebuilder_constants():
+        a = ts(T.cf[:, 10:11], p8, -1.0, Op.add)
+        ts(T.cf[:, 11:12], p8, 0.0, Op.is_equal, s=a)
+        ts(T.cf[:, 12:13], p16, 8.0, Op.is_ge, -1000.0, Op.mult, s=a)
+        ts(T.cf[:, 13:14], p16, 8.0, Op.is_lt, -1000.0, Op.mult, s=a)
+        ms(T.mk[:], 0.0, s=a)
+        e_or = qz(od[:], os_[:], T.hz[:])
+        b = ts(T.to[:, 64:128], T.tq[:], T.cf[:, 10:11], Op.is_le, T.cf[:, 10:11], Op.add, d=[a, i_tq])
+        ts(T.to[:, 128:192], T.tq[:], T.cf[:, 11:12], Op.mult, s=b)
+        s = NK * I
+        e = ts(T.mk[:, s:s + 8:2], T.irow[:, 0:8:2], T.cf[:, 12:13], Op.add)
+        ts(T.mk[:, s + 1:s + 8:2], T.irow[:, 1:8:2], T.cf[:, 13:14], Op.add, s=e)
+        c = tt(T.to[:, 192:256], T.to[:, 64:128], T.to[:, 128:192], Op.max, [b])
+        if mine:
+            ts(T.mk[:, 32 + s:40 + s:2], T.hz[:, 0:4], T.cf[:, 12:13], Op.add, s=e)
+            ts(T.mk[:, 33 + s:40 + s:2], T.hz[:, 0:4], T.cf[:, 13:14], Op.add, s=e)
+        d_ = tt(T.to[:, 64:128], T.to[:, 192:256], T.tl[:], Op.is_equal, [c, i_tl])
+        ts(T.to[:, 128:192], T.to[:, 192:256], 8.0, Op.mult, s=d_)
+        f = ts(T.to[:, 256:320], T.to[:, 64:128], 96.0, Op.mult, d=[d_])
+        tt(T.to[:, 0:64], T.to[:, 256:320], T.to[:, 128:192], Op.max, [f], e)
+        return [e, e_or]
 
     def unpacker():
-        wait(V, e_eb)
-        return ev(V.quantize_mx(T.eq[:], T.eqs[:], T.eb[:]))
+        s = step()
+        for b in range(4):
+            qz(T.eq[:, 128 * b:128 * b + 128], T.eqs[:, 128 * b:128 * b + 128], T.eb[:, 3 - b:515 - b], [i_eb], s)
+        return s
 
-    def turn(buf, o, w, n, k):
-        m = (n + k) % 4
-        return buf[32 * n:32 * n + 32, o + k * w:o + k * w + w], buf[32 * m:32 * m + 32, o:o + w]
+    def second_constants():
+        a = ts(T.rp[:, 8:15], T.irow[:, 0:7], q1, Op.is_ge)
+        ts(T.rp[:, 16:23], T.irow[:, 0:7], q1, Op.is_lt, s=a)
+        ts(T.cf[:, 14:15], p16, 8.0, Op.mult, 7.0 - rank, Op.add, s=a)
+        ts(T.cf[:, 15:16], p16, 8.0, Op.mult, 1031.0 - 9 * rank, Op.add, s=a)
+        z = ts(T.dg[:], T.i16[:], p16, Op.is_equal, d=[i_16])
+        b = cp(T.rp[:, 0:1], q1)
+        tt(T.rp[:, 1:8], T.rp[:, 8:15], T.irow[:, 0:7], Op.add, [a], b)
+        c = ts(T.ki[:, 8:16], rr, 128.0, Op.mult, T.cf[:, 14:15], Op.add)
+        ts(T.ki[:, 16:24], rr, 128.0, Op.mult, T.cf[:, 15:16], Op.add, s=c)
+        ts(T.ofx[:, 0:8], rr, 16.0, Op.mult, p16, Op.add, s=z)
+        ts(T.ki[:, 0:8], T.rp[:, 0:8], 7.0, Op.mult, T.cf[:, 8:9], Op.add, d=[b, i_p8], s=c)
+        ts(T.rp[:, 24:32], T.rp[:, 0:8], 4.0, Op.mult, 2.0, Op.add, s=z)
+        ts(T.rp[:, 32:39], T.rp[:, 1:8], -0.125, Op.mult, 1.0, Op.add, s=z)
+        e = ts(T.ki[:, 24:48], T.ki[:, 0:24], 1023, Op.bitwise_and, d=[c])
+        for f in range(2):
+            for e2 in range(2):
+                v = [8 + f if mine == 0 and i == I else 2 * i + f for i in (2 * e2, 2 * e2 + 1)]
+                c0 = 4 + 4 * f + 2 * e2
+                ts(T.co[:, c0:c0 + 2], hp, float(v[1] - v[0]), Op.mult, float(v[0]), Op.add, s=z)
+        cp(T.ku[:], T.ki[:, 24:48], [e], z)
+        return [z, a]
 
-    def half(buf, o, w, n):
-        return buf[64 * n:64 * n + 64, o + 2 * w:o + 3 * w], buf[64 - 64 * n:128 - 64 * n, o:o + w]
+    if mine == 0:
+        k_r = rebuilder_constants()
+        k_sn = ts(T.co[:, 2:3], p8, 8.0, Op.mult, x0 + 7.0, Op.add)
 
-    def order(t, so, e_s, lost, e_tab):
-        sr, ar, thr, gg, yo, yb, sm = (T["%s%d" % (n, t)] for n in ("sr", "ar", "thr", "g", "yo", "yb", "sm"))
-        lost[0]()
-        wait(A, e_s, e_fac)
-        e_th = ev(A.activation(thr[:], T.fac[:], AF.Abs, scale=so[0]))
-        wait(V, e_s)
-        e_tp = ev(V.transpose(sr[:], so[1]))
-        vw()
-        lost[1]()
-        wait(V, e_tp)
-        wait(A, e_tp)
-        vw()
+    def order(t, e_s, s_col, s_rep, vals, wts, e_v, before):
+        sr, ar, thr, yo, yb, sm, of = (T["%s%d" % (n, t)] for n in ("sr", "ar", "thr", "yo", "yb", "sm", "of"))
+        n = vals[1] - vals[0]
+        gv = vals[2][:, vals[0]:vals[1]]
+        l0 = red(sm[:, 6:7], gv, Op.max, [e_v])
+        e_th = act(thr[:], T.fac[:], AF.Abs, [e_s, k4], scale=s_col)
+        e_tp = tp(sr[:], s_rep, [e_s])
+        l1 = ts(T.lw[:, 0:n], gv, sm[:, 6:7], Op.is_equal, d=[l0, before])
+        sz = step()
 
-        def size(p0, p1, c, q0, q1):
-            v(tt(ar[p0:p1, c:c + 32], sr[q0:q1, 0:32], sr[q0:q1, 32:64], Op.max))
-        size(0, 128, 0, 0, 128)
+        def size(p0, p1, c, q0, q1_, d=()):
+            tt(ar[p0:p1, c:c + 32], sr[q0:q1_, 0:32], sr[q0:q1_, 32:64], Op.max, d, sz)
+        size(0, 128, 0, 0, 128, [e_tp])
         size(0, 64, 64, 64, 128)
         size(64, 128, 64, 0, 64)
-        for n in range(3):
-            size(32 * n, 32 * n + 32, 32, 32 * n + 32, 32 * n + 64)
-        for n in range(4):
-            m = (n + 3) % 4
-            a(A.activation(ar[32 * n:32 * n + 32, 96:128], sr[32 * m:32 * m + 32, 0:32], AF.Abs))
-        e_tn = ev(A.activation(ar[96:128, 32:64], sr[0:32, 0:32], AF.Abs))
-        lost[2]()
-        vw()
-        wait(V, e_th, e_tn)
-        V.wait_ge(T.sem.a, na[0])
-        v(tt(gg[:, 0:128], ar[:], thr[:], Op.is_gt))
-        lost[3]()
-        vw()
-        v(V.tensor_tensor_scan(yo[:], T.dz[:, 0:193], gg[:], 0.0, Op.mult, Op.add))
-        vw()
-        v(V.transpose(yb[:], yo[:, 129:193]))
-        vw()
-        e_z0 = ev(V.tensor_reduce(sm[:, 8:9], yb[:, 0:32], X, Op.min, apply_absolute_value=True))
-        e_z1 = ev(V.tensor_reduce(sm[:, 9:10], yb[:, 32:64], X, Op.min, apply_absolute_value=True))
-        wait(A, e_z0, e_z1)
-        wait(V, e_z0, e_z1)
-        for n in range(4):
-            v(V.tensor_copy(*turn(sm, 8, 2, n, 1)))
-        v(V.tensor_copy(*half(sm, 8, 2, 0)))
-        for n in range(4):
-            a(A.activation(*turn(sm, 8, 2, n, 3), AF.Copy))
-        e_zn = ev(A.activation(*half(sm, 8, 2, 1), AF.Copy))
-        vw()
-        wait(V, e_zn)
-        V.wait_ge(T.sem.a, na[0])
-        v(V.tensor_reduce(sm[:, 16:17], sm[:, 8:16:2], X, Op.min))
-        v(V.tensor_reduce(sm[:, 17:18], sm[:, 9:16:2], X, Op.min))
-        vw()
-        of = T["of%d" % t]
-        e_of = ev(ts(of[:], sm[:, 16:18], 256.0, Op.mult))
-        tab, tabs = (T.t0, T.t0s) if t == 0 else (T.t1, T.t1s)
-        sc, ss, la, ls = (T["%s%d" % (n, t)] for n in ("sc", "ss", "la", "ls"))
-        wait(V, *e_tab)
-        wait(A, *e_tab)
-        wait(V, e_of)
-        wait(A, e_of)
-        e_sc = ev(V.tensor_copy(u32(sc[:]), u32(tab[:, 0:128]).indirect(of[:])))
-        e_ss = ev(A.activation(ss[:], tabs[:, 0:128].indirect(of[:]), AF.Copy))
-        sl = slice(NK * rank, NK * rank + NK)
-        wait(g, e_sc)
-        to_rebuilders([(r, u8(sc[:, NK * i:NK * i + NK]), u8(la[:, sl])) for i, r in enumerate(REB[t]) if r != rank], T.sem["s_la%d" % t])
-        wait(g, e_ss)
-        to_rebuilders([(r, ss[:, NK * i:NK * i + NK], ls[:, sl]) for i, r in enumerate(REB[t]) if r != rank], T.sem["s_la%d" % t])
-        own = []
-        if rank in REB[t]:
-            i = REB[t].index(rank)
-            wait(SY, e_sc)
-            own.append(ev(SY.dma_start(u8(la[:, sl]), u8(sc[:, NK * i:NK * i + NK])), 16))
-            wait(SY, e_ss)
-            own.append(ev(SY.dma_start(ls[:, sl], ss[:, NK * i:NK * i + NK]), 16))
-        vx, vr, vi, bsb = T["vx%d" % t], T["vr%d" % t], T["vi%d" % t], T["bsb%d" % t]
-        for h in range(2):
-            v(ts(vx[:, 32 * h:32 * h + 32], T.ones[:, 0:32], sm[:, 16 + h:17 + h], Op.mult, 256.0, Op.mult))
-        vw()
-        v(V.transpose(vx[:, 64:128], vx[:, 0:64]))
-        vw()
-        for h in range(2):
-            s = vx[:, 64 + 32 * h:80 + 32 * h]
-            v(V.tensor_copy(vi[:, 16 * h:16 * h + 16], s))
-            if t:
-                v(ts(vi[:, 32 + 16 * h:48 + 16 * h], s, float(t), Op.add))
-            v(V.tensor_copy(vr[:, 16 * h:16 * h + 16], s))
-        vw()
-        v(V.tensor_copy(bsb[:, 0:32], vi[:, 0:32]))
-        v(ts(vi[:, 64:96], vi[:, 32 * t:32 * t + 32], 7, Op.bitwise_and))
-        vw()
-        v(tt(vr[:, 32:64], vr[:, 0:32], bsb[:, 0:32], Op.subtract))
-        v(V.tensor_copy(vr[:, 64:96], vi[:, 64:96]))
-        vw()
-        e_b = ev(ts(bsb[:, 32:64], vr[:, 32:64], -32.0, Op.mult, 8.0, Op.add))
-        wait(SY, e_b)
-        fin.append(ev(SY.dma_start(T.bs[2 * t:2 * t + 2, 0:32], bsb[0:1, 0:64]), 16))
-        return own, e_b
-
-    def rebuild_list(t, e_b):
-        s = NK * REB[t].index(rank)
-        vr, bsb, rl, ol = T["vr%d" % t], T["bsb%d" % t], T["rl%d" % t], T["ol%d" % t]
-        q, lost = vr[:, 64 + s:72 + s], bsb[:, 32 + s:40 + s]
-        v(ts(rl[:, 0:8], q, im1, Op.is_le, float(NK), Op.mult))
-        v(ts(rl[:, 8:16], q, im1, Op.is_le))
-        v(ts(rl[:, 16:24], q, is08, Op.mult))
-        vw()
-        wait(V, e_b)
-        v(tt(rl[:, 24:32], lost, rl[:, 8:16], Op.subtract))
-        v(tt(rl[:, 32:40], rl[:, 0:8], T.kb[:], Op.add))
-        v(tt(rl[:, 40:48], rl[:, 16:24], T.rm[:], Op.add))
-        vw()
-        v(ts(rl[:, 48:56:2], rl[:, 24:32:2], im1, Op.is_equal, lo64, Op.mult))
-        v(ts(rl[:, 49:56:2], rl[:, 25:32:2], im1, Op.is_equal, hi64, Op.mult))
-        v(tt(rl[:, 56:64], rl[:, 32:40], rl[:, 40:48], Op.max))
-        vw()
-        v(tt(rl[:, 64:72], rl[:, 48:56], rl[:, 56:64], Op.max))
-        vw()
-        v(tt(rl[:, 72:76], rl[:, 64:72:2], rl[:, 65:72:2], Op.max))
-        vw()
-        return ev(V.tensor_copy(ol[:], rl[:, 72:76]))
-
-    def rebuild(t, own, e_ol, e_eq, e_free):
-        la, ls, od, os_, h, nq, ns, sb, ol = (T["%s%d" % (n, t)] for n in ("la", "ls", "or", "os", "h", "nq", "ns", "sb", "ol"))
-        D, banks = (T.da, 4) if t == 0 else (T.db, 3)
-        arr = (T.sem["s_la%d" % t], 7 * 2 * (EW // 4))
-        wait(V, e_ol, e_eq, *own)
-        wait(V, arr)
-        e_oc = ev(V.tensor_copy(u32(od[:, 0:64]), u32(la[:, 0:96]).indirect(ol[:])))
-        wait(A, e_ol, *own)
-        wait(A, arr)
-        e_os = ev(A.activation(os_[:, 0:64], ls[:, 0:96].indirect(ol[:]), AF.Copy))
-        wait(PE, *e_free)
-        wait(PE, e_eq, e_oc, e_os)
-        scans, cps = [], []
-        for b in range(4):
-            k = 512 * (b % banks)
-            if b >= banks:
-                wait(PE, scans[b - banks])
-            e_d = ev(PE.matmul_mx(D[:, k:k + 128], T.eq[:, 128 * b:128 * b + 128], T.eqs[:, 128 * b:128 * b + 128], od[:], os_[:], True, True))
-            wait(V, e_d)
-            scans.append(ev(V.tensor_tensor_scan(sb[:, 64 * b:64 * b + 64], T.d0[:], D[:, k:k + 64], 0.0, Op.mult, Op.subtract)))
+        l2 = tt(T.lw[:, 48:48 + n], T.lw[:, 0:n], wts, Op.mult, [l1])
         for b in range(3):
-            wait(A, scans[b])
-            cps.append(ev(A.activation(h[:, b:4 * NK:4], sb[:, 64 * b + 7:64 * b + 64:8], AF.Copy)))
-        wait(V, scans[3])
-        cps.append(ev(V.tensor_copy(h[:, 3:4 * NK:4], sb[:, 199:256:8])))
-        wait(V, e_eb, *scans)
-        wait(V, *cps)
-        e_nq = ev(V.quantize_mx(nq[:], ns[:], h[:]))
-        i = REB[t].index(rank)
-        sl = slice(P + NK * i, P + NK * i + NK)
-        tw, tws = T["tw%d" % t], T["tws%d" % t]
-        wait(g, e_nq)
-        to_all(u8(nq[:, 0:NK]), u8(tw[:, sl]), T.sem["s_nw%d" % t])
-        to_all(ns[:, 0:NK], tws[:, sl], T.sem["s_nw%d" % t])
-        wait(SY, e_nq)
-        return [ev(SY.dma_start(u8(tw[:, sl]), u8(nq[:, 0:NK])), 16), ev(SY.dma_start(tws[:, sl], ns[:, 0:NK]), 16)]
+            size(32 * b, 32 * b + 32, 32, 32 * b + 32, 32 * b + 64)
+        for b in range(4):
+            m = (b + 3) % 4
+            act(ar[32 * b:32 * b + 32, 96:128], sr[32 * m:32 * m + 32, 0:32], AF.Abs, [e_tp], sz)
+        act(ar[96:128, 32:64], sr[0:32, 0:32], AF.Abs, s=sz)
+        l3 = red(T.gg[:, 129:130], T.lw[:, 48:48 + n], Op.max, [l2, before])
+        e_gt = tt(T.gg[:, 0:128], ar[:], thr[:], Op.is_gt, [sz, e_th, before])
+        e_y = scan(yo[:], dzc, T.gg[:], Op.add, [e_gt, l3, k_a])
+        e_t2 = tp(yb[:], yo[:, 129:193], [e_y])
+        e_z = red(sm[:, 0:1], yb[:, 0:32], Op.min, [e_t2], ab=True)
+        red(sm[:, 1:2], yb[:, 32:64], Op.min, s=e_z, ab=True)
+        e_m = tt(sm[0:64, 2:4], sm[0:64, 0:2], sm[64:128, 0:2], Op.min, [e_z])
+        e_wv = step()
+        for b in range(4):
+            tt(sm[32 * b:32 * b + 32, 4:6], sm[0:32, 2:4], sm[32:64, 2:4], Op.min, [e_m], e_wv)
+        w = sm[:, 4:6]
+        e_of = ts(of[:, 0:2], w, RND - 1.0, Op.add, RND, Op.subtract, d=[e_wv])
+        ci = T["ci%d" % t]
+        c1 = ts(ci[:, 0:2], w, 8.0, Op.mult, 8.0 * t - 4.5, Op.add)
+        tab, tabs = (T.t0, T.t0s) if t == 0 else (T.tr, T.trs)
+        sc, ss, lt, lst = (T["%s%d" % (x, t)] for x in ("sc", "ss", "la", "ls"))
+        e_sc = cp(u32(sc[:]), u32(tab[:]).indirect(of[:, 0:2]), [e_of])
+        e_ss = act(ss[:], tabs[:].indirect(of[:, 0:2]), d=[e_of])
+        sl = slice(NK * rank, NK * rank + NK)
+        to_each([(r, u8(sc[:, NK * i:NK * i + NK]), u8(lt[:, sl])) for i, r in enumerate(REB[t]) if r != rank], T.sem["s_la%d" % t], [e_sc], 0)
+        to_each([(r, ss[:, NK * i:NK * i + NK], lst[:, sl]) for i, r in enumerate(REB[t]) if r != rank], T.sem["s_la%d" % t], [e_ss], 2)
+        own = []
+        if t == mine:
+            own = [dma("S", u8(lt[:, sl]), u8(sc[:, NK * I:NK * I + NK]), [e_sc]), dma("S", lst[:, sl], ss[:, NK * I:NK * I + NK], [e_ss])]
+        c2 = ts(ci[:, 2:4], ci[:, 0:2], 63, Op.bitwise_and, d=[c1])
+        e_cd = ts(of[:, 2:4], w, 8.0, Op.mult, -4.5, Op.add)
+        e_c64 = cp(of[:, 4:6], ci[:, 2:4], [c2])
+        bsb = T["bsb%d" % t]
+        e_b = act(bsb[:, 0:32], T.irow[:].indirect(of[:, 0:2]), d=[i_ir])
+        act(bsb[:, 32:64], T.tl[:].indirect(of[:, 4:6]), d=[e_c64, i_tl], s=e_b)
+        fin.append(dma("S", T.bs[2 * t:2 * t + 2, 0:32], bsb[0:1, 0:64], [e_b]))
+        return own, e_of, e_cd, e_c64, e_b, e_y
 
-    def table0(t):
-        for c in range(8):
-            v(ts(T["ei%d" % t][:, 32 * c:32 * c + 32], T["vr%d" % t][:, 0:32], T.tgt[:, 8 * t + c:8 * t + c + 1], Op.is_equal))
+    def rebuild_list(t, e_c64, e_of, d):
+        rl, of, ol = T["rl%d" % t], T["of%d" % t], T["ol%d" % t]
+        s = NK * I
+        a = tt(rl[:, 0:32], T.to[:, 0:64].indirect(of[:, 4:6]), T.mk[:, 0:32], Op.add, [e_c64, d])
+        if t:
+            tt(rl[:, 32:64], T.sub[:].indirect(of[:, 0:2]), T.mk[:, 32:64], Op.add, [e_of], a)
+            a = tt(rl[:, 64:72], rl[:, s:s + 8], rl[:, 32 + s:40 + s], Op.max, [a])
+            s = 64
+        a = tt(rl[:, 72:76], rl[:, s:s + 8:2], rl[:, s + 1:s + 8:2], Op.max, [a])
+        return cp(ol[:], rl[:, 72:76], [a])
 
-    def table1(t):
-        ei = T["ei%d" % t]
-        v(tt(ei[:, 256:512], ei[:, 0:256], T.kw[:], Op.mult))
+    def unpack(t, d):
+        ol = T["ol%d" % t]
+        wide = [[x for x in REB[t] if x != r].index(rank) != 1 for r in REB[t] if r != rank]
+        arr = (T.sem["s_la%d" % t], (14 + sum(wide)) * (EW // 4))
+        e_oc = cp(u32(od[:, 0:64]), u32(la[:, 0:104]).indirect(ol[:]), [d, arr])
+        e_os = act(os_[:, 0:64], ls[:, 0:104].indirect(ol[:]), d=[d, arr])
+        return [mm(T.da[:, 512 * b:512 * b + 128], T.eq[:, 128 * b:128 * b + 128], T.eqs[:, 128 * b:128 * b + 128], od[:], os_[:], [d, e_oc, e_os]) for b in range(4)]
 
-    def table2(t):
-        ei = T["ei%d" % t]
-        v(V.tensor_tensor_scan(ei[:, 512:768], T.seg[:], ei[:, 256:512], 0.0, Op.mult, Op.max))
+    def lookup(c, tab, keys, d):
+        a = tt(T.gs[:, c:c + 128], tab[:].indirect(keys), T.dg[:], Op.mult, d)
+        return lambda: scan(T.gs[:, c + 128:c + 256], seg, T.gs[:, c:c + 128], Op.max, [a, k_b])
 
-    def table3(t):
-        ei = T["ei%d" % t]
-        v(tt(ei[:, 768:776], ei[:, 543:768:32], T.src[:, 8 * t:8 * t + 8], Op.max))
-
-    def table4(t):
-        return ev(V.tensor_copy(T["oi%d" % t][:], T["ei%d" % t][:, 768:776]))
-
-    def arrived(t):
-        return (T.sem["s_nw%d" % t], EW * (6 if mine == t else 8))
+    def old_table(e_sa):
+        b = lookup(256, T.sa, T.ku[:, 8:16], [e_sa, k_2])()
+        v = T.gs[:, 256 + 143:512:16]
+        c = ts(T.ofx[:, 8:16], v, 0.5, Op.mult, 111.5, Op.add, d=[b])
+        ts(T.ofx[:, 16:24], v, 100.0, Op.mult, s=c)
+        c = tt(T.ofx[:, 24:32], T.ofx[:, 8:16], T.ofx[:, 16:24], Op.min, [c])
+        return tt(T.ofx[:, 32:40], T.ofx[:, 24:32], T.ofx[:, 0:8], Op.max, [c])
 
     s_ck = (T.sem.s_ck, 7 * EW)
-    wait(A, e_c0, e_c1)
-    wait(A, s_ck)
-    e_ag0 = ev(A.activation(T.ag[:, 0:8], T.ck[:, 2:64:8], AF.Abs))
-    e_ag1 = ev(A.activation(T.ag[:, 8:16], T.ck[:, 4:64:8], AF.Abs))
-    vw()
-    wait(V, s_ck)
-    v(V.tensor_reduce(T.cf[:, 5:6], T.ck[:, 0:64:8], X, Op.add))
-    vw()
-    e_s = ev(V.tensor_tensor_scan(T.so[:], T.dz[:, 289:361], T.ck[:, 1:576:8], T.cf[:, 5:6], Op.mult, Op.subtract))
-
-    def l0a():
-        wait(V, e_ag0)
-        v(V.tensor_reduce(T.cf[:, 6:7], T.ag[:, 0:8], X, Op.max))
-
-    def l0b():
-        v(ts(T.gt[:, 8:16], T.ag[:, 0:8], T.cf[:, 6:7], Op.is_equal))
-
-    def l0c():
-        v(tt(T.gt[:, 16:24], T.gt[:, 8:16], T.w0[:], Op.mult))
-
-    def l0d():
-        v(V.tensor_reduce(T.g0[:, 129:130], T.gt[:, 16:24], X, Op.max))
-
-    own, e_b = order(0, (T.so[:, 8:9], T.so[:, 8:72]), e_s, (l0a, l0b, l0c, l0d), [e_t0])
-    new_own = []
+    e_x = tt(T.xs[:, 96:128], T.ck[:, 0:32].indirect(T.co[:, 0:2]), T.m32[:], Op.mult, [k3, k4, e_c, s_ck])
+    e_s = scan(T.so[:, 0:80], dz0, T.xs[:, 112:192], Op.subtract, [e_x, k_a])
+    own, e_of, e_cd, e_c64, e_b, e_y0 = order(0, e_s, T.so[:, 16:17], T.so[:, 16:80], (96, 112, T.xs), T.w16[:, 0:16], e_x, [])
+    e_ag = act(T.ag[:, 0:8], T.ck[:, 3:32:4], AF.Abs)
     if mine == 0:
-        e_ol = rebuild_list(0, e_b)
+        e_ol = rebuild_list(0, e_c64, e_of, k_r)
         e_eq = unpacker()
-        new_own = rebuild(0, own, e_ol, e_eq, [])
-    vr, bsb = T.vr0, T.bsb0
-    hit, hi = T.hit, T.hiti
-    wait(V, e_b)
-    e_ms = []
-    for r in range(N):
-        e_ms.append(ev(ts(T.msk[:, 32 * r:32 * r + 32], vr[:, 0:32], T.c1[:, 8 + r:9 + r], Op.is_equal, T.dm[:, r:r + 1], Op.mult)))
-    v(V.tensor_reduce(T.cf[:, 4:5], T.c1[:, 16:24], X, Op.add))
-    table0(0)
-    v(tt(hit[:, 0:32], bsb[:, 0:32], bsb[:, 32:64], Op.subtract))
-    v(tt(T.gt[:, 24:32], T.ck[:, 3:64:8], T.pm[:], Op.mult))
-    v(ts(hit[:, 32:64], bsb[:, 32:64], q1, Op.not_equal))
-    v(ts(hit[:, 160:192], vr[:, 32:64], 1.0 / 256, Op.mult))
-    vw()
-    e_ms.append(ev(ts(T.msk[:, 256:288], vr[:, 0:32], T.cf[:, 4:5], Op.is_equal, -1.0, Op.mult)))
-    for r in range(N + 1):
-        wait(A, e_ms[r])
-        a(A.activation(T.junk[:, 32 * r:32 * r + 32], T.msk[:, 32 * r:32 * r + 32], AF.Copy, accum_out=T.rep[:, r:r + 1]))
-    aw()
-    e_rep = ev(A.activation(T.gt[:, 64:73], T.rep[:], AF.Copy))
-    v(ts(hi[:, 0:32], hit[:, 0:32], 128.0, Op.add))
-    v(V.tensor_reduce(T.cf[:, 7:8], T.gt[:, 24:32], X, Op.add))
-    table1(0)
-    vw()
-    v(ts(hi[:, 32:64], hi[:, 0:32], 127, Op.bitwise_and))
-    wait(V, e_seg)
-    table2(0)
-    vw()
-    v(V.tensor_copy(hit[:, 64:96], hi[:, 32:64]))
-    table3(0)
-    e_ur0 = ev(V.tensor_copy(u32(T.ur[:, 0:128]), u32(T.uq[:]).indirect(T.oz[:, 0:8])))
-    vw()
-    e_oi = table4(0)
-    v(ts(hit[:, 96:128], hit[:, 64:96], T.pf[:, 0:1], Op.is_equal))
-    wait(V, e_rep, *e_ms)
-    v(tt(T.gt[:, 32:40], T.dm[:], T.gt[:, 64:72], Op.subtract))
-    v(ts(T.gt[:, 40:41], T.gt[:, 72:73], 1.0, Op.add, -1.0, Op.mult))
-    vw()
-    v(tt(hit[:, 128:160], hit[:, 96:128], hit[:, 32:64], Op.mult))
-    v(tt(T.xs[:, 65:297:33], T.ck[:, 3:64:8], T.gt[:, 32:40], Op.mult))
-    v(tt(T.xs[:, 32:33], T.cf[:, 7:8], T.gt[:, 40:41], Op.mult))
-    v(tt(T.w40[:, 0:8], T.gt[:, 32:40], T.wr[:], Op.mult))
-    wait(V, e_ag1)
-    v(tt(T.gv[:, 0:8], T.gt[:, 32:40], T.ag[:, 8:16], Op.mult))
-    e_ur1 = ev(V.tensor_copy(u32(T.ur[:, 128:256]), u32(T.uq[:]).indirect(T.oz[:, 8:16])))
-    vw()
-    v(tt(T.w40[:, 8:40], hit[:, 128:160], hit[:, 160:192], Op.mult))
-    wait(A, e_uq, e_oz, e_ur0, e_ur1)
-    e_us0 = ev(A.activation(T.urs[:, 0:128], T.uqs[:].indirect(T.oz[:, 0:8]), AF.Copy))
-    e_us1 = ev(A.activation(T.urs[:, 128:256], T.uqs[:].indirect(T.oz[:, 8:16]), AF.Copy))
-    wait(V, e_oi)
-
-    nw = arrived(0)
-    wait(PE, e_us0, e_us1, e_ur0, e_ur1)
-    wait(PE, e_c0, e_c1, *new_own)
-    wait(PE, nw)
-    e_cn = ev(PE.matmul_mx(T.ps[:, 0:128], T.ur[:, 0:128], T.urs[:, 0:128], T.tw0[:, 128:256], T.tws0[:, 128:256], True, True))
-    e_gn = ev(PE.matmul_mx(T.db[:, 0:128], T.ur[:, 128:256], T.urs[:, 128:256], T.tw0[:, 128:256], T.tws0[:, 128:256], True, True))
-    wait(V, *e_tw0)
-    wait(V, *new_own)
-    vw()
-    wait(V, nw)
-    p1 = ev(V.tensor_copy(u32(T.t1[:]), u32(T.tw0[:, 0:160]).indirect(T.oi0[:])))
-    wait(A, e_gn)
-    e_agn = ev(A.activation(T.agn[:], T.db[:, 0:32], AF.Abs))
-    wait(A, e_oi, *e_tw0)
-    wait(A, *new_own)
-    wait(A, nw)
-    p2 = ev(A.activation(T.t1s[:], T.tws0[:, 0:160].indirect(T.oi0[:]), AF.Copy))
-    wait(SY, p1, p2)
-    e_tw1 = [ev(SY.dma_start(u8(T.tw1[:, 0:128]), u8(T.t1[:])), 16), ev(SY.dma_start(T.tws1[:, 0:128], T.t1s[:]), 16)]
-    wait(V, e_cn)
-    for r in range(N):
-        v(tt(T.xs[:, 33 + 33 * r:65 + 33 * r], T.msk[:, 32 * r:32 * r + 32], T.ps[:, 0:32], Op.mult))
-    e_xp = ev(tt(T.xs[:, 0:32], T.msk[:, 256:288], T.ps[:, 0:32], Op.mult))
-    wait(V, e_agn)
-    v(tt(T.gv[:, 8:40], T.agn[:], hit[:, 128:160], Op.mult))
-    wait(V, e_xp)
-    vw()
-    e_s = ev(V.tensor_tensor_scan(T.xo[:], T.dz[:], T.xs[:], 0.0, Op.mult, Op.subtract))
-
-    def l1a():
-        v(V.tensor_reduce(T.gt[:, 42:43], T.gv[:], X, Op.max))
-
-    def l1b():
-        v(ts(T.lw[:, 0:40], T.gv[:], T.gt[:, 42:43], Op.is_equal))
-
-    def l1c():
-        v(tt(T.lw[:, 40:80], T.lw[:, 0:40], T.w40[:], Op.mult))
-
-    def l1d():
-        v(V.tensor_reduce(T.g1[:, 129:130], T.lw[:, 40:80], X, Op.max))
-
-    own, e_b = order(1, (T.xo[:, 297:298], T.xo[:, 297:361]), e_s, (l1a, l1b, l1c, l1d), [p1, p2])
-    new_own = []
+        e_u2 = qz(T.u2[:], T.u2s[:], T.ut2[:], [k_u2])
+    k_2 = second_constants()
+    e_sa = cp(T.sa[:].indirect(T.of0[:, 2:4]), T.val[:, 0:32], [e_cd, i_v0, k_s])
+    bsb, hit = T.bsb0, T.hit
+    h0 = tt(hit[:, 0:32], bsb[:, 0:32], bsb[:, 32:64], Op.subtract, [e_b])
+    h1 = act(hit[:, 32:64], hit[:, 0:32], AF.Abs, [h0, i_pn], bias=T.cf[:, 9:10])
+    if mine == 0:
+        ds = unpack(0, [e_ol, e_eq, e_la, k_r, own])
+        e_h = step()
+        for b in range(4):
+            scan(h[:, 4 * x0 + b:4 * x0 + 256:4], dzr, T.da[:, 512 * b:512 * b + 64], Op.subtract, [ds[b], k_h, k_b], e_h)
+        e_nq = qz(nq[:], ns[:], h[:], [e_h])
+        m2 = mm(T.ps[:, 1024:1152], T.u2[:], T.u2s[:], nq[:], ns[:], [e_nq, e_u2])
+        e_sn = cp(u32(T.sn[:]), u32(nq[:]).indirect(T.co[:, 2:3]), [e_nq, k_sn])
+        e_sns = act(T.sns[:], ns[:].indirect(T.co[:, 2:3]), d=[e_nq, k_sn])
+        e_tk = tp(T.tk[:], T.ps[:, 1027:1152:4], [m2])
+        to_many(sorted(others, key=lambda r: r in REB[1]), T.tk[:, 0:2], T.na[:, 2 * I:2 * I + 2], T.sem.s_na, [e_tk])
+        sl = slice(64 + NK * I, 64 + NK * I + NK)
+        to_many(REB[1], u8(T.sn[:, 0:NK]), u8(T.la1[:, sl]), T.sem.s_nb, [e_sn])
+        to_many(REB[1], T.sns[:, 0:NK], T.ls1[:, sl], T.sem.s_nb, [e_sns])
+        e_no = [cp(T.na[:, 8:10], T.tk[:, 0:2], [e_tk])]
+    else:
+        e_no = []
+    fn = lookup(0, T.sa, T.ku[:, 0:8], [e_sa, k_2])
+    g1 = tt(T.ag[:, 8:15], T.ag[:, 0:7], T.rp[:, 16:23], Op.mult, [e_ag, k_2])
+    tt(T.ag[:, 16:23], T.ag[:, 1:8], T.rp[:, 8:15], Op.mult, s=g1)
+    b = fn()
+    h2 = ts(hit[:, 64:96], hit[:, 32:64], 64.0, Op.is_equal, d=[h1])
+    ts(hit[:, 96:128], bsb[:, 32:64], q1, Op.not_equal, s=h2)
+    ts(hit[:, 128:160], bsb[:, 32:64], -0.125, Op.mult, 1.0, Op.add, s=h2)
+    g2 = tt(T.ag[:, 24:31], T.ag[:, 8:15], T.ag[:, 16:23], Op.add, [g1])
+    sub = T.gs[:, 143:256:16]
+    c = tt(T.ofx[:, 40:48], sub, T.rp[:, 24:32], Op.max, [b])
+    ts(T.rp[:, 40:47], T.gs[:, 159:256:16], 1.0, Op.is_lt, s=c)
+    h3 = tt(hit[:, 160:192], hit[:, 64:96], hit[:, 96:128], Op.mult, [h2])
+    e_o1 = cp(T.o1[:], T.ofx[:, 40:48], [c])
+    e_gv = tt(T.gv[:, 0:7], T.ag[:, 24:31], T.rp[:, 40:47], Op.mult, [g2])
+    tt(T.w40[:, 0:7], T.rp[:, 32:39], T.rp[:, 40:47], Op.mult, s=e_gv)
+    tt(T.w40[:, 7:39], hit[:, 160:192], hit[:, 128:160], Op.mult, [h3], e_gv)
+    k_z = act(T.sz[:, 0:512], T.hz[:])
+    act(T.sz[:, 512:1024], T.hz[:], s=k_z)
     if mine == 1:
-        e_ol = rebuild_list(1, e_b)
+        k_r = rebuilder_constants()
         e_eq = unpacker()
-        new_own = rebuild(1, own, e_ol, e_eq, [e_agn])
-    wait(V, e_b)
-    table0(1)
-    wait(V, e_w, e_eb)
-    e_wq = ev(V.quantize_mx(T.wq[:], T.wqs[:], T.wt[:]))
-    vw()
-    table1(1)
-    vw()
-    table2(1)
-    vw()
-    table3(1)
-    vw()
-    e_oi = table4(1)
-    nw = arrived(1)
-    wait(V, e_oi, *e_tw1)
-    wait(V, *new_own)
-    wait(V, nw)
-    p1 = ev(V.tensor_copy(u32(T.t2[:]), u32(T.tw1[:, 0:160]).indirect(T.oi1[:])))
-    wait(A, e_oi, *e_tw1)
-    wait(A, *new_own)
-    wait(A, nw)
-    p2 = ev(A.activation(T.t2s[:], T.tws1[:, 0:160].indirect(T.oi1[:]), AF.Copy))
-    wait(SY, p1)
-    fin.append(ev(SY.dma_start(T.oc[:, 0:512], u8(T.t2[:])), 16))
-    wait(A, p2)
+        c = ts(T.rl0[:, 0:8], sub, 0.5, Op.mult, 47.5, Op.add)
+        ts(T.rl0[:, 8:16], sub, 100.0, Op.mult, s=c)
+        c2 = step()
+        for n in range(4):
+            tt(T.st[:, 8 * n:8 * n + 8], T.rl0[:, 0:8], T.rl0[:, 8:16], Op.min, [c], c2)
+        c = tp(T.st[:, 32:64], T.st[:, 0:32], [c2])
+        e_sub = step()
+        for n in range(4):
+            for m in range(4):
+                (cp if m < 2 else act)(T.sub[32 * n:32 * n + 32, 32 * m:32 * m + 32], T.st[32 * m:32 * m + 32, 32:64], d=[c], s=e_sub)
+        e_f0 = old_table(e_sa)
+        e_v1 = ts(T.val[:, 32 + NK * I:40 + NK * I], rr, 192.0, Op.add, d=[i_v1])
+        e_tw = qz(T.tw[:, 0:128], T.tws[:, 0:128], T.tbt[:, 0:512])
+        e_wq = qz(T.wq[:], T.wqs[:], T.wt[:], [e_w])
+        s_nb = (T.sem.s_nb, 8 * EW)
+        new0 = [dma("S", u8(T.tw[:, 128:160]), u8(T.la1[:, 64:96]), [s_nb]), dma("S", T.tws[:, 128:160], T.ls1[:, 64:96])]
+
+    s_na = (T.sem.s_na, EW * (3 if mine == 0 else 4))
+    r0 = cp(T.rc[:, 0:64], T.na[:].indirect(T.co[:, 4:8]), [k_2, e_no, s_na])
+    r1 = act(T.rc[:, 64:128], T.na[:].indirect(T.co[:, 8:12]), AF.Abs, [k_2, e_no, s_na])
+    r2 = tp(T.ck[:, 32:96], T.rc[:, 0:64], [r0])
+    r3 = tp(T.ng[:], T.rc[:, 64:128], [r1])
+    e_x = tt(T.xs[:, 0:128], T.ck[:].indirect(T.o1[:]), T.dg[:], Op.mult, [r2, e_o1])
+    r4 = tt(T.gv[:, 7:39], T.ng[:, 1:64:2], hit[:, 160:192], Op.mult, [r3, h3])
+    e_s = scan(T.so[:], dz1, T.xs[:], Op.subtract, [e_x, k_b])
+    own, e_of, e_cd, e_c64, e_b, e_y1 = order(1, e_s, T.so[:, 128:129], T.so[:, 128:192], (0, 39, T.gv), T.w40[:, 0:39], [r4, e_gv], [e_y0])
+    new1 = []
+    if mine == 0:
+        sl = slice(P + NK * I, P + NK * I + NK)
+        rs = [r for r in REB[0] if r != rank]
+        to_many(rs, u8(T.sn[:, 0:NK]), u8(T.tw[:, sl]), T.sem.s_nb, [])
+        to_many(rs, T.sns[:, 0:NK], T.tws[:, sl], T.sem.s_nb, [])
+        new0 = [dma("S", u8(T.tw[:, sl]), u8(T.sn[:, 0:NK]), [e_sn, e_b]), dma("S", T.tws[:, sl], T.sns[:, 0:NK], [e_sns]), (T.sem.s_nb, 6 * EW)]
+        e_f0 = old_table(e_sa)
+        e_v1 = i_v1
+        e_tw = qz(T.tw[:, 0:128], T.tws[:, 0:128], T.tbt[:, 0:512])
+        e_wq = qz(T.wq[:], T.wqs[:], T.wt[:], [e_w])
+    else:
+        e_ol = rebuild_list(1, e_c64, e_of, [k_r, e_sub])
+    e_sz = cp(T.sz[:].indirect(T.of1[:, 2:4]), T.val[:, 32:64], [e_cd, e_v1, k_z])
+    b = lookup(512, T.sz, T.ku[:, 16:24], [e_sz])()
+    c = tt(T.ofx[:, 8:16], T.gs[:, 512 + 143:768:16], T.ofx[:, 32:40], Op.max, [b, e_f0])
+    e_oi = cp(T.oi[:], T.ofx[:, 8:16], [c])
+    if mine == 1:
+        ds = unpack(1, [e_ol, e_eq, e_la, k_r, own, s_nb])
+        scans = [scan(T.sb[:, 64 * b:64 * b + 64], dzr, T.da[:, 512 * b:512 * b + 64], Op.subtract, [ds[b], k_b]) for b in range(4)]
+        e_h = step()
+        for b in range(3):
+            act(h[:, b:4 * NK:4], T.sb[:, 64 * b + 7:64 * b + 64:8], d=[scans[b], k_h], s=e_h)
+        cp(h[:, 3:4 * NK:4], T.sb[:, 199:256:8], [scans[3], k_h], e_h)
+        e_nq = qz(nq[:], ns[:], h[:], [e_h])
+        sl = slice(160 + NK * I, 160 + NK * I + NK)
+        to_many(others, u8(nq[:, 0:NK]), u8(T.tw[:, sl]), T.sem.s_nw, [e_nq])
+        to_many(others, ns[:, 0:NK], T.tws[:, sl], T.sem.s_nw, [])
+        new1 = [qz(T.tw[:, 192:320], T.tws[:, 192:320], h[:])]
+
+    s_nw = (T.sem.s_nw, EW * (8 if mine == 0 else 6))
+    p1 = cp(u32(T.t2[:]), u32(T.tw[:, 0:200]).indirect(T.oi[:]), [e_oi, e_tw, new0, new1, s_nw])
+    p2 = act(T.t2s[:], T.tws[:, 0:200].indirect(T.oi[:]), d=[e_oi, e_tw, new0, new1, s_nw])
+    fin.append(dma("S", T.oc[:, 0:512], u8(T.t2[:]), [p1]))
+    e_os = step(True)
     for k in range(4):
-        fin.append(ev(A.dma_start(T.osc[4 * k:4 * k + 4, 0:128], T.t2s[32 * k:32 * k + 4, 0:128]), 16))
-    wait(PE, e_wq, e_xp, p1, p2)
-    e_y = ev(PE.matmul_mx(T.ps[:, 0:128], T.wq[:], T.wqs[:], T.t2[:], T.t2s[:], True, True))
-    wait(V, e_y)
-    e_yc = ev(V.tensor_copy(T.ysb[:], T.ps[:, 0:128]))
-    wait(SY, e_yc)
-    fin.append(ev(SY.dma_start(T.y[:, 0:128], T.ysb[:]), 16))
-    wait(g, *fin)
-    g.wait_ge(T.sem.sl, nsl[0])
+        dma("A", T.osc[4 * k:4 * k + 4, 0:128], T.t2s[32 * k:32 * k + 4, 0:128], [p2], e_os)
+    e_y = mm(T.ps[:, 1536:1664], T.wq[:], T.wqs[:], T.t2[:], T.t2s[:], [e_wq, p1, p2])
+    e_yc = cp(T.ysb[:], T.ps[:, 1536:1664], [e_y])
+    fin.append(dma("S", T.y[:, 0:128], T.ysb[:], [e_yc]))
+    op("g", None, [(T.sem.sl, nsl[0]), fin, e_os])
+    emit()

@@ -5,7 +5,9 @@ N, P, K = 8, 128, 32
 REB = ((0, 2, 4, 6), (1, 3, 5, 7))
 NK = K // 4
 TINY = 2.0 ** -121
+LESS = 1.0 - 2.0 ** -24
 PITCH = 512.0
+W8 = 0.125 / PITCH
 RND = 1.5 * 2.0 ** 23
 X4, U8, F32, I32, U16, BF = "float8_e4m3fn_x4", "uint8", "float32", "int32", "uint16", "bfloat16"
 
@@ -15,35 +17,78 @@ def _sb(n, d):
 
 
 SCRATCH = {
-    "tbt": _sb(544, BF), "ut": _sb(512, BF), "ut2": _sb(512, BF), "wt": _sb(512, BF), "hz": _sb(512, BF), "eb": _sb(516, BF),
+    "tbt": _sb(544, BF), "ut": _sb(512, BF), "wt": _sb(512, BF), "hz": _sb(516, BF), "eb": _sb(516, BF),
     "t0": _sb(128, X4), "t0s": _sb(128, U8), "tr": _sb(128, X4), "trs": _sb(128, U8),
     "uq": _sb(128, X4), "uqs": _sb(128, U8), "u2": _sb(128, X4), "u2s": _sb(128, U8), "wq": _sb(128, X4), "wqs": _sb(128, U8),
     "eq": _sb(512, X4), "eqs": _sb(512, U8), "tw": _sb(320, X4), "tws": _sb(320, U8), "t2": _sb(128, X4), "t2s": _sb(128, U8),
     "sn": _sb(16, X4), "sns": _sb(16, U8),
-    "dz": _sb(657, BF), "ck": _sb(96, F32), "xs": _sb(192, F32), "so": _sb(192, F32), "fac": _sb(128, F32), "gg": _sb(193, F32),
+    "dz": _sb(657, BF), "dw": _sb(64, F32), "ck": _sb(18, F32), "cn": _sb(82, F32), "xs": _sb(192, F32), "so": _sb(192, F32), "fac": _sb(33, F32), "gg": _sb(192, F32),
     "pi": _sb(4, I32), "pj": _sb(8, I32), "cf": _sb(16, F32), "irow": _sb(128, F32), "i16": _sb(128, F32), "dg": _sb(128, F32),
-    "m32": _sb(32, F32), "w16": _sb(24, F32), "co": _sb(16, U16), "tl": _sb(64, F32), "tq": _sb(64, F32), "to": _sb(320, F32),
-    "mk": _sb(64, F32), "val": _sb(64, F32), "sa": _sb(1024, BF), "sz": _sb(1024, BF), "rp": _sb(48, F32), "ki": _sb(48, I32), "ku": _sb(24, U16),
-    "ag": _sb(32, F32), "gv": _sb(40, F32), "w40": _sb(40, F32), "lw": _sb(96, F32), "hit": _sb(192, F32), "gs": _sb(768, F32),
-    "o1": _sb(8, U16), "ofx": _sb(48, F32), "oi": _sb(8, U16), "na": _sb(16, F32), "tk": _sb(32, F32), "rc": _sb(128, F32), "ng": _sb(64, F32),
-    "st": _sb(64, F32), "sub": _sb(128, F32), "sb": _sb(256, F32), "ysb": _sb(128, F32),
+    "m32": _sb(32, F32), "w16": _sb(40, F32), "co": _sb(16, U16), "tl": _sb(64, F32), "tq": _sb(64, F32), "to": _sb(448, F32),
+    "mk": _sb(64, F32), "val": _sb(96, F32), "sa": _sb(1024, BF), "sz": _sb(1088, BF), "rp": _sb(64, F32), "ki": _sb(48, I32), "ku": _sb(16, U16),
+    "ag": _sb(32, F32), "gv": _sb(40, F32), "w40": _sb(44, F32), "lw": _sb(96, F32), "hit": _sb(192, F32), "gs": _sb(512, F32),
+    "o1": _sb(10, U16), "ofx": _sb(48, F32), "oi": _sb(8, U16), "na": _sb(16, F32), "tk": _sb(32, F32), "rc": _sb(128, F32), "ng": _sb(64, F32),
+    "st": _sb(64, F32), "sub": _sb(128, F32), "sb": _sb(256, F32), "ysb": _sb(128, F32), "yw": _sb(200, F32),
     "ps": ("psum", [128, 2048], F32), "da": ("psum", [128, 2048], F32),
 }
 for _t in "01":
     SCRATCH.update({
-        "sc" + _t: _sb(32, X4), "ss" + _t: _sb(32, U8), "la" + _t: _sb(224, X4), "ls" + _t: _sb(224, U8),
+        "sc" + _t: _sb(32, X4), "ss" + _t: _sb(32, U8), "la" + _t: _sb(288, X4), "ls" + _t: _sb(288, U8),
         "or" + _t: _sb(128, X4), "os" + _t: _sb(128, U8), "h" + _t: _sb(512, BF), "nq" + _t: _sb(128, X4), "ns" + _t: _sb(128, U8),
-        "sr" + _t: _sb(64, F32), "ar" + _t: _sb(128, F32), "thr" + _t: _sb(128, F32), "yo" + _t: _sb(193, F32),
-        "yb" + _t: _sb(64, F32), "sm" + _t: _sb(8, F32), "of" + _t: _sb(6, U16), "ci" + _t: _sb(4, I32),
+        "sr" + _t: _sb(64, F32), "ar" + _t: _sb(128, F32), "thr" + _t: _sb(33, F32), "yo" + _t: _sb(192, F32),
+        "yb" + _t: _sb(128, F32), "sm" + _t: _sb(8, F32), "of" + _t: _sb(6, U16), "ci" + _t: _sb(4, I32),
         "bsb" + _t: _sb(64, F32), "rl" + _t: _sb(96, F32), "ol" + _t: _sb(4, U16),
     })
-NE, ND = 110, 28
-SEMAPHORES = ["sl", "s_ck", "s_la0", "s_la1", "s_na", "s_nb", "s_nw"] + ["e%d" % _i for _i in range(NE)] + ["d%d" % _i for _i in range(ND)]
+NE, ND = 115, 24
+SEMAPHORES = ["sl", "sl2", "s_ck", "s_cn", "s_la0", "s_la1", "s_na", "s_nb", "s_nw", "s_f0", "s_f1"] + ["e%d" % _i for _i in range(NE)] + ["d%d" % _i for _i in range(ND)]
+
+
+def ring(buf, rank, rs):
+    return [buf[:, 2 + 2 * ((rank - r) % N):4 + 2 * ((rank - r) % N)] for r in rs]
+
+
+def helpers(T, topo, r):
+    c0 = T.cores[r]
+    cs = [c for c in topo.cores_of(c0) if T.rank_of(c) is None and topo.die(c) == topo.die(c0) and all(topo.may_write(c, x) for x in T.cores)]
+    return cs[:2 if r in REB[0] else 3]
+
+
+def address(topo, to, core):
+    rid, pid = topo.addr(to, core)
+    return DstId(rid=int(rid), pnc=int(pid))
+
+
+def helper_program(g, core, T, topo, rank, n):
+    others = [r for r in range(N) if r != rank]
+    c0, nh = T.cores[rank], len(helpers(T, topo, rank))
+    m = int(topo.mask(core, T.cores[others[0]]))
+    came = len(set(topo.engines(c0, core)) - set(topo.engines(c0, T.cores[others[0]])))
+
+    def on(rs, src, outs, sem):
+        g.remote_dma_fused([RemoteDMATransfer(dst_ids=[address(topo, T.cores[r], core) for r in rs], dma_engine_mask=m, remote_sem=sem, srcs=[src], dsts=outs)], local_sem=T.sem.sl)
+    g.wait_ge(T.sem.s_f0, came)
+    on(others[n::nh], T.cn[:, 2:4], ring(T.cn, rank, others[n::nh]), T.sem.s_cn)
+    g.wait_ge(T.sem.s_f1, came)
+    if rank in REB[0]:
+        s0 = P + NK * REB[0].index(rank)
+        rs = list(REB[1]) + [r for r in REB[0] if r != rank]
+        if n == 0:
+            on(rs, T.sn[:, 0:NK].bitcast(dt.uint8), [(T.la1 if r in REB[1] else T.tw)[:, s0:s0 + NK].bitcast(dt.uint8) for r in rs], T.sem.s_nb)
+        else:
+            on(rs, T.sns[:, 0:NK], [(T.ls1 if r in REB[1] else T.tws)[:, s0:s0 + NK] for r in rs], T.sem.s_nb)
+    else:
+        at = T.tws[:, 160 + NK * REB[1].index(rank):168 + NK * REB[1].index(rank)]
+        rs = others[(1, 4, 6)[n]:(4, 6, 7)[n]]
+        on(rs, at, [at for r in rs], T.sem.s_nw)
+    g.wait_ge(T.sem.sl, 2 * len(topo.engines(core, T.cores[others[0]])))
 
 
 def rank_program(g, core, T, topo):
     rank = T.rank_of(core)
     if rank is None:
+        for r in range(N):
+            if core in helpers(T, topo, r):
+                helper_program(g, core, T, topo, r, helpers(T, topo, r).index(core))
         return
     V, A, PE, SY = g.vector, g.scalar, g.tensor, g.sync
     X = AxisListType.X
@@ -115,8 +160,8 @@ def rank_program(g, core, T, topo):
             return op("V", lambda: V.tensor_reduce(out, i0, X, o, apply_absolute_value=True), d, s)
         return op("V", lambda: V.tensor_reduce(out, i0, X, o), d, s)
 
-    def scan(out, d0, d1, o1, d=(), s=None):
-        return op("V", lambda: V.tensor_tensor_scan(out, d0, d1, 0.0, Op.mult, o1), d, s)
+    def scan(out, d0, d1, o1, d=(), s=None, o0=Op.mult, first=0.0):
+        return op("V", lambda: V.tensor_tensor_scan(out, d0, d1, first, o0, o1), d, s)
 
     def tp(out, i0, d=(), s=None):
         return op("V", lambda: V.transpose(out, i0), d, s)
@@ -146,220 +191,226 @@ def rank_program(g, core, T, topo):
 
     others = [r for r in range(N) if r != rank]
     EW = len(topo.engines(core, T.cores[others[0]]))
-    nsl, fin = [0], []
+    nsl, fin = {"sl": 0, "sl2": 0}, []
+    hs = helpers(T, topo, rank)
+    near = [e for e in topo.engines(core, hs[0]) if e not in topo.engines(core, T.cores[others[0]])]
 
     def dst(r):
-        rid, pid = topo.addr(T.cores[r], core)
-        return DstId(rid=int(rid), pnc=int(pid))
+        return address(topo, T.cores[r], core)
+
+    def to_helpers(cs, src, out, sem, d, more=()):
+        tr = [RemoteDMATransfer(dst_ids=[address(topo, c, core) for c in cs], dma_engine_mask=sum(1 << e for e in near), remote_sem=sem, srcs=[src], dsts=[out for c in cs])]
+        nsl["sl"] += len(near)
+        for r, sem2 in more:
+            tr.append(RemoteDMATransfer(dst_ids=[dst(r)], dma_engine_mask=int(topo.mask(core, T.cores[r])), remote_sem=sem2, srcs=[src], dsts=[out]))
+            nsl["sl"] += EW
+        op("g", lambda: g.remote_dma_fused(tr, local_sem=T.sem.sl), d)
 
     def to_many(rs, src, out, sem, d):
         m = int(topo.mask(core, T.cores[rs[0]]))
-        nsl[0] += EW
-        op("g", lambda: g.remote_dma_fused([RemoteDMATransfer(dst_ids=[dst(r) for r in rs], dma_engine_mask=m, remote_sem=sem, srcs=[src], dsts=[out for r in rs])], local_sem=T.sem.sl), d)
+        outs = out if isinstance(out, list) else [out for r in rs]
+        nsl["sl"] += EW
+        op("g", lambda: g.remote_dma_fused([RemoteDMATransfer(dst_ids=[dst(r) for r in rs], dma_engine_mask=m, remote_sem=sem, srcs=[src], dsts=outs)], local_sem=T.sem.sl), d)
 
-    def to_each(pairs, sem, d, wide):
+    def to_each(pairs, sem, d, wide, left):
         tr, w, e0 = [], EW // 4, 0
         for i, (r, s, o) in enumerate(pairs):
             n = 2 * w if len(pairs) == 3 and i == wide else w
             m = sum(1 << e for e in topo.engines(core, T.cores[r])[e0:e0 + n])
             tr.append(RemoteDMATransfer(dst_ids=[dst(r)], dma_engine_mask=m, remote_sem=sem, srcs=[s], dsts=[o]))
-            nsl[0] += n
+            nsl[left] += n
             e0 += n
-        op("g", lambda: g.remote_dma_fused(tr, local_sem=T.sem.sl), d)
+        op("g", lambda: g.remote_dma_fused(tr, local_sem=T.sem[left]), d)
+        return (T.sem[left], nsl[left])
 
     mine = [t for t in range(2) if rank in REB[t]][0]
     I = REB[mine].index(rank)
+    peers = [r for r in REB[mine] if r != rank]
+    s8 = NK * I
     la, ls, od, os_, h, nq, ns = (T["%s%d" % (n, mine)] for n in ("la", "ls", "or", "os", "h", "nq", "ns"))
     x0 = 64 * (I & 1) if mine == 0 else 0
-    ones, dzc, dz0, dz1, dzr, seg = T.dz[:, 0:128], T.dz[:, 0:193], T.dz[:, 193:273], T.dz[:, 273:465], T.dz[:, 465:529], T.dz[:, 529:657]
-    rr = T.irow[:, 0:8]
-    p8, p16, p32, q1, pf = (T.cf[:, i:i + 1] for i in range(5))
-    hp = T.cf[:, 5:7]
+    dzc, dz0, dz1, dzr, seg = T.dz[:, 0:192], T.dz[:, 193:273], T.dz[:, 273:465], T.dz[:, 465:529], T.dz[:, 529:657]
+    rr, hz = T.irow[:, 0:8], T.hz[:, 0:512]
+    p8, p16, p32, q1, pf, hp, pd = (T.cf[:, i:i + 1] for i in range(7))
 
+    e_u = dma("A", T.ut[:, 8:16], T.u[:, 0:8])
     e_tb = dma("S", T.tbt[:, 0:512], T.tb[:, 0:512])
-    e_u = dma("A", T.ut[:, 0:8], T.u[:, 0:8])
-    e_tb2 = dma("A", T.tbt[:, 512:544], T.tb[:, 0:32])
-    i_pi = iota(T.pi[:], [[1, 2], [0, 2]], 0, 1, False)
+    i_pi = iota(T.pi[:], [[N - rank, 2], [1, 2]], 0, 1, False)
     i_ir = iota(T.irow[:], [[1, P]], 0, 0)
     i_tl = iota(T.tl[:], [[0, 8], [-1, 8]], 7, 0)
     i_tq = iota(T.tq[:], [[1, 8], [0, 8]], 0, 0)
-    i_16 = iota(T.i16[:], [[0, 8], [1, 16]], 0, 0)
-    z_ut = ms(T.ut[:, 8:512], 0.0)
     z_hz = ms(T.hz[:], 0.0)
-    z_dz = ms(T.dz[:], 1.0)
-    z_na = ms(T.na[:], 0.0)
+    z_ut = ms(T.ut[:, 16:512], 0.0)
+    ms(T.ut[:, 0:8], 0.0, s=z_ut)
+    k1 = ts(T.pj[:, 0:1], T.pi[:, 0:1], 7, Op.bitwise_and, d=[i_pi])
+    ts(T.pj[:, 1:2], T.pi[:, 0:1], 15, Op.bitwise_and, s=k1)
+    ts(T.pj[:, 2:3], T.pi[:, 0:1], 31, Op.bitwise_and, s=k1)
+    ts(T.pj[:, 3:4], T.pi[:, 1:2], 7, Op.bitwise_and, s=k1)
+    ts(T.pj[:, 5:6], T.pi[:, 0:1], 2, Op.arith_shift_right, 4, Op.bitwise_and, s=k1)
+    ts(T.pj[:, 6:7], T.pi[:, 2:3], 7, Op.bitwise_and, s=k1)
+    cp(T.pj[:, 4:5], T.pi[:, 0:1], s=k1)
     e_uq = qz(T.uq[:], T.uqs[:], T.ut[:], [z_ut, e_u])
+    k2 = cp(T.cf[:, 0:7], T.pj[:, 0:7], [k1])
+    z_eb = act(T.eb[:], T.hz[:], d=[z_hz])
+    z_dz = act(T.dz[:, 0:273], T.hz[:, 0:273], AF.Identity, bias=1.0)
+    e_tb2 = act(T.tbt[:, 512:544], T.tbt[:, 0:32], d=[e_tb])
+    act(T.dz[:, 273:657], T.hz[:, 0:384], AF.Identity, s=z_dz, bias=1.0)
+    z_na = act(T.na[:], T.hz[:, 0:16])
+    i_eb = op("g", lambda: g.affine_select(T.eb[:, 3:515:4], T.hz[:, 0:P], [[-1, P]], Op.not_equal, 1.0, 0, 1), [z_eb])
     e_t0 = qz(T.t0[:], T.t0s[:], T.tbt[:, 0:512], [e_tb])
-    e_tr = qz(T.tr[:], T.trs[:], T.tbt[:, 4 * rank:4 * rank + 512], [e_tb2])
     m0 = mm(T.ps[:, 0:128], T.t0[:], T.t0s[:], T.uq[:], T.uqs[:], [e_uq, e_t0])
+    e_la = qz(la[:, 160:288], ls[:, 160:288], hz, [z_hz])
+    e_c = cp(T.ck[:, 0:4], T.ps[:, 0:4], [m0])
+    rs = sorted(others, key=lambda r: r in REB[0])
+    to_many(rs, T.ck[:, 2:4], ring(T.ck, rank, rs), T.sem.s_ck, [e_c])
+    e_tr = qz(T.tr[:], T.trs[:], T.tbt[:, 4 * rank:4 * rank + 512], [e_tb2])
     m1 = mm(T.ps[:, 512:640], T.tr[:], T.trs[:], T.uq[:], T.uqs[:], [e_tr])
-    o = 4 * rank
-    e_c = cp(T.ck[:, o:o + 2], T.ps[:, 0:2], [m0, z_na])
-    cp(T.ck[:, o + 2:o + 4], T.ps[:, 512:514], [m1], e_c)
-    to_many(sorted(others, key=lambda r: r in REB[0]), T.ck[:, o:o + 4], T.ck[:, o:o + 4], T.sem.s_ck, [e_c])
-    e_w = dma("S", T.wt[:], T.w[:, 0:512], [e_c])
-    z_eb = ms(T.eb[:], 0.0)
-    i_eb = op("g", lambda: g.affine_select(T.eb[:, 3:515:4], ones, [[-1, P]], Op.is_equal, 0.0, 0, 1), [z_eb, z_dz])
-    i_v0 = iota(T.val[:, 0:32], [[2, K]], 33, 0)
+    k5 = ts(T.m32[:, 0:8], rr, p8, Op.not_equal, d=[k2, i_ir])
+    ts(T.m32[:, 8:16], rr, p8, Op.not_equal, -1.0, Op.mult, s=k5)
+    k4 = ts(T.m32[:, 16:24], rr, p8, Op.is_equal)
+    e_c1 = cp(T.cn[:, 0:4], T.ps[:, 512:516], [m1])
+    to_helpers(hs, T.cn[:, 2:4], T.cn[:, 2:4], T.sem.s_f0, [e_c1])
+    i_16 = iota(T.i16[:], [[0, 8], [1, 16]], 0, 0)
+    i_v0 = iota(T.val[:, 0:32], [[2, K]], 19, 0)
     i_v1 = iota(T.val[:, 32:64], [[1, K]], 160, 0)
     i_p8 = iota(T.cf[:, 8:9], [[0, 1]], 7, 8)
     i_pn = iota(T.cf[:, 9:10], [[0, 1]], 64, -1)
+    i_rp = iota(T.rp[:, 40:48], [[1, 2], [8, 2], [0, 2]], 0, 0)
+    i_sz = [iota(T.rp[:, 56:64], [[16, 8]], P - rank, 0), iota(T.val[:, 64:96], [[1, K]], P, 0), iota(T.sz[:, 0:512], [[1, 64], [0, 8]], 0, 0)]
 
-    k_a = act(T.xs[:, 128:129], T.dz[:, 0:1], d=[z_dz, z_hz], scale=-TINY)
+    k3 = act(T.w16[:, 24:32], rr, AF.Identity, [i_ir, k2], scale=-W8, bias=8 * W8)
+    act(T.w16[:, 32:40], rr, AF.Identity, s=k3, scale=W8, bias=-8 * W8)
+    act(T.w16[:, 0:18:17], T.hz[:, 0:2], s=k3)
+    k_g = act(T.gg[:, 129:192], T.hz[:, 0:63], AF.Identity, bias=-PITCH)
+    k_c = act(T.cf[:, 10:11], p8, AF.Identity, bias=-1.0)
+    k_a = act(T.xs[:, 128:129], T.dz[:, 0:1], d=[z_dz], scale=-TINY)
     act(T.xs[:, 129:192], T.hz[:, 0:63], s=k_a)
-    for a, b in ((130, 145), (146, 177), (178, 193)):
-        act(T.gg[:, a:b], T.dz[:, 0:b - a], s=k_a, scale=-PITCH)
-    act(T.gg[:, 145:178:32], T.dz[:, 0:2], s=k_a, scale=15 * PITCH)
+    act(T.lw[:, 39:40], T.dz[:, 0:1], s=k_a, scale=-8.0)
+    act(T.gg[:, 128:129], pf, AF.Identity, s=k_a, bias=1.0 - 4.5 / 8)
+    act(T.gg[:, 144:177:32], T.dz[:, 0:2], d=[k_g], s=k_a, scale=15 * PITCH)
     act(T.dz[:, 128:129], T.dz[:, 0:1], s=k_a, scale=PITCH)
     act(T.dz[:, 201:242:40], T.dz[:, 0:2], s=k_a, scale=-1.0)
     k_b = act(T.dz[:, 289:434:144], T.dz[:, 0:2], scale=-1.0)
     act(T.dz[:, 465:529:8], T.hz[:, 0:8], s=k_b)
+    act(T.w40[:, 0:41:40], T.hz[:, 0:2], s=k_b)
     act(T.dz[:, 466:529:8], T.dz[:, 0:8], s=k_b, scale=-1.0)
     act(T.dz[:, 529:657:16], T.hz[:, 0:8], s=k_b)
-    k_h = act(h[:], T.hz[:])
-    k_s = act(T.sa[:, 0:512], T.hz[:])
-    act(T.sa[:, 512:1024], T.hz[:], s=k_s)
-    if mine == 0:
-        k_u = act(T.ut2[:], T.hz[:])
-        k_u2 = step()
-        for n in range(4):
-            act(T.ut2[:, 128 * n:128 * n + 8], T.ut[:, 0:8], d=[k_u, e_u], s=k_u2)
 
-    k1 = ts(T.pj[:, 0:1], T.pi[:, 0:1], 7, Op.bitwise_and, d=[i_pi])
-    ts(T.pj[:, 1:2], T.pi[:, 0:1], 15, Op.bitwise_and, s=k1)
-    ts(T.pj[:, 2:3], T.pi[:, 0:1], 31, Op.bitwise_and, s=k1)
-    ts(T.pj[:, 3:4], T.pi[:, 2:3], 7, Op.bitwise_and, s=k1)
-    ts(T.pj[:, 5:7], T.pi[:, 0:2], 4, Op.arith_shift_right, 1, Op.bitwise_and, s=k1)
-    cp(T.pj[:, 4:5], T.pi[:, 0:1], s=k1)
-    k3 = ts(T.w16[:, 16:24], rr, -0.125, Op.mult, 1.0, Op.add, d=[i_ir])
-    k2 = cp(T.cf[:, 0:7], T.pj[:, 0:7], [k1])
-    e_la = qz(la[:, 96:224], ls[:, 96:224], T.hz[:], [z_hz])
-    ts(T.m32[:, 0:8], rr, p8, Op.not_equal, d=[k2], s=k3)
-    ts(T.cf[:, 7:8], p32, pf, Op.subtract, float(P), Op.add, s=k3)
-    k4 = ts(T.m32[:, 8:16], rr, p8, Op.not_equal, -1.0, Op.mult)
-    ts(T.m32[:, 16:24], rr, p8, Op.is_equal, s=k4)
     ts(T.m32[:, 24:32], rr, p8, Op.not_equal, s=k4)
-    ts(T.co[:, 0:1], p8, 4.0, Op.mult, 1.0, Op.add, s=k4)
-    ts(T.co[:, 1:2], p8, 4.0, Op.mult, s=k4)
-    ts(T.fac[:, 0:32], T.irow[:, 0:32], p32, Op.is_ge, 1.0 - 2.0 ** -24, Op.max, s=k4)
-    ts(T.gg[:, 128:129], pf, 1.0 - 4.5 / 8, Op.add, s=k4)
-    tt(T.w16[:, 0:8], T.w16[:, 16:24], T.m32[:, 0:8], Op.mult, [k3], k4)
-    tt(T.w16[:, 8:16], T.w16[:, 16:24], T.m32[:, 0:8], Op.mult, s=k4)
-    ts(T.fac[:, 32:128], T.irow[:, 32:128], T.cf[:, 7:8], Op.is_lt, 1.0 - 2.0 ** -24, Op.max, s=k4)
+    ts(T.co[:, 0:1], pd, 2.0, Op.mult, 3.0, Op.add, s=k4)
+    ts(T.co[:, 1:2], pd, 2.0, Op.mult, 2.0, Op.add, s=k4)
+    k6 = tt(T.w16[:, 1:17], T.w16[:, 24:40], T.m32[:, 0:16], Op.mult, [k3, k5])
+    ts(T.fac[:], T.irow[:, 0:33], p32, Op.is_ge, LESS, Op.max, s=k4)
+    tt(T.dw[:, 0:17], T.w16[:, 0:17], T.w16[:, 1:18], Op.subtract, [k6], k4)
 
-    def rebuilder_constants():
-        a = ts(T.cf[:, 10:11], p8, -1.0, Op.add)
-        ts(T.cf[:, 11:12], p8, 0.0, Op.is_equal, s=a)
-        ts(T.cf[:, 12:13], p16, 8.0, Op.is_ge, -1000.0, Op.mult, s=a)
-        ts(T.cf[:, 13:14], p16, 8.0, Op.is_lt, -1000.0, Op.mult, s=a)
-        ms(T.mk[:], 0.0, s=a)
-        e_or = qz(od[:], os_[:], T.hz[:])
-        b = ts(T.to[:, 64:128], T.tq[:], T.cf[:, 10:11], Op.is_le, T.cf[:, 10:11], Op.add, d=[a, i_tq])
-        ts(T.to[:, 128:192], T.tq[:], T.cf[:, 11:12], Op.mult, s=b)
-        s = NK * I
-        e = ts(T.mk[:, s:s + 8:2], T.irow[:, 0:8:2], T.cf[:, 12:13], Op.add)
-        ts(T.mk[:, s + 1:s + 8:2], T.irow[:, 1:8:2], T.cf[:, 13:14], Op.add, s=e)
-        c = tt(T.to[:, 192:256], T.to[:, 64:128], T.to[:, 128:192], Op.max, [b])
-        if mine:
-            ts(T.mk[:, 32 + s:40 + s:2], T.hz[:, 0:4], T.cf[:, 12:13], Op.add, s=e)
-            ts(T.mk[:, 33 + s:40 + s:2], T.hz[:, 0:4], T.cf[:, 13:14], Op.add, s=e)
-        d_ = tt(T.to[:, 64:128], T.to[:, 192:256], T.tl[:], Op.is_equal, [c, i_tl])
-        ts(T.to[:, 128:192], T.to[:, 192:256], 8.0, Op.mult, s=d_)
-        f = ts(T.to[:, 256:320], T.to[:, 64:128], 96.0, Op.mult, d=[d_])
-        tt(T.to[:, 0:64], T.to[:, 256:320], T.to[:, 128:192], Op.max, [f], e)
-        return [e, e_or]
+    e_eq = step()
 
-    def unpacker():
-        s = step()
-        for b in range(4):
-            qz(T.eq[:, 128 * b:128 * b + 128], T.eqs[:, 128 * b:128 * b + 128], T.eb[:, 3 - b:515 - b], [i_eb], s)
-        return s
-
-    def second_constants():
-        a = ts(T.rp[:, 8:15], T.irow[:, 0:7], q1, Op.is_ge)
-        ts(T.rp[:, 16:23], T.irow[:, 0:7], q1, Op.is_lt, s=a)
-        ts(T.cf[:, 14:15], p16, 8.0, Op.mult, 7.0 - rank, Op.add, s=a)
-        ts(T.cf[:, 15:16], p16, 8.0, Op.mult, 1031.0 - 9 * rank, Op.add, s=a)
-        z = ts(T.dg[:], T.i16[:], p16, Op.is_equal, d=[i_16])
-        b = cp(T.rp[:, 0:1], q1)
-        tt(T.rp[:, 1:8], T.rp[:, 8:15], T.irow[:, 0:7], Op.add, [a], b)
-        c = ts(T.ki[:, 8:16], rr, 128.0, Op.mult, T.cf[:, 14:15], Op.add)
-        ts(T.ki[:, 16:24], rr, 128.0, Op.mult, T.cf[:, 15:16], Op.add, s=c)
-        ts(T.ofx[:, 0:8], rr, 16.0, Op.mult, p16, Op.add, s=z)
-        ts(T.ki[:, 0:8], T.rp[:, 0:8], 7.0, Op.mult, T.cf[:, 8:9], Op.add, d=[b, i_p8], s=c)
-        ts(T.rp[:, 24:32], T.rp[:, 0:8], 4.0, Op.mult, 2.0, Op.add, s=z)
-        ts(T.rp[:, 32:39], T.rp[:, 1:8], -0.125, Op.mult, 1.0, Op.add, s=z)
-        e = ts(T.ki[:, 24:48], T.ki[:, 0:24], 1023, Op.bitwise_and, d=[c])
-        for f in range(2):
-            for e2 in range(2):
-                v = [8 + f if mine == 0 and i == I else 2 * i + f for i in (2 * e2, 2 * e2 + 1)]
-                c0 = 4 + 4 * f + 2 * e2
-                ts(T.co[:, c0:c0 + 2], hp, float(v[1] - v[0]), Op.mult, float(v[0]), Op.add, s=z)
-        cp(T.ku[:], T.ki[:, 24:48], [e], z)
-        return [z, a]
-
+    def unpacker(b):
+        qz(T.eq[:, 128 * b:128 * b + 128], T.eqs[:, 128 * b:128 * b + 128], T.eb[:, 3 - b:515 - b], [i_eb], e_eq)
+    a = ts(T.cf[:, 11:12], p8, 0.0, Op.is_equal)
+    b = ts(T.to[:, 64:128], T.tq[:], T.cf[:, 10:11], Op.is_le, T.cf[:, 10:11], Op.add, d=[k_c, i_tq])
+    e_or = qz(od[:], os_[:], hz)
+    ts(T.to[:, 128:192], T.tq[:], T.cf[:, 11:12], Op.mult, d=[a], s=b)
+    unpacker(0)
+    c = tt(T.to[:, 192:256], T.to[:, 64:128], T.to[:, 128:192], Op.max, [b])
+    unpacker(1)
+    a = tt(T.to[:, 64:128], T.to[:, 192:256], T.tl[:], Op.is_equal, [c, i_tl])
+    b = act(T.to[:, 128:192], T.to[:, 192:256], AF.Identity, [c], scale=8.0, bias=32.0)
+    ts(T.to[:, 320:384], T.to[:, 192:256], float(rank), Op.not_equal, 1000.0, Op.mult, s=b)
+    unpacker(2)
+    c = act(T.to[:, 256:320], T.to[:, 64:128], d=[a], scale=128.0)
+    tt(T.to[:, 384:448], T.to[:, 320:384], T.to[:, 128:192], Op.min, [b], c)
+    unpacker(3)
+    k_r = [tt(T.to[:, 0:64], T.to[:, 256:320], T.to[:, 384:448], Op.max, [c]), e_or, e_eq]
     if mine == 0:
-        k_r = rebuilder_constants()
-        k_sn = ts(T.co[:, 2:3], p8, 8.0, Op.mult, x0 + 7.0, Op.add)
+        k_h = act(h[:, 256 - 4 * x0:512 - 4 * x0], T.hz[:, 0:256])
+        k_u2 = step()
+        for n in range(1, 4):
+            act(T.ut[:, 128 * n + 8:128 * n + 16], T.ut[:, 8:16], d=[e_uq], s=k_u2)
 
-    def order(t, e_s, s_col, s_rep, vals, wts, e_v, before):
-        sr, ar, thr, yo, yb, sm, of = (T["%s%d" % (n, t)] for n in ("sr", "ar", "thr", "yo", "yb", "sm", "of"))
-        n = vals[1] - vals[0]
-        gv = vals[2][:, vals[0]:vals[1]]
+    k_m, k_mk, k_l = step(), step(), step()
+    small = [
+        lambda: ts(T.cf[:, 12:13], p16, 8.0, Op.is_ge, -1000.0, Op.mult, s=k_m),
+        lambda: ts(T.cf[:, 13:14], p16, 8.0, Op.is_lt, -1000.0, Op.mult, s=k_m),
+        lambda: ms(T.mk[:], 0.0, s=k_m),
+        lambda: ts(T.co[:, 4:12], T.rp[:, 40:48], hp, Op.add, d=[i_rp], s=k_l),
+        lambda: ts(T.mk[:, s8:s8 + 8:2], T.irow[:, 0:8:2], T.cf[:, 12:13], Op.add, d=[k_m], s=k_mk),
+        lambda: ts(T.mk[:, s8 + 1:s8 + 8:2], T.irow[:, 1:8:2], T.cf[:, 13:14], Op.add, s=k_mk),
+        lambda: ts(T.co[:, 2:3], p8, 8.0, Op.mult, x0 + 7.0, Op.add, s=k_l),
+    ]
+
+    def order(t, e_s, s_col, s_rep, gv, n, steps, e_v, before, fill, late):
+        sr, ar, thr, yo, yb, sm, of = (T["%s%d" % (x, t)] for x in ("sr", "ar", "thr", "yo", "yb", "sm", "of"))
+        fill = list(fill)
+
+        def slot():
+            if fill:
+                fill.pop(0)()
         l0 = red(sm[:, 6:7], gv, Op.max, [e_v])
         e_th = act(thr[:], T.fac[:], AF.Abs, [e_s, k4], scale=s_col)
         e_tp = tp(sr[:], s_rep, [e_s])
-        l1 = ts(T.lw[:, 0:n], gv, sm[:, 6:7], Op.is_equal, d=[l0, before])
+        l1 = ts(T.lw[:, 39 - n:39], gv, sm[:, 6:7], Op.not_equal, -8.0, Op.mult, d=[l0, before])
         sz = step()
 
         def size(p0, p1, c, q0, q1_, d=()):
             tt(ar[p0:p1, c:c + 32], sr[q0:q1_, 0:32], sr[q0:q1_, 32:64], Op.max, d, sz)
         size(0, 128, 0, 0, 128, [e_tp])
-        size(0, 64, 64, 64, 128)
         size(64, 128, 64, 0, 64)
-        l2 = tt(T.lw[:, 48:48 + n], T.lw[:, 0:n], wts, Op.mult, [l1])
+        size(96, 128, 32, 0, 32)
+        for b in range(1, 4):
+            size(32 * b, 32 * b + 32, 96, 32 * b - 32, 32 * b)
+        act(ar[0:64, 64:96], sr[64:128, 0:32], AF.Abs, [e_tp], sz, scale=LESS)
+        act(ar[0:32, 96:128], sr[96:128, 0:32], AF.Abs, s=sz, scale=LESS)
         for b in range(3):
-            size(32 * b, 32 * b + 32, 32, 32 * b + 32, 32 * b + 64)
-        for b in range(4):
-            m = (b + 3) % 4
-            act(ar[32 * b:32 * b + 32, 96:128], sr[32 * m:32 * m + 32, 0:32], AF.Abs, [e_tp], sz)
-        act(ar[96:128, 32:64], sr[0:32, 0:32], AF.Abs, s=sz)
-        l3 = red(T.gg[:, 129:130], T.lw[:, 48:48 + n], Op.max, [l2, before])
-        e_gt = tt(T.gg[:, 0:128], ar[:], thr[:], Op.is_gt, [sz, e_th, before])
-        e_y = scan(yo[:], dzc, T.gg[:], Op.add, [e_gt, l3, k_a])
-        e_t2 = tp(yb[:], yo[:, 129:193], [e_y])
-        e_z = red(sm[:, 0:1], yb[:, 0:32], Op.min, [e_t2], ab=True)
-        red(sm[:, 1:2], yb[:, 32:64], Op.min, s=e_z, ab=True)
-        e_m = tt(sm[0:64, 2:4], sm[0:64, 0:2], sm[64:128, 0:2], Op.min, [e_z])
+            act(ar[32 * b:32 * b + 32, 32:64], sr[32 * b + 32:32 * b + 64, 0:32], AF.Abs, s=sz, scale=LESS)
+        l3 = scan(T.lw[:, 48:49 + n], steps, T.lw[:, 39 - n:40], Op.max, [l1, k_a, before], o0=Op.add, first=-8.0)
+        e_gt = ts(T.gg[:, 32:128], ar[:, 32:128], thr[:, 32:33], Op.is_ge, d=[sz, e_th, before])
+        tt(T.gg[:, 0:32], ar[:, 0:32], thr[:, 0:32], Op.is_gt, s=e_gt)
+        slot()
+        late()
+        e_y = scan(yo[:], dzc, T.gg[:], Op.add, [e_gt, l3, k_a], first=T.lw[:, 48 + n:49 + n])
+        slot()
+        e_t2 = tp(yb[0:64, 32:96], yo[64:128, 128:192], [e_y])
+        tp(yb[0:64, 0:32], yo[0:64, 128:160], s=e_t2)
+        tp(yb[0:64, 96:128], yo[0:64, 160:192], s=e_t2)
+        slot()
+        e_z = red(sm[0:64, 0:1], yb[0:64, 0:64], Op.min, [e_t2], ab=True)
+        red(sm[0:64, 1:2], yb[0:64, 64:128], Op.min, s=e_z, ab=True)
+        slot()
         e_wv = step()
-        for b in range(4):
-            tt(sm[32 * b:32 * b + 32, 4:6], sm[0:32, 2:4], sm[32:64, 2:4], Op.min, [e_m], e_wv)
-        w = sm[:, 4:6]
-        e_of = ts(of[:, 0:2], w, RND - 1.0, Op.add, RND, Op.subtract, d=[e_wv])
+        for b in range(2):
+            tt(sm[32 * b:32 * b + 32, 4:6], sm[0:32, 0:2], sm[32:64, 0:2], Op.min, [e_z], e_wv)
+        w, e_of = sm[:, 4:6], step()
+        for b in range(2):
+            ts(of[64 * b:64 * b + 64, 0:2], sm[0:64, 4:6], RND - 1.0, Op.add, RND, Op.subtract, d=[e_wv], s=e_of)
         ci = T["ci%d" % t]
-        c1 = ts(ci[:, 0:2], w, 8.0, Op.mult, 8.0 * t - 4.5, Op.add)
+        c0 = cp(sm[64:128, 4:6], sm[0:64, 4:6])
         tab, tabs = (T.t0, T.t0s) if t == 0 else (T.tr, T.trs)
         sc, ss, lt, lst = (T["%s%d" % (x, t)] for x in ("sc", "ss", "la", "ls"))
         e_sc = cp(u32(sc[:]), u32(tab[:]).indirect(of[:, 0:2]), [e_of])
         e_ss = act(ss[:], tabs[:].indirect(of[:, 0:2]), d=[e_of])
-        sl = slice(NK * rank, NK * rank + NK)
-        to_each([(r, u8(sc[:, NK * i:NK * i + NK]), u8(lt[:, sl])) for i, r in enumerate(REB[t]) if r != rank], T.sem["s_la%d" % t], [e_sc], 0)
-        to_each([(r, ss[:, NK * i:NK * i + NK], lst[:, sl]) for i, r in enumerate(REB[t]) if r != rank], T.sem["s_la%d" % t], [e_ss], 2)
+        sl, left = slice(64 + NK * rank, 64 + NK * rank + NK), "sl2" if t else "sl"
+        to_each([(r, u8(sc[:, NK * i:NK * i + NK]), u8(lt[:, sl])) for i, r in enumerate(REB[t]) if r != rank], T.sem["s_la%d" % t], [e_sc], 0, left)
+        gone = to_each([(r, ss[:, NK * i:NK * i + NK], lst[:, sl]) for i, r in enumerate(REB[t]) if r != rank], T.sem["s_la%d" % t], [e_ss], 2, left)
+        c1 = ts(ci[:, 0:2], w, 8.0, Op.mult, 8.0 * t - 4.5, Op.add, d=[c0])
+        e_cd = ts(of[:, 2:4], w, 8.0, Op.mult, 8.0 * rank * t - 4.5, Op.add)
+        c2 = ts(ci[:, 2:4], ci[:, 0:2], 63, Op.bitwise_and, d=[c1])
+        slot()
+        e_c64 = cp(of[:, 4:6], ci[:, 2:4], [c2])
+        slot()
+        slot()
         own = []
         if t == mine:
-            own = [dma("S", u8(lt[:, sl]), u8(sc[:, NK * I:NK * I + NK]), [e_sc]), dma("S", lst[:, sl], ss[:, NK * I:NK * I + NK], [e_ss])]
-        c2 = ts(ci[:, 2:4], ci[:, 0:2], 63, Op.bitwise_and, d=[c1])
-        e_cd = ts(of[:, 2:4], w, 8.0, Op.mult, -4.5, Op.add)
-        e_c64 = cp(of[:, 4:6], ci[:, 2:4], [c2])
+            own = [cp(u32(lt[:, 32 - s8:64 - s8]), u32(tab[:]).indirect(of[:, 0:2])), act(lst[:, 32 - s8:64 - s8], tabs[:].indirect(of[:, 0:2]))]
         bsb = T["bsb%d" % t]
         e_b = act(bsb[:, 0:32], T.irow[:].indirect(of[:, 0:2]), d=[i_ir])
         act(bsb[:, 32:64], T.tl[:].indirect(of[:, 4:6]), d=[e_c64, i_tl], s=e_b)
         fin.append(dma("S", T.bs[2 * t:2 * t + 2, 0:32], bsb[0:1, 0:64], [e_b]))
-        return own, e_of, e_cd, e_c64, e_b, e_y
+        return own, e_of, e_cd, e_c64, e_b, e_y, gone
 
     def rebuild_list(t, e_c64, e_of, d):
         rl, of, ol = T["rl%d" % t], T["of%d" % t], T["ol%d" % t]
-        s = NK * I
+        s = s8
         a = tt(rl[:, 0:32], T.to[:, 0:64].indirect(of[:, 4:6]), T.mk[:, 0:32], Op.add, [e_c64, d])
         if t:
             tt(rl[:, 32:64], T.sub[:].indirect(of[:, 0:2]), T.mk[:, 32:64], Op.add, [e_of], a)
@@ -372,75 +423,84 @@ def rank_program(g, core, T, topo):
         ol = T["ol%d" % t]
         wide = [[x for x in REB[t] if x != r].index(rank) != 1 for r in REB[t] if r != rank]
         arr = (T.sem["s_la%d" % t], (14 + sum(wide)) * (EW // 4))
-        e_oc = cp(u32(od[:, 0:64]), u32(la[:, 0:104]).indirect(ol[:]), [d, arr])
-        e_os = act(os_[:, 0:64], ls[:, 0:104].indirect(ol[:]), d=[d, arr])
+        e_oc = cp(u32(od[:, 0:64]), u32(la[:, 32:168]).indirect(ol[:]), [d, arr])
+        e_os = act(os_[:, 0:64], ls[:, 32:168].indirect(ol[:]), d=[d, arr])
         return [mm(T.da[:, 512 * b:512 * b + 128], T.eq[:, 128 * b:128 * b + 128], T.eqs[:, 128 * b:128 * b + 128], od[:], os_[:], [d, e_oc, e_os]) for b in range(4)]
 
     def lookup(c, tab, keys, d):
         a = tt(T.gs[:, c:c + 128], tab[:].indirect(keys), T.dg[:], Op.mult, d)
         return lambda: scan(T.gs[:, c + 128:c + 256], seg, T.gs[:, c:c + 128], Op.max, [a, k_b])
 
-    def old_table(e_sa):
-        b = lookup(256, T.sa, T.ku[:, 8:16], [e_sa, k_2])()
-        v = T.gs[:, 256 + 143:512:16]
-        c = ts(T.ofx[:, 8:16], v, 0.5, Op.mult, 111.5, Op.add, d=[b])
-        ts(T.ofx[:, 16:24], v, 100.0, Op.mult, s=c)
-        c = tt(T.ofx[:, 24:32], T.ofx[:, 8:16], T.ofx[:, 16:24], Op.min, [c])
-        return tt(T.ofx[:, 32:40], T.ofx[:, 24:32], T.ofx[:, 0:8], Op.max, [c])
+    def old_places(d):
+        w = T.sm0[:, 4:6]
+        a = ts(T.ofx[:, 0:2], w, rank + 0.5, Op.is_lt, 128.0, Op.mult)
+        a = tt(T.ofx[:, 2:4], T.ofx[:, 0:2], w, Op.add, [a])
+        a = ts(T.o1[:, 8:10], T.ofx[:, 2:4], 8.0, Op.mult, -4.5, Op.add, d=[a])
+        return cp(T.sz[:].indirect(T.o1[:, 8:10]), T.val[:, 64:96], [a, d])
 
     s_ck = (T.sem.s_ck, 7 * EW)
-    e_x = tt(T.xs[:, 96:128], T.ck[:, 0:32].indirect(T.co[:, 0:2]), T.m32[:], Op.mult, [k3, k4, e_c, s_ck])
+    e_x = tt(T.xs[:, 96:128], T.ck[:].indirect(T.co[:, 0:2]), T.m32[:], Op.mult, [k5, k4, z_na, e_c, s_ck])
+    e_w = dma("S", T.wt[:], T.w[:, 0:512], [e_x])
+    small.pop(0)()
+    k_s = step()
+
+    def clear():
+        act(T.sa[:, 0:512], hz, s=k_s)
+        act(T.sa[:, 512:1024], hz, s=k_s)
     e_s = scan(T.so[:, 0:80], dz0, T.xs[:, 112:192], Op.subtract, [e_x, k_a])
-    own, e_of, e_cd, e_c64, e_b, e_y0 = order(0, e_s, T.so[:, 16:17], T.so[:, 16:80], (96, 112, T.xs), T.w16[:, 0:16], e_x, [])
-    e_ag = act(T.ag[:, 0:8], T.ck[:, 3:32:4], AF.Abs)
+    own, e_of, e_cd, e_c64, e_b, e_y0, _ = order(0, e_s, T.so[:, 16:17], T.so[:, 16:80], T.xs[:, 96:112], 16, T.dw[:, 0:17], e_x, [], small, clear)
+    i_sz += [iota(T.sz[:, 512:1024], [[1, 64], [0, 8]], 64, 0), iota(T.sz[:, 1024:1088], [[1, 8], [0, 8]], 0, 0)]
     if mine == 0:
-        e_ol = rebuild_list(0, e_c64, e_of, k_r)
-        e_eq = unpacker()
-        e_u2 = qz(T.u2[:], T.u2s[:], T.ut2[:], [k_u2])
-    k_2 = second_constants()
+        e_ol = rebuild_list(0, e_c64, e_of, [k_r, k_mk])
+        e_u2 = qz(T.u2[:], T.u2s[:], T.ut[:], [k_u2])
+    a = ts(T.rp[:, 8:15], T.irow[:, 0:7], q1, Op.is_ge)
+    ts(T.rp[:, 16:23], T.irow[:, 0:7], q1, Op.is_lt, s=a)
+    b = cp(T.rp[:, 0:1], q1)
+    k_d = ts(T.dg[:], T.i16[:], p16, Op.is_equal, d=[i_16])
+    tt(T.rp[:, 1:8], T.rp[:, 8:15], T.irow[:, 0:7], Op.add, [a], b)
     e_sa = cp(T.sa[:].indirect(T.of0[:, 2:4]), T.val[:, 0:32], [e_cd, i_v0, k_s])
     bsb, hit = T.bsb0, T.hit
+    c = ts(T.ki[:, 0:8], T.rp[:, 0:8], 7.0, Op.mult, T.cf[:, 8:9], Op.add, d=[b, i_p8])
+    ts(T.ki[:, 8:16], T.rp[:, 0:8], 128.0, Op.mult, 128.0 * (N - rank), Op.add, s=c)
+    k_k = act(T.rp[:, 32:39], T.rp[:, 1:8], AF.Identity, [b], scale=-W8, bias=8 * W8)
     h0 = tt(hit[:, 0:32], bsb[:, 0:32], bsb[:, 32:64], Op.subtract, [e_b])
+    c = ts(T.ki[:, 24:40], T.ki[:, 0:16], 1023, Op.bitwise_and, d=[c])
+    h2 = ts(hit[:, 96:128], bsb[:, 32:64], q1, Op.not_equal)
+    cp(T.ku[:, 0:8], T.ki[:, 24:32], [c], k_k)
+    ts(T.rp[:, 24:32], T.ki[:, 32:40], 1.0 / 64, Op.mult, 2.0, Op.add, s=k_k)
     h1 = act(hit[:, 32:64], hit[:, 0:32], AF.Abs, [h0, i_pn], bias=T.cf[:, 9:10])
+    h4 = act(hit[:, 128:160], bsb[:, 32:64], AF.Identity, [e_b], scale=-W8, bias=8 * W8)
+    e_no = []
     if mine == 0:
-        ds = unpack(0, [e_ol, e_eq, e_la, k_r, own])
+        ds = unpack(0, [e_ol, e_la, k_r, own])
         e_h = step()
         for b in range(4):
             scan(h[:, 4 * x0 + b:4 * x0 + 256:4], dzr, T.da[:, 512 * b:512 * b + 64], Op.subtract, [ds[b], k_h, k_b], e_h)
         e_nq = qz(nq[:], ns[:], h[:], [e_h])
         m2 = mm(T.ps[:, 1024:1152], T.u2[:], T.u2s[:], nq[:], ns[:], [e_nq, e_u2])
-        e_sn = cp(u32(T.sn[:]), u32(nq[:]).indirect(T.co[:, 2:3]), [e_nq, k_sn])
-        e_sns = act(T.sns[:], ns[:].indirect(T.co[:, 2:3]), d=[e_nq, k_sn])
+        e_sn = cp(u32(T.sn[:]), u32(nq[:]).indirect(T.co[:, 2:3]), [e_nq, k_l])
+        e_sns = act(T.sns[:], ns[:].indirect(T.co[:, 2:3]), d=[e_nq, k_l])
         e_tk = tp(T.tk[:], T.ps[:, 1027:1152:4], [m2])
-        to_many(sorted(others, key=lambda r: r in REB[1]), T.tk[:, 0:2], T.na[:, 2 * I:2 * I + 2], T.sem.s_na, [e_tk])
-        sl = slice(64 + NK * I, 64 + NK * I + NK)
-        to_many(REB[1], u8(T.sn[:, 0:NK]), u8(T.la1[:, sl]), T.sem.s_nb, [e_sn])
-        to_many(REB[1], T.sns[:, 0:NK], T.ls1[:, sl], T.sem.s_nb, [e_sns])
-        e_no = [cp(T.na[:, 8:10], T.tk[:, 0:2], [e_tk])]
-    else:
-        e_no = []
-    fn = lookup(0, T.sa, T.ku[:, 0:8], [e_sa, k_2])
-    g1 = tt(T.ag[:, 8:15], T.ag[:, 0:7], T.rp[:, 16:23], Op.mult, [e_ag, k_2])
-    tt(T.ag[:, 16:23], T.ag[:, 1:8], T.rp[:, 8:15], Op.mult, s=g1)
+        to_many(peers + list(REB[1]), T.tk[:, 2:4], T.na[:, 4 * I:4 * I + 2], T.sem.s_na, [e_tk])
+        to_helpers(hs[0:1], u8(T.sn[:, 0:NK]), u8(T.sn[:, 0:NK]), T.sem.s_f1, [e_sn])
+        to_helpers(hs[1:2], T.sns[:, 0:NK], T.sns[:, 0:NK], T.sem.s_f1, [e_sns])
+        e_no = [cp(T.na[:, 4 * I:4 * I + 2], T.tk[:, 2:4], [e_tk])]
+    fn = lookup(0, T.sa, T.ku[:, 0:8], [e_sa, k_d, k_k])
+    ts(hit[:, 64:96], hit[:, 32:64], 64.0, Op.is_equal, d=[h1], s=h2)
     b = fn()
-    h2 = ts(hit[:, 64:96], hit[:, 32:64], 64.0, Op.is_equal, d=[h1])
-    ts(hit[:, 96:128], bsb[:, 32:64], q1, Op.not_equal, s=h2)
-    ts(hit[:, 128:160], bsb[:, 32:64], -0.125, Op.mult, 1.0, Op.add, s=h2)
-    g2 = tt(T.ag[:, 24:31], T.ag[:, 8:15], T.ag[:, 16:23], Op.add, [g1])
+    h3 = tt(hit[:, 160:192], hit[:, 64:96], hit[:, 96:128], Op.mult, [h2])
     sub = T.gs[:, 143:256:16]
     c = tt(T.ofx[:, 40:48], sub, T.rp[:, 24:32], Op.max, [b])
-    ts(T.rp[:, 40:47], T.gs[:, 159:256:16], 1.0, Op.is_lt, s=c)
-    h3 = tt(hit[:, 160:192], hit[:, 64:96], hit[:, 96:128], Op.mult, [h2])
-    e_o1 = cp(T.o1[:], T.ofx[:, 40:48], [c])
-    e_gv = tt(T.gv[:, 0:7], T.ag[:, 24:31], T.rp[:, 40:47], Op.mult, [g2])
-    tt(T.w40[:, 0:7], T.rp[:, 32:39], T.rp[:, 40:47], Op.mult, s=e_gv)
-    tt(T.w40[:, 7:39], hit[:, 160:192], hit[:, 128:160], Op.mult, [h3], e_gv)
-    k_z = act(T.sz[:, 0:512], T.hz[:])
-    act(T.sz[:, 512:1024], T.hz[:], s=k_z)
+    ts(T.rp[:, 48:55], T.gs[:, 159:256:16], 1.0, Op.is_lt, s=c)
+    e_w4 = tt(T.w40[:, 8:40], hit[:, 160:192], hit[:, 128:160], Op.mult, [h3, h4])
+    e_o1 = cp(T.o1[:, 0:8], T.ofx[:, 40:48], [c])
+    tt(T.w40[:, 1:8], T.rp[:, 32:39], T.rp[:, 48:55], Op.mult, s=e_w4)
     if mine == 1:
-        k_r = rebuilder_constants()
-        e_eq = unpacker()
-        c = ts(T.rl0[:, 0:8], sub, 0.5, Op.mult, 47.5, Op.add)
+        k_h = act(h[:], hz)
+        e_tw = [qz(T.tw[:, 0:128], T.tws[:, 0:128], T.tbt[:, 0:512]), qz(T.tw[:, 160:288], T.tws[:, 160:288], hz)]
+        k_m2 = ts(T.mk[:, 32 + s8:40 + s8:2], T.hz[:, 0:4], T.cf[:, 12:13], Op.add, d=[k_mk])
+        ts(T.mk[:, 33 + s8:40 + s8:2], T.hz[:, 0:4], T.cf[:, 13:14], Op.add, s=k_m2)
+        c = ts(T.rl0[:, 0:8], sub, 0.5, Op.mult, 86.5, Op.add)
         ts(T.rl0[:, 8:16], sub, 100.0, Op.mult, s=c)
         c2 = step()
         for n in range(4):
@@ -449,62 +509,73 @@ def rank_program(g, core, T, topo):
         e_sub = step()
         for n in range(4):
             for m in range(4):
-                (cp if m < 2 else act)(T.sub[32 * n:32 * n + 32, 32 * m:32 * m + 32], T.st[32 * m:32 * m + 32, 32:64], d=[c], s=e_sub)
-        e_f0 = old_table(e_sa)
-        e_v1 = ts(T.val[:, 32 + NK * I:40 + NK * I], rr, 192.0, Op.add, d=[i_v1])
-        e_tw = qz(T.tw[:, 0:128], T.tws[:, 0:128], T.tbt[:, 0:512])
-        e_wq = qz(T.wq[:], T.wqs[:], T.wt[:], [e_w])
+                (cp if m < 1 else act)(T.sub[32 * n:32 * n + 32, 32 * m:32 * m + 32], T.st[32 * m:32 * m + 32, 32:64], d=[c], s=e_sub)
+        e_v1 = ts(T.val[:, 32 + s8:40 + s8], rr, 192.0, Op.add, d=[i_v1, e_tw])
+        e_s0 = old_places(i_sz)
         s_nb = (T.sem.s_nb, 8 * EW)
-        new0 = [dma("S", u8(T.tw[:, 128:160]), u8(T.la1[:, 64:96]), [s_nb]), dma("S", T.tws[:, 128:160], T.ls1[:, 64:96])]
+    e_ag = act(T.ag[:, rank:8], T.cn[:, 3:19 - 2 * rank:2], AF.Abs, [e_c1, (T.sem.s_cn, 7 * EW)])
+    if rank:
+        act(T.ag[:, 0:rank], T.cn[:, 19 - 2 * rank:18:2], AF.Abs, s=e_ag)
+    g1 = tt(T.ag[:, 8:15], T.ag[:, 0:7], T.rp[:, 16:23], Op.mult, [e_ag])
+    tt(T.ag[:, 16:23], T.ag[:, 1:8], T.rp[:, 8:15], Op.mult, s=g1)
+    e_dw = tt(T.dw[:, 24:64], T.w40[:, 0:40], T.w40[:, 1:41], Op.subtract, [e_w4, k_b])
+    g2 = tt(T.ag[:, 24:31], T.ag[:, 8:15], T.ag[:, 16:23], Op.add, [g1])
 
     s_na = (T.sem.s_na, EW * (3 if mine == 0 else 4))
-    r0 = cp(T.rc[:, 0:64], T.na[:].indirect(T.co[:, 4:8]), [k_2, e_no, s_na])
-    r1 = act(T.rc[:, 64:128], T.na[:].indirect(T.co[:, 8:12]), AF.Abs, [k_2, e_no, s_na])
-    r2 = tp(T.ck[:, 32:96], T.rc[:, 0:64], [r0])
+    r0 = cp(T.rc[:, 0:64], T.na[:].indirect(T.co[:, 4:8]), [k_l, e_no, s_na])
+    r1 = act(T.rc[:, 64:128], T.na[:].indirect(T.co[:, 8:12]), AF.Abs, [k_l, z_na, e_no, s_na])
+    e_gv = tt(T.gv[:, 0:7], T.ag[:, 24:31], T.rp[:, 48:55], Op.mult, [g2])
+    r2 = tp(T.cn[:, 18:82], T.rc[:, 0:64], [r0])
     r3 = tp(T.ng[:], T.rc[:, 64:128], [r1])
-    e_x = tt(T.xs[:, 0:128], T.ck[:].indirect(T.o1[:]), T.dg[:], Op.mult, [r2, e_o1])
+    e_x = tt(T.xs[:, 0:128], T.cn[:].indirect(T.o1[:, 0:8]), T.dg[:], Op.mult, [r2, e_o1])
     r4 = tt(T.gv[:, 7:39], T.ng[:, 1:64:2], hit[:, 160:192], Op.mult, [r3, h3])
     e_s = scan(T.so[:], dz1, T.xs[:], Op.subtract, [e_x, k_b])
-    own, e_of, e_cd, e_c64, e_b, e_y1 = order(1, e_s, T.so[:, 128:129], T.so[:, 128:192], (0, 39, T.gv), T.w40[:, 0:39], [r4, e_gv], [e_y0])
-    new1 = []
+    own, e_of, e_cd, e_c64, e_b, e_y1, gone = order(1, e_s, T.so[:, 128:129], T.so[:, 128:192], T.gv[:, 0:39], 39, T.dw[:, 24:64], [r4, e_gv], [e_y0, e_dw], [], lambda: None)
+    sl = slice(160 + s8, 160 + s8 + NK)
     if mine == 0:
-        sl = slice(P + NK * I, P + NK * I + NK)
-        rs = [r for r in REB[0] if r != rank]
-        to_many(rs, u8(T.sn[:, 0:NK]), u8(T.tw[:, sl]), T.sem.s_nb, [])
-        to_many(rs, T.sns[:, 0:NK], T.tws[:, sl], T.sem.s_nb, [])
-        new0 = [dma("S", u8(T.tw[:, sl]), u8(T.sn[:, 0:NK]), [e_sn, e_b]), dma("S", T.tws[:, sl], T.sns[:, 0:NK], [e_sns]), (T.sem.s_nb, 6 * EW)]
-        e_f0 = old_table(e_sa)
+        s0 = slice(P + s8, P + s8 + NK)
+        new0 = [dma("S", u8(T.tw[:, s0]), u8(T.sn[:, 0:NK]), [e_sn, gone]), dma("S", T.tws[:, s0], T.sns[:, 0:NK], [e_sns]), (T.sem.s_nb, 6 * EW)]
+        new1 = [(T.sem.s_nw, 8 * EW)]
         e_v1 = i_v1
-        e_tw = qz(T.tw[:, 0:128], T.tws[:, 0:128], T.tbt[:, 0:512])
-        e_wq = qz(T.wq[:], T.wqs[:], T.wt[:], [e_w])
+        e_s0 = old_places(i_sz)
     else:
-        e_ol = rebuild_list(1, e_c64, e_of, [k_r, e_sub])
-    e_sz = cp(T.sz[:].indirect(T.of1[:, 2:4]), T.val[:, 32:64], [e_cd, e_v1, k_z])
-    b = lookup(512, T.sz, T.ku[:, 16:24], [e_sz])()
-    c = tt(T.ofx[:, 8:16], T.gs[:, 512 + 143:768:16], T.ofx[:, 32:40], Op.max, [b, e_f0])
-    e_oi = cp(T.oi[:], T.ofx[:, 8:16], [c])
+        new0 = [dma("S", u8(T.tw[:, 128:160]), u8(T.la1[:, 128:160]), [s_nb, gone]), dma("S", T.tws[:, 128:160], T.ls1[:, 128:160])]
+        e_ol = rebuild_list(1, e_c64, e_of, [k_r, k_mk, k_m2, e_sub])
+    e_sz = cp(T.sz[:].indirect(T.of1[:, 2:4]), T.val[:, 32:64], [e_cd, e_v1, e_s0])
     if mine == 1:
-        ds = unpack(1, [e_ol, e_eq, e_la, k_r, own, s_nb])
+        ds = unpack(1, [e_ol, e_la, k_r, own, s_nb])
         scans = [scan(T.sb[:, 64 * b:64 * b + 64], dzr, T.da[:, 512 * b:512 * b + 64], Op.subtract, [ds[b], k_b]) for b in range(4)]
         e_h = step()
         for b in range(3):
             act(h[:, b:4 * NK:4], T.sb[:, 64 * b + 7:64 * b + 64:8], d=[scans[b], k_h], s=e_h)
         cp(h[:, 3:4 * NK:4], T.sb[:, 199:256:8], [scans[3], k_h], e_h)
         e_nq = qz(nq[:], ns[:], h[:], [e_h])
-        sl = slice(160 + NK * I, 160 + NK * I + NK)
-        to_many(others, u8(nq[:, 0:NK]), u8(T.tw[:, sl]), T.sem.s_nw, [e_nq])
-        to_many(others, ns[:, 0:NK], T.tws[:, sl], T.sem.s_nw, [])
-        new1 = [qz(T.tw[:, 192:320], T.tws[:, 192:320], h[:])]
+        to_helpers(hs, ns[:, 0:NK], T.tws[:, sl], T.sem.s_f1, [e_nq], [(others[0], T.sem.s_nw)])
+        to_many(others, u8(nq[:, 0:NK]), u8(T.tw[:, sl]), T.sem.s_nw, [])
+        new1 = [qz(T.tw[:, 192:320], T.tws[:, 192:320], h[:]), (T.sem.s_nw, 6 * EW)]
+    c = ts(T.ki[:, 16:24], T.rp[:, 56:64], p16, Op.add, 8.0, Op.mult)
+    e_wq = qz(T.wq[:], T.wqs[:], T.wt[:], [e_w])
+    c = ts(T.ki[:, 40:48], T.ki[:, 16:24], 1023, Op.bitwise_and, d=[c])
+    if mine == 0:
+        e_tw = qz(T.tw[:, 0:128], T.tws[:, 0:128], T.tbt[:, 0:512])
+    c = ts(T.ku[:, 8:16], T.ki[:, 40:48], 7.0 * rank + 7, Op.add, d=[c])
+    e_oi = cp(T.oi[:], T.gs[:, 256 + 143:512:16], [lookup(256, T.sz, T.ku[:, 8:16], [e_sz, c])()])
 
-    s_nw = (T.sem.s_nw, EW * (8 if mine == 0 else 6))
-    p1 = cp(u32(T.t2[:]), u32(T.tw[:, 0:200]).indirect(T.oi[:]), [e_oi, e_tw, new0, new1, s_nw])
-    p2 = act(T.t2s[:], T.tws[:, 0:200].indirect(T.oi[:]), d=[e_oi, e_tw, new0, new1, s_nw])
+    ye = 192 + NK * mine
+    m3 = mm(T.ps[:, 0:160], T.wq[:], T.wqs[:], T.tw[:, 0:160], T.tws[:, 0:160], [e_wq, e_tw, new0])
+    y0 = act(T.yw[:, 0:160], T.ps[:, 0:160], d=[m3])
+    m4 = mm(T.ps[:, 1536:1664], T.wq[:], T.wqs[:], T.tw[:, ye - 128:ye], T.tws[:, ye - 128:ye], [new1])
+    p1 = cp(u32(T.t2[:]), u32(T.tw[:, 0:200]).indirect(T.oi[:]), [e_oi, e_tw, new0, new1])
+    p2 = act(T.t2s[:], T.tws[:, 0:200].indirect(T.oi[:]), d=[e_oi, e_tw, new0, new1])
     fin.append(dma("S", T.oc[:, 0:512], u8(T.t2[:]), [p1]))
     e_os = step(True)
-    for k in range(4):
+    for k in range(2):
+        dma("S", T.osc[4 * k:4 * k + 4, 0:128], T.t2s[32 * k:32 * k + 4, 0:128], [p2], e_os)
+    y1 = cp(T.yw[:, 160:ye], T.ps[:, 1824 - ye:1664], [m4])
+    e_yc = cp(T.ysb[:, 0:64], T.yw[:, 0:ye].indirect(T.oi[:, 0:4]), [y0, y1])
+    act(T.ysb[:, 64:128], T.yw[:, 0:ye].indirect(T.oi[:, 4:8]), d=[y0, y1], s=e_yc)
+    for k in range(2, 4):
         dma("A", T.osc[4 * k:4 * k + 4, 0:128], T.t2s[32 * k:32 * k + 4, 0:128], [p2], e_os)
-    e_y = mm(T.ps[:, 1536:1664], T.wq[:], T.wqs[:], T.t2[:], T.t2s[:], [e_wq, p1, p2])
-    e_yc = cp(T.ysb[:], T.ps[:, 1536:1664], [e_y])
     fin.append(dma("S", T.y[:, 0:128], T.ysb[:], [e_yc]))
-    op("g", None, [(T.sem.sl, nsl[0]), fin, e_os])
+    op("g", None, [(T.sem.sl, nsl["sl"]), fin, e_os])
     emit()

from concourse.bass import DstId, RemoteDMATransfer
from concourse.mybir import dt, AluOpType as Op, AxisListType, ActivationFunctionType as AF

N, P, K = 8, 128, 32
REB = ((0, 2, 4, 6), (1, 3, 5, 7))
NK = K // 4
TINY = 2.0 ** -121
LESS = 1.0 - 2.0 ** -24
PITCH = 512.0
W8 = 0.125 / PITCH
RND = 1.5 * 2.0 ** 23
X4, U8, F32, I32, U16, BF = "float8_e4m3fn_x4", "uint8", "float32", "int32", "uint16", "bfloat16"


def _sb(n, d):
    return ("sbuf", [128, n], d)


SCRATCH = {
    "tbt": _sb(544, BF), "ut": _sb(512, BF), "wt": _sb(512, BF), "hz": _sb(516, BF), "eb": _sb(516, BF),
    "t0": _sb(128, X4), "t0s": _sb(128, U8), "tr": _sb(128, X4), "trs": _sb(128, U8),
    "uq": _sb(128, X4), "uqs": _sb(128, U8), "u2": _sb(128, X4), "u2s": _sb(128, U8), "wq": _sb(128, X4), "wqs": _sb(128, U8),
    "eq": _sb(512, X4), "eqs": _sb(512, U8), "tw": _sb(320, X4), "tws": _sb(320, U8), "t2": _sb(128, X4), "t2s": _sb(128, U8),
    "sn": _sb(16, X4), "sns": _sb(16, U8),
    "dz": _sb(657, BF), "dw": _sb(64, F32), "ck": _sb(18, F32), "cn": _sb(82, F32), "xs": _sb(192, F32), "so": _sb(192, F32), "fac": _sb(33, F32), "gg": _sb(192, F32),
    "pi": _sb(4, I32), "pj": _sb(8, I32), "cf": _sb(16, F32), "irow": _sb(128, F32), "i16": _sb(128, F32), "dg": _sb(128, F32),
    "m32": _sb(32, F32), "w16": _sb(40, F32), "co": _sb(16, U16), "tl": _sb(64, F32), "tq": _sb(64, F32), "to": _sb(448, F32),
    "mk": _sb(64, F32), "val": _sb(96, F32), "sa": _sb(1024, BF), "sz": _sb(1088, BF), "rp": _sb(64, F32), "ki": _sb(48, I32), "ku": _sb(16, U16),
    "ag": _sb(32, F32), "gv": _sb(40, F32), "w40": _sb(44, F32), "lw": _sb(96, F32), "hit": _sb(192, F32), "gs": _sb(512, F32),
    "o1": _sb(10, U16), "ofx": _sb(48, F32), "oi": _sb(8, U16), "na": _sb(16, F32), "tk": _sb(32, F32), "rc": _sb(128, F32), "ng": _sb(64, F32),
    "st": _sb(64, F32), "sub": _sb(128, F32), "sb": _sb(256, F32), "ysb": _sb(128, F32), "yw": _sb(200, F32),
    "ps": ("psum", [128, 2048], F32), "da": ("psum", [128, 2048], F32),
}
for _t in "01":
    SCRATCH.update({
        "sc" + _t: _sb(32, X4), "ss" + _t: _sb(32, U8), "la" + _t: _sb(288, X4), "ls" + _t: _sb(288, U8),
        "or" + _t: _sb(128, X4), "os" + _t: _sb(128, U8), "h" + _t: _sb(512, BF), "nq" + _t: _sb(128, X4), "ns" + _t: _sb(128, U8),
        "sr" + _t: _sb(64, F32), "ar" + _t: _sb(128, F32), "thr" + _t: _sb(33, F32), "yo" + _t: _sb(192, F32),
        "yb" + _t: _sb(128, F32), "sm" + _t: _sb(8, F32), "of" + _t: _sb(6, U16), "ci" + _t: _sb(4, I32),
        "bsb" + _t: _sb(64, F32), "rl" + _t: _sb(96, F32), "ol" + _t: _sb(4, U16),
    })
NE, ND = 115, 24
SEMAPHORES = ["sl", "sl2", "s_ck", "s_cn", "s_la0", "s_la1", "s_na", "s_nb", "s_nw", "s_f0", "s_f1"] + ["e%d" % _i for _i in range(NE)] + ["d%d" % _i for _i in range(ND)]


def ring(buf, rank, rs):
    return [buf[:, 2 + 2 * ((rank - r) % N):4 + 2 * ((rank - r) % N)] for r in rs]


def helpers(T, topo, r):
    c0 = T.cores[r]
    cs = [c for c in topo.cores_of(c0) if T.rank_of(c) is None and topo.die(c) == topo.die(c0) and all(topo.may_write(c, x) for x in T.cores)]
    return cs[:2 if r in REB[0] else 3]


def address(topo, to, core):
    rid, pid = topo.addr(to, core)
    return DstId(rid=int(rid), pnc=int(pid))


def helper_program(g, core, T, topo, rank, n):
    others = [r for r in range(N) if r != rank]
    c0, nh = T.cores[rank], len(helpers(T, topo, rank))
    m = int(topo.mask(core, T.cores[others[0]]))
    came = len(set(topo.engines(c0, core)) - set(topo.engines(c0, T.cores[others[0]])))

    def on(rs, src, outs, sem):
        g.remote_dma_fused([RemoteDMATransfer(dst_ids=[address(topo, T.cores[r], core) for r in rs], dma_engine_mask=m, remote_sem=sem, srcs=[src], dsts=outs)], local_sem=T.sem.sl)
    g.wait_ge(T.sem.s_f0, came)
    on(others[n::nh], T.cn[:, 2:4], ring(T.cn, rank, others[n::nh]), T.sem.s_cn)
    g.wait_ge(T.sem.s_f1, came)
    if rank in REB[0]:
        s0 = P + NK * REB[0].index(rank)
        rs = list(REB[1]) + [r for r in REB[0] if r != rank]
        if n == 0:
            on(rs, T.sn[:, 0:NK].bitcast(dt.uint8), [(T.la1 if r in REB[1] else T.tw)[:, s0:s0 + NK].bitcast(dt.uint8) for r in rs], T.sem.s_nb)
        else:
            on(rs, T.sns[:, 0:NK], [(T.ls1 if r in REB[1] else T.tws)[:, s0:s0 + NK] for r in rs], T.sem.s_nb)
    else:
        at = T.tws[:, 160 + NK * REB[1].index(rank):168 + NK * REB[1].index(rank)]
        rs = others[(1, 4, 6)[n]:(4, 6, 7)[n]]
        on(rs, at, [at for r in rs], T.sem.s_nw)
    g.wait_ge(T.sem.sl, 2 * len(topo.engines(core, T.cores[others[0]])))


def rank_program(g, core, T, topo):
    rank = T.rank_of(core)
    if rank is None:
        for r in range(N):
            if core in helpers(T, topo, r):
                helper_program(g, core, T, topo, r, helpers(T, topo, r).index(core))
        return
    V, A, PE, SY = g.vector, g.scalar, g.tensor, g.sync
    X = AxisListType.X
    QS = {"g": g, "V": V, "A": A, "P": PE, "S": SY}

    ops = []

    def step(dma=False):
        return {"n": 0, "used": False, "dma": dma, "ids": 0, "know": 0}

    def flatten(deps):
        return [x for d in deps for x in (flatten(d) if isinstance(d, list) else [d])]

    def op(q, fn, deps, s=None, dma=False):
        s = step(dma) if s is None else s
        s["n"] += 1
        flat = flatten(deps)
        for d in flat:
            if isinstance(d, dict):
                d["used"] = True
        ops.append((q, fn, flat, s))
        return s

    def emit():
        know = {q: 0 for q in QS}
        pool = {False: [["e%d" % i, 0, 0] for i in range(NE)], True: [["d%d" % i, 0, 0] for i in range(ND)]}
        for i, (q, fn, deps, s) in enumerate(ops):
            for d in deps:
                if not isinstance(d, dict):
                    QS[q].wait_ge(d[0], d[1])
                elif d["ids"] & ~know[q] or not d["waited"]:
                    QS[q].wait_ge(T.sem[d["sem"]], d["top"])
                    know[q] |= d["know"]
                    d["waited"] = True
            if fn is None:
                continue
            ins = fn()
            if s["used"]:
                w = 16 if s["dma"] else 1
                if "sem" not in s:
                    e = [x for x in pool[s["dma"]] if x[2] >= 0 and not x[2] & ~know[q]][0]
                    pool[s["dma"]].remove(e)
                    pool[s["dma"]].append(e)
                    s.update(sem=e[0], top=e[1] + w * s["n"], left=s["n"], slot=e, waited=False)
                    e[1], e[2] = s["top"], -1
                ins.then_inc(T.sem[s["sem"]], w)
                s["ids"] |= 1 << i
                s["know"] |= know[q] | 1 << i
                s["left"] -= 1
                if not s["left"]:
                    s["slot"][2] = s["ids"]

    def ts(out, i0, s1, op0, s2=None, op1=None, d=(), s=None):
        if op1 is None:
            return op("V", lambda: V.tensor_scalar(out, i0, s1, None, op0), d, s)
        return op("V", lambda: V.tensor_scalar(out, i0, s1, s2, op0, op1), d, s)

    def tt(out, i0, i1, o, d=(), s=None):
        return op("V", lambda: V.tensor_tensor(out, i0, i1, o), d, s)

    def cp(out, i0, d=(), s=None):
        return op("V", lambda: V.tensor_copy(out, i0), d, s)

    def ms(out, c, d=(), s=None):
        return op("V", lambda: V.memset(out, c), d, s)

    def red(out, i0, o, d=(), s=None, ab=False):
        if ab:
            return op("V", lambda: V.tensor_reduce(out, i0, X, o, apply_absolute_value=True), d, s)
        return op("V", lambda: V.tensor_reduce(out, i0, X, o), d, s)

    def scan(out, d0, d1, o1, d=(), s=None, o0=Op.mult, first=0.0):
        return op("V", lambda: V.tensor_tensor_scan(out, d0, d1, first, o0, o1), d, s)

    def tp(out, i0, d=(), s=None):
        return op("V", lambda: V.transpose(out, i0), d, s)

    def qz(q, sc, i0, d=(), s=None):
        return op("V", lambda: V.quantize_mx(q, sc, i0), d, s)

    def act(out, i0, f=AF.Copy, d=(), s=None, **kw):
        return op("A", lambda: A.activation(out, i0, f, **kw), d, s)

    def mm(out, w, ws, x, xs_, d=()):
        return op("P", lambda: PE.matmul_mx(out, w, ws, x, xs_, True, True), d)

    def dma(q, out, i0, d=(), s=None):
        return op(q, lambda: QS[q].dma_start(out, i0), d, s, True)

    def iota(out, pat, base, cm, f=True):
        if f:
            return op("g", lambda: g.iota(out, pat, base, cm, allow_small_or_imprecise_dtypes=True), ())
        return op("g", lambda: g.iota(out, pat, base, cm), ())

    def u8(view):
        return view.bitcast(dt.uint8)

    def u32(view):
        return view.bitcast(dt.uint32)

    others = [r for r in range(N) if r != rank]
    EW = len(topo.engines(core, T.cores[others[0]]))
    nsl, fin = {"sl": 0, "sl2": 0}, []
    hs = helpers(T, topo, rank)
    near = [e for e in topo.engines(core, hs[0]) if e not in topo.engines(core, T.cores[others[0]])]

    def dst(r):
        return address(topo, T.cores[r], core)

    def to_helpers(cs, src, out, sem, d, more=()):
        tr = [RemoteDMATransfer(dst_ids=[address(topo, c, core) for c in cs], dma_engine_mask=sum(1 << e for e in near), remote_sem=sem, srcs=[src], dsts=[out for c in cs])]
        nsl["sl"] += len(near)
        for r, sem2 in more:
            tr.append(RemoteDMATransfer(dst_ids=[dst(r)], dma_engine_mask=int(topo.mask(core, T.cores[r])), remote_sem=sem2, srcs=[src], dsts=[out]))
            nsl["sl"] += EW
        op("g", lambda: g.remote_dma_fused(tr, local_sem=T.sem.sl), d)

    def to_many(rs, src, out, sem, d):
        m = int(topo.mask(core, T.cores[rs[0]]))
        outs = out if isinstance(out, list) else [out for r in rs]
        nsl["sl"] += EW
        op("g", lambda: g.remote_dma_fused([RemoteDMATransfer(dst_ids=[dst(r) for r in rs], dma_engine_mask=m, remote_sem=sem, srcs=[src], dsts=outs)], local_sem=T.sem.sl), d)

    def to_each(pairs, sem, d, wide, left):
        tr, w, e0 = [], EW // 4, 0
        for i, (r, s, o) in enumerate(pairs):
            n = 2 * w if len(pairs) == 3 and i == wide else w
            m = sum(1 << e for e in topo.engines(core, T.cores[r])[e0:e0 + n])
            tr.append(RemoteDMATransfer(dst_ids=[dst(r)], dma_engine_mask=m, remote_sem=sem, srcs=[s], dsts=[o]))
            nsl[left] += n
            e0 += n
        op("g", lambda: g.remote_dma_fused(tr, local_sem=T.sem[left]), d)
        return (T.sem[left], nsl[left])

    mine = [t for t in range(2) if rank in REB[t]][0]
    I = REB[mine].index(rank)
    peers = [r for r in REB[mine] if r != rank]
    s8 = NK * I
    la, ls, od, os_, h, nq, ns = (T["%s%d" % (n, mine)] for n in ("la", "ls", "or", "os", "h", "nq", "ns"))
    x0 = 64 * (I & 1) if mine == 0 else 0
    dzc, dz0, dz1, dzr, seg = T.dz[:, 0:192], T.dz[:, 193:273], T.dz[:, 273:465], T.dz[:, 465:529], T.dz[:, 529:657]
    rr, hz = T.irow[:, 0:8], T.hz[:, 0:512]
    p8, p16, p32, q1, pf, hp, pd = (T.cf[:, i:i + 1] for i in range(7))

    e_u = dma("A", T.ut[:, 8:16], T.u[:, 0:8])
    e_tb = dma("S", T.tbt[:, 0:512], T.tb[:, 0:512])
    i_pi = iota(T.pi[:], [[N - rank, 2], [1, 2]], 0, 1, False)
    i_ir = iota(T.irow[:], [[1, P]], 0, 0)
    i_tl = iota(T.tl[:], [[0, 8], [-1, 8]], 7, 0)
    i_tq = iota(T.tq[:], [[1, 8], [0, 8]], 0, 0)
    z_hz = ms(T.hz[:], 0.0)
    z_ut = ms(T.ut[:, 16:512], 0.0)
    ms(T.ut[:, 0:8], 0.0, s=z_ut)
    k1 = ts(T.pj[:, 0:1], T.pi[:, 0:1], 7, Op.bitwise_and, d=[i_pi])
    ts(T.pj[:, 1:2], T.pi[:, 0:1], 15, Op.bitwise_and, s=k1)
    ts(T.pj[:, 2:3], T.pi[:, 0:1], 31, Op.bitwise_and, s=k1)
    ts(T.pj[:, 3:4], T.pi[:, 1:2], 7, Op.bitwise_and, s=k1)
    ts(T.pj[:, 5:6], T.pi[:, 0:1], 2, Op.arith_shift_right, 4, Op.bitwise_and, s=k1)
    ts(T.pj[:, 6:7], T.pi[:, 2:3], 7, Op.bitwise_and, s=k1)
    cp(T.pj[:, 4:5], T.pi[:, 0:1], s=k1)
    e_uq = qz(T.uq[:], T.uqs[:], T.ut[:], [z_ut, e_u])
    k2 = cp(T.cf[:, 0:7], T.pj[:, 0:7], [k1])
    z_eb = act(T.eb[:], T.hz[:], d=[z_hz])
    z_dz = act(T.dz[:, 0:273], T.hz[:, 0:273], AF.Identity, bias=1.0)
    e_tb2 = act(T.tbt[:, 512:544], T.tbt[:, 0:32], d=[e_tb])
    act(T.dz[:, 273:657], T.hz[:, 0:384], AF.Identity, s=z_dz, bias=1.0)
    z_na = act(T.na[:], T.hz[:, 0:16])
    i_eb = op("g", lambda: g.affine_select(T.eb[:, 3:515:4], T.hz[:, 0:P], [[-1, P]], Op.not_equal, 1.0, 0, 1), [z_eb])
    e_t0 = qz(T.t0[:], T.t0s[:], T.tbt[:, 0:512], [e_tb])
    m0 = mm(T.ps[:, 0:128], T.t0[:], T.t0s[:], T.uq[:], T.uqs[:], [e_uq, e_t0])
    e_la = qz(la[:, 160:288], ls[:, 160:288], hz, [z_hz])
    e_c = cp(T.ck[:, 0:4], T.ps[:, 0:4], [m0])
    rs = sorted(others, key=lambda r: r in REB[0])
    to_many(rs, T.ck[:, 2:4], ring(T.ck, rank, rs), T.sem.s_ck, [e_c])
    e_tr = qz(T.tr[:], T.trs[:], T.tbt[:, 4 * rank:4 * rank + 512], [e_tb2])
    m1 = mm(T.ps[:, 512:640], T.tr[:], T.trs[:], T.uq[:], T.uqs[:], [e_tr])
    k5 = ts(T.m32[:, 0:8], rr, p8, Op.not_equal, d=[k2, i_ir])
    ts(T.m32[:, 8:16], rr, p8, Op.not_equal, -1.0, Op.mult, s=k5)
    k4 = ts(T.m32[:, 16:24], rr, p8, Op.is_equal)
    e_c1 = cp(T.cn[:, 0:4], T.ps[:, 512:516], [m1])
    to_helpers(hs, T.cn[:, 2:4], T.cn[:, 2:4], T.sem.s_f0, [e_c1])
    i_16 = iota(T.i16[:], [[0, 8], [1, 16]], 0, 0)
    i_v0 = iota(T.val[:, 0:32], [[2, K]], 19, 0)
    i_v1 = iota(T.val[:, 32:64], [[1, K]], 160, 0)
    i_p8 = iota(T.cf[:, 8:9], [[0, 1]], 7, 8)
    i_pn = iota(T.cf[:, 9:10], [[0, 1]], 64, -1)
    i_rp = iota(T.rp[:, 40:48], [[1, 2], [8, 2], [0, 2]], 0, 0)
    i_sz = [iota(T.rp[:, 56:64], [[16, 8]], P - rank, 0), iota(T.val[:, 64:96], [[1, K]], P, 0), iota(T.sz[:, 0:512], [[1, 64], [0, 8]], 0, 0)]

    k3 = act(T.w16[:, 24:32], rr, AF.Identity, [i_ir, k2], scale=-W8, bias=8 * W8)
    act(T.w16[:, 32:40], rr, AF.Identity, s=k3, scale=W8, bias=-8 * W8)
    act(T.w16[:, 0:18:17], T.hz[:, 0:2], s=k3)
    k_g = act(T.gg[:, 129:192], T.hz[:, 0:63], AF.Identity, bias=-PITCH)
    k_c = act(T.cf[:, 10:11], p8, AF.Identity, bias=-1.0)
    k_a = act(T.xs[:, 128:129], T.dz[:, 0:1], d=[z_dz], scale=-TINY)
    act(T.xs[:, 129:192], T.hz[:, 0:63], s=k_a)
    act(T.lw[:, 39:40], T.dz[:, 0:1], s=k_a, scale=-8.0)
    act(T.gg[:, 128:129], pf, AF.Identity, s=k_a, bias=1.0 - 4.5 / 8)
    act(T.gg[:, 144:177:32], T.dz[:, 0:2], d=[k_g], s=k_a, scale=15 * PITCH)
    act(T.dz[:, 128:129], T.dz[:, 0:1], s=k_a, scale=PITCH)
    act(T.dz[:, 201:242:40], T.dz[:, 0:2], s=k_a, scale=-1.0)
    k_b = act(T.dz[:, 289:434:144], T.dz[:, 0:2], scale=-1.0)
    act(T.dz[:, 465:529:8], T.hz[:, 0:8], s=k_b)
    act(T.w40[:, 0:41:40], T.hz[:, 0:2], s=k_b)
    act(T.dz[:, 466:529:8], T.dz[:, 0:8], s=k_b, scale=-1.0)
    act(T.dz[:, 529:657:16], T.hz[:, 0:8], s=k_b)

    ts(T.m32[:, 24:32], rr, p8, Op.not_equal, s=k4)
    ts(T.co[:, 0:1], pd, 2.0, Op.mult, 3.0, Op.add, s=k4)
    ts(T.co[:, 1:2], pd, 2.0, Op.mult, 2.0, Op.add, s=k4)
    k6 = tt(T.w16[:, 1:17], T.w16[:, 24:40], T.m32[:, 0:16], Op.mult, [k3, k5])
    ts(T.fac[:], T.irow[:, 0:33], p32, Op.is_ge, LESS, Op.max, s=k4)
    tt(T.dw[:, 0:17], T.w16[:, 0:17], T.w16[:, 1:18], Op.subtract, [k6], k4)

    e_eq = step()

    def unpacker(b):
        qz(T.eq[:, 128 * b:128 * b + 128], T.eqs[:, 128 * b:128 * b + 128], T.eb[:, 3 - b:515 - b], [i_eb], e_eq)
    a = ts(T.cf[:, 11:12], p8, 0.0, Op.is_equal)
    b = ts(T.to[:, 64:128], T.tq[:], T.cf[:, 10:11], Op.is_le, T.cf[:, 10:11], Op.add, d=[k_c, i_tq])
    e_or = qz(od[:], os_[:], hz)
    ts(T.to[:, 128:192], T.tq[:], T.cf[:, 11:12], Op.mult, d=[a], s=b)
    unpacker(0)
    c = tt(T.to[:, 192:256], T.to[:, 64:128], T.to[:, 128:192], Op.max, [b])
    unpacker(1)
    a = tt(T.to[:, 64:128], T.to[:, 192:256], T.tl[:], Op.is_equal, [c, i_tl])
    b = act(T.to[:, 128:192], T.to[:, 192:256], AF.Identity, [c], scale=8.0, bias=32.0)
    ts(T.to[:, 320:384], T.to[:, 192:256], float(rank), Op.not_equal, 1000.0, Op.mult, s=b)
    unpacker(2)
    c = act(T.to[:, 256:320], T.to[:, 64:128], d=[a], scale=128.0)
    tt(T.to[:, 384:448], T.to[:, 320:384], T.to[:, 128:192], Op.min, [b], c)
    unpacker(3)
    k_r = [tt(T.to[:, 0:64], T.to[:, 256:320], T.to[:, 384:448], Op.max, [c]), e_or, e_eq]
    if mine == 0:
        k_h = act(h[:, 256 - 4 * x0:512 - 4 * x0], T.hz[:, 0:256])
        k_u2 = step()
        for n in range(1, 4):
            act(T.ut[:, 128 * n + 8:128 * n + 16], T.ut[:, 8:16], d=[e_uq], s=k_u2)

    k_m, k_mk, k_l = step(), step(), step()
    small = [
        lambda: ts(T.cf[:, 12:13], p16, 8.0, Op.is_ge, -1000.0, Op.mult, s=k_m),
        lambda: ts(T.cf[:, 13:14], p16, 8.0, Op.is_lt, -1000.0, Op.mult, s=k_m),
        lambda: ms(T.mk[:], 0.0, s=k_m),
        lambda: ts(T.co[:, 4:12], T.rp[:, 40:48], hp, Op.add, d=[i_rp], s=k_l),
        lambda: ts(T.mk[:, s8:s8 + 8:2], T.irow[:, 0:8:2], T.cf[:, 12:13], Op.add, d=[k_m], s=k_mk),
        lambda: ts(T.mk[:, s8 + 1:s8 + 8:2], T.irow[:, 1:8:2], T.cf[:, 13:14], Op.add, s=k_mk),
        lambda: ts(T.co[:, 2:3], p8, 8.0, Op.mult, x0 + 7.0, Op.add, s=k_l),
    ]

    def order(t, e_s, s_col, s_rep, gv, n, steps, e_v, before, fill, late):
        sr, ar, thr, yo, yb, sm, of = (T["%s%d" % (x, t)] for x in ("sr", "ar", "thr", "yo", "yb", "sm", "of"))
        fill = list(fill)

        def slot():
            if fill:
                fill.pop(0)()
        l0 = red(sm[:, 6:7], gv, Op.max, [e_v])
        e_th = act(thr[:], T.fac[:], AF.Abs, [e_s, k4], scale=s_col)
        e_tp = tp(sr[:], s_rep, [e_s])
        l1 = ts(T.lw[:, 39 - n:39], gv, sm[:, 6:7], Op.not_equal, -8.0, Op.mult, d=[l0, before])
        sz = step()

        def size(p0, p1, c, q0, q1_, d=()):
            tt(ar[p0:p1, c:c + 32], sr[q0:q1_, 0:32], sr[q0:q1_, 32:64], Op.max, d, sz)
        size(0, 128, 0, 0, 128, [e_tp])
        size(64, 128, 64, 0, 64)
        size(96, 128, 32, 0, 32)
        for b in range(1, 4):
            size(32 * b, 32 * b + 32, 96, 32 * b - 32, 32 * b)
        act(ar[0:64, 64:96], sr[64:128, 0:32], AF.Abs, [e_tp], sz, scale=LESS)
        act(ar[0:32, 96:128], sr[96:128, 0:32], AF.Abs, s=sz, scale=LESS)
        for b in range(3):
            act(ar[32 * b:32 * b + 32, 32:64], sr[32 * b + 32:32 * b + 64, 0:32], AF.Abs, s=sz, scale=LESS)
        l3 = scan(T.lw[:, 48:49 + n], steps, T.lw[:, 39 - n:40], Op.max, [l1, k_a, before], o0=Op.add, first=-8.0)
        e_gt = ts(T.gg[:, 32:128], ar[:, 32:128], thr[:, 32:33], Op.is_ge, d=[sz, e_th, before])
        tt(T.gg[:, 0:32], ar[:, 0:32], thr[:, 0:32], Op.is_gt, s=e_gt)
        slot()
        late()
        e_y = scan(yo[:], dzc, T.gg[:], Op.add, [e_gt, l3, k_a], first=T.lw[:, 48 + n:49 + n])
        slot()
        e_t2 = tp(yb[0:64, 32:96], yo[64:128, 128:192], [e_y])
        tp(yb[0:64, 0:32], yo[0:64, 128:160], s=e_t2)
        tp(yb[0:64, 96:128], yo[0:64, 160:192], s=e_t2)
        slot()
        e_z = red(sm[0:64, 0:1], yb[0:64, 0:64], Op.min, [e_t2], ab=True)
        red(sm[0:64, 1:2], yb[0:64, 64:128], Op.min, s=e_z, ab=True)
        slot()
        e_wv = step()
        for b in range(2):
            tt(sm[32 * b:32 * b + 32, 4:6], sm[0:32, 0:2], sm[32:64, 0:2], Op.min, [e_z], e_wv)
        w, e_of = sm[:, 4:6], step()
        for b in range(2):
            ts(of[64 * b:64 * b + 64, 0:2], sm[0:64, 4:6], RND - 1.0, Op.add, RND, Op.subtract, d=[e_wv], s=e_of)
        ci = T["ci%d" % t]
        c0 = cp(sm[64:128, 4:6], sm[0:64, 4:6])
        tab, tabs = (T.t0, T.t0s) if t == 0 else (T.tr, T.trs)
        sc, ss, lt, lst = (T["%s%d" % (x, t)] for x in ("sc", "ss", "la", "ls"))
        e_sc = cp(u32(sc[:]), u32(tab[:]).indirect(of[:, 0:2]), [e_of])
        e_ss = act(ss[:], tabs[:].indirect(of[:, 0:2]), d=[e_of])
        sl, left = slice(64 + NK * rank, 64 + NK * rank + NK), "sl2" if t else "sl"
        to_each([(r, u8(sc[:, NK * i:NK * i + NK]), u8(lt[:, sl])) for i, r in enumerate(REB[t]) if r != rank], T.sem["s_la%d" % t], [e_sc], 0, left)
        gone = to_each([(r, ss[:, NK * i:NK * i + NK], lst[:, sl]) for i, r in enumerate(REB[t]) if r != rank], T.sem["s_la%d" % t], [e_ss], 2, left)
        c1 = ts(ci[:, 0:2], w, 8.0, Op.mult, 8.0 * t - 4.5, Op.add, d=[c0])
        e_cd = ts(of[:, 2:4], w, 8.0, Op.mult, 8.0 * rank * t - 4.5, Op.add)
        c2 = ts(ci[:, 2:4], ci[:, 0:2], 63, Op.bitwise_and, d=[c1])
        slot()
        e_c64 = cp(of[:, 4:6], ci[:, 2:4], [c2])
        slot()
        slot()
        own = []
        if t == mine:
            own = [cp(u32(lt[:, 32 - s8:64 - s8]), u32(tab[:]).indirect(of[:, 0:2])), act(lst[:, 32 - s8:64 - s8], tabs[:].indirect(of[:, 0:2]))]
        bsb = T["bsb%d" % t]
        e_b = act(bsb[:, 0:32], T.irow[:].indirect(of[:, 0:2]), d=[i_ir])
        act(bsb[:, 32:64], T.tl[:].indirect(of[:, 4:6]), d=[e_c64, i_tl], s=e_b)
        fin.append(dma("S", T.bs[2 * t:2 * t + 2, 0:32], bsb[0:1, 0:64], [e_b]))
        return own, e_of, e_cd, e_c64, e_b, e_y, gone

    def rebuild_list(t, e_c64, e_of, d):
        rl, of, ol = T["rl%d" % t], T["of%d" % t], T["ol%d" % t]
        s = s8
        a = tt(rl[:, 0:32], T.to[:, 0:64].indirect(of[:, 4:6]), T.mk[:, 0:32], Op.add, [e_c64, d])
        if t:
            tt(rl[:, 32:64], T.sub[:].indirect(of[:, 0:2]), T.mk[:, 32:64], Op.add, [e_of], a)
            a = tt(rl[:, 64:72], rl[:, s:s + 8], rl[:, 32 + s:40 + s], Op.max, [a])
            s = 64
        a = tt(rl[:, 72:76], rl[:, s:s + 8:2], rl[:, s + 1:s + 8:2], Op.max, [a])
        return cp(ol[:], rl[:, 72:76], [a])

    def unpack(t, d):
        ol = T["ol%d" % t]
        wide = [[x for x in REB[t] if x != r].index(rank) != 1 for r in REB[t] if r != rank]
        arr = (T.sem["s_la%d" % t], (14 + sum(wide)) * (EW // 4))
        e_oc = cp(u32(od[:, 0:64]), u32(la[:, 32:168]).indirect(ol[:]), [d, arr])
        e_os = act(os_[:, 0:64], ls[:, 32:168].indirect(ol[:]), d=[d, arr])
        return [mm(T.da[:, 512 * b:512 * b + 128], T.eq[:, 128 * b:128 * b + 128], T.eqs[:, 128 * b:128 * b + 128], od[:], os_[:], [d, e_oc, e_os]) for b in range(4)]

    def lookup(c, tab, keys, d):
        a = tt(T.gs[:, c:c + 128], tab[:].indirect(keys), T.dg[:], Op.mult, d)
        return lambda: scan(T.gs[:, c + 128:c + 256], seg, T.gs[:, c:c + 128], Op.max, [a, k_b])

    def old_places(d):
        w = T.sm0[:, 4:6]
        a = ts(T.ofx[:, 0:2], w, rank + 0.5, Op.is_lt, 128.0, Op.mult)
        a = tt(T.ofx[:, 2:4], T.ofx[:, 0:2], w, Op.add, [a])
        a = ts(T.o1[:, 8:10], T.ofx[:, 2:4], 8.0, Op.mult, -4.5, Op.add, d=[a])
        return cp(T.sz[:].indirect(T.o1[:, 8:10]), T.val[:, 64:96], [a, d])

    s_ck = (T.sem.s_ck, 7 * EW)
    e_x = tt(T.xs[:, 96:128], T.ck[:].indirect(T.co[:, 0:2]), T.m32[:], Op.mult, [k5, k4, z_na, e_c, s_ck])
    e_w = dma("S", T.wt[:], T.w[:, 0:512], [e_x])
    small.pop(0)()
    k_s = step()

    def clear():
        act(T.sa[:, 0:512], hz, s=k_s)
        act(T.sa[:, 512:1024], hz, s=k_s)
    e_s = scan(T.so[:, 0:80], dz0, T.xs[:, 112:192], Op.subtract, [e_x, k_a])
    own, e_of, e_cd, e_c64, e_b, e_y0, _ = order(0, e_s, T.so[:, 16:17], T.so[:, 16:80], T.xs[:, 96:112], 16, T.dw[:, 0:17], e_x, [], small, clear)
    i_sz += [iota(T.sz[:, 512:1024], [[1, 64], [0, 8]], 64, 0), iota(T.sz[:, 1024:1088], [[1, 8], [0, 8]], 0, 0)]
    if mine == 0:
        e_ol = rebuild_list(0, e_c64, e_of, [k_r, k_mk])
        e_u2 = qz(T.u2[:], T.u2s[:], T.ut[:], [k_u2])
    a = ts(T.rp[:, 8:15], T.irow[:, 0:7], q1, Op.is_ge)
    ts(T.rp[:, 16:23], T.irow[:, 0:7], q1, Op.is_lt, s=a)
    b = cp(T.rp[:, 0:1], q1)
    k_d = ts(T.dg[:], T.i16[:], p16, Op.is_equal, d=[i_16])
    tt(T.rp[:, 1:8], T.rp[:, 8:15], T.irow[:, 0:7], Op.add, [a], b)
    e_sa = cp(T.sa[:].indirect(T.of0[:, 2:4]), T.val[:, 0:32], [e_cd, i_v0, k_s])
    bsb, hit = T.bsb0, T.hit
    c = ts(T.ki[:, 0:8], T.rp[:, 0:8], 7.0, Op.mult, T.cf[:, 8:9], Op.add, d=[b, i_p8])
    ts(T.ki[:, 8:16], T.rp[:, 0:8], 128.0, Op.mult, 128.0 * (N - rank), Op.add, s=c)
    k_k = act(T.rp[:, 32:39], T.rp[:, 1:8], AF.Identity, [b], scale=-W8, bias=8 * W8)
    h0 = tt(hit[:, 0:32], bsb[:, 0:32], bsb[:, 32:64], Op.subtract, [e_b])
    c = ts(T.ki[:, 24:40], T.ki[:, 0:16], 1023, Op.bitwise_and, d=[c])
    h2 = ts(hit[:, 96:128], bsb[:, 32:64], q1, Op.not_equal)
    cp(T.ku[:, 0:8], T.ki[:, 24:32], [c], k_k)
    ts(T.rp[:, 24:32], T.ki[:, 32:40], 1.0 / 64, Op.mult, 2.0, Op.add, s=k_k)
    h1 = act(hit[:, 32:64], hit[:, 0:32], AF.Abs, [h0, i_pn], bias=T.cf[:, 9:10])
    h4 = act(hit[:, 128:160], bsb[:, 32:64], AF.Identity, [e_b], scale=-W8, bias=8 * W8)
    e_no = []
    if mine == 0:
        ds = unpack(0, [e_ol, e_la, k_r, own])
        e_h = step()
        for b in range(4):
            scan(h[:, 4 * x0 + b:4 * x0 + 256:4], dzr, T.da[:, 512 * b:512 * b + 64], Op.subtract, [ds[b], k_h, k_b], e_h)
        e_nq = qz(nq[:], ns[:], h[:], [e_h])
        m2 = mm(T.ps[:, 1024:1152], T.u2[:], T.u2s[:], nq[:], ns[:], [e_nq, e_u2])
        e_sn = cp(u32(T.sn[:]), u32(nq[:]).indirect(T.co[:, 2:3]), [e_nq, k_l])
        e_sns = act(T.sns[:], ns[:].indirect(T.co[:, 2:3]), d=[e_nq, k_l])
        e_tk = tp(T.tk[:], T.ps[:, 1027:1152:4], [m2])
        to_many(peers + list(REB[1]), T.tk[:, 2:4], T.na[:, 4 * I:4 * I + 2], T.sem.s_na, [e_tk])
        to_helpers(hs[0:1], u8(T.sn[:, 0:NK]), u8(T.sn[:, 0:NK]), T.sem.s_f1, [e_sn])
        to_helpers(hs[1:2], T.sns[:, 0:NK], T.sns[:, 0:NK], T.sem.s_f1, [e_sns])
        e_no = [cp(T.na[:, 4 * I:4 * I + 2], T.tk[:, 2:4], [e_tk])]
    fn = lookup(0, T.sa, T.ku[:, 0:8], [e_sa, k_d, k_k])
    ts(hit[:, 64:96], hit[:, 32:64], 64.0, Op.is_equal, d=[h1], s=h2)
    b = fn()
    h3 = tt(hit[:, 160:192], hit[:, 64:96], hit[:, 96:128], Op.mult, [h2])
    sub = T.gs[:, 143:256:16]
    c = tt(T.ofx[:, 40:48], sub, T.rp[:, 24:32], Op.max, [b])
    ts(T.rp[:, 48:55], T.gs[:, 159:256:16], 1.0, Op.is_lt, s=c)
    e_w4 = tt(T.w40[:, 8:40], hit[:, 160:192], hit[:, 128:160], Op.mult, [h3, h4])
    e_o1 = cp(T.o1[:, 0:8], T.ofx[:, 40:48], [c])
    tt(T.w40[:, 1:8], T.rp[:, 32:39], T.rp[:, 48:55], Op.mult, s=e_w4)
    if mine == 1:
        k_h = act(h[:], hz)
        e_tw = [qz(T.tw[:, 0:128], T.tws[:, 0:128], T.tbt[:, 0:512]), qz(T.tw[:, 160:288], T.tws[:, 160:288], hz)]
        k_m2 = ts(T.mk[:, 32 + s8:40 + s8:2], T.hz[:, 0:4], T.cf[:, 12:13], Op.add, d=[k_mk])
        ts(T.mk[:, 33 + s8:40 + s8:2], T.hz[:, 0:4], T.cf[:, 13:14], Op.add, s=k_m2)
        c = ts(T.rl0[:, 0:8], sub, 0.5, Op.mult, 86.5, Op.add)
        ts(T.rl0[:, 8:16], sub, 100.0, Op.mult, s=c)
        c2 = step()
        for n in range(4):
            tt(T.st[:, 8 * n:8 * n + 8], T.rl0[:, 0:8], T.rl0[:, 8:16], Op.min, [c], c2)
        c = tp(T.st[:, 32:64], T.st[:, 0:32], [c2])
        e_sub = step()
        for n in range(4):
            for m in range(4):
                (cp if m < 1 else act)(T.sub[32 * n:32 * n + 32, 32 * m:32 * m + 32], T.st[32 * m:32 * m + 32, 32:64], d=[c], s=e_sub)
        e_v1 = ts(T.val[:, 32 + s8:40 + s8], rr, 192.0, Op.add, d=[i_v1, e_tw])
        e_s0 = old_places(i_sz)
        s_nb = (T.sem.s_nb, 8 * EW)
    e_ag = act(T.ag[:, rank:8], T.cn[:, 3:19 - 2 * rank:2], AF.Abs, [e_c1, (T.sem.s_cn, 7 * EW)])
    if rank:
        act(T.ag[:, 0:rank], T.cn[:, 19 - 2 * rank:18:2], AF.Abs, s=e_ag)
    g1 = tt(T.ag[:, 8:15], T.ag[:, 0:7], T.rp[:, 16:23], Op.mult, [e_ag])
    tt(T.ag[:, 16:23], T.ag[:, 1:8], T.rp[:, 8:15], Op.mult, s=g1)
    e_dw = tt(T.dw[:, 24:64], T.w40[:, 0:40], T.w40[:, 1:41], Op.subtract, [e_w4, k_b])
    g2 = tt(T.ag[:, 24:31], T.ag[:, 8:15], T.ag[:, 16:23], Op.add, [g1])

    s_na = (T.sem.s_na, EW * (3 if mine == 0 else 4))
    r0 = cp(T.rc[:, 0:64], T.na[:].indirect(T.co[:, 4:8]), [k_l, e_no, s_na])
    r1 = act(T.rc[:, 64:128], T.na[:].indirect(T.co[:, 8:12]), AF.Abs, [k_l, z_na, e_no, s_na])
    e_gv = tt(T.gv[:, 0:7], T.ag[:, 24:31], T.rp[:, 48:55], Op.mult, [g2])
    r2 = tp(T.cn[:, 18:82], T.rc[:, 0:64], [r0])
    r3 = tp(T.ng[:], T.rc[:, 64:128], [r1])
    e_x = tt(T.xs[:, 0:128], T.cn[:].indirect(T.o1[:, 0:8]), T.dg[:], Op.mult, [r2, e_o1])
    r4 = tt(T.gv[:, 7:39], T.ng[:, 1:64:2], hit[:, 160:192], Op.mult, [r3, h3])
    e_s = scan(T.so[:], dz1, T.xs[:], Op.subtract, [e_x, k_b])
    own, e_of, e_cd, e_c64, e_b, e_y1, gone = order(1, e_s, T.so[:, 128:129], T.so[:, 128:192], T.gv[:, 0:39], 39, T.dw[:, 24:64], [r4, e_gv], [e_y0, e_dw], [], lambda: None)
    sl = slice(160 + s8, 160 + s8 + NK)
    if mine == 0:
        s0 = slice(P + s8, P + s8 + NK)
        new0 = [dma("S", u8(T.tw[:, s0]), u8(T.sn[:, 0:NK]), [e_sn, gone]), dma("S", T.tws[:, s0], T.sns[:, 0:NK], [e_sns]), (T.sem.s_nb, 6 * EW)]
        new1 = [(T.sem.s_nw, 8 * EW)]
        e_v1 = i_v1
        e_s0 = old_places(i_sz)
    else:
        new0 = [dma("S", u8(T.tw[:, 128:160]), u8(T.la1[:, 128:160]), [s_nb, gone]), dma("S", T.tws[:, 128:160], T.ls1[:, 128:160])]
        e_ol = rebuild_list(1, e_c64, e_of, [k_r, k_mk, k_m2, e_sub])
    e_sz = cp(T.sz[:].indirect(T.of1[:, 2:4]), T.val[:, 32:64], [e_cd, e_v1, e_s0])
    if mine == 1:
        ds = unpack(1, [e_ol, e_la, k_r, own, s_nb])
        scans = [scan(T.sb[:, 64 * b:64 * b + 64], dzr, T.da[:, 512 * b:512 * b + 64], Op.subtract, [ds[b], k_b]) for b in range(4)]
        e_h = step()
        for b in range(3):
            act(h[:, b:4 * NK:4], T.sb[:, 64 * b + 7:64 * b + 64:8], d=[scans[b], k_h], s=e_h)
        cp(h[:, 3:4 * NK:4], T.sb[:, 199:256:8], [scans[3], k_h], e_h)
        e_nq = qz(nq[:], ns[:], h[:], [e_h])
        to_helpers(hs, ns[:, 0:NK], T.tws[:, sl], T.sem.s_f1, [e_nq], [(others[0], T.sem.s_nw)])
        to_many(others, u8(nq[:, 0:NK]), u8(T.tw[:, sl]), T.sem.s_nw, [])
        new1 = [qz(T.tw[:, 192:320], T.tws[:, 192:320], h[:]), (T.sem.s_nw, 6 * EW)]
    c = ts(T.ki[:, 16:24], T.rp[:, 56:64], p16, Op.add, 8.0, Op.mult)
    e_wq = qz(T.wq[:], T.wqs[:], T.wt[:], [e_w])
    c = ts(T.ki[:, 40:48], T.ki[:, 16:24], 1023, Op.bitwise_and, d=[c])
    if mine == 0:
        e_tw = qz(T.tw[:, 0:128], T.tws[:, 0:128], T.tbt[:, 0:512])
    c = ts(T.ku[:, 8:16], T.ki[:, 40:48], 7.0 * rank + 7, Op.add, d=[c])
    e_oi = cp(T.oi[:], T.gs[:, 256 + 143:512:16], [lookup(256, T.sz, T.ku[:, 8:16], [e_sz, c])()])

    ye = 192 + NK * mine
    m3 = mm(T.ps[:, 0:160], T.wq[:], T.wqs[:], T.tw[:, 0:160], T.tws[:, 0:160], [e_wq, e_tw, new0])
    y0 = act(T.yw[:, 0:160], T.ps[:, 0:160], d=[m3])
    m4 = mm(T.ps[:, 1536:1664], T.wq[:], T.wqs[:], T.tw[:, ye - 128:ye], T.tws[:, ye - 128:ye], [new1])
    p1 = cp(u32(T.t2[:]), u32(T.tw[:, 0:200]).indirect(T.oi[:]), [e_oi, e_tw, new0, new1])
    p2 = act(T.t2s[:], T.tws[:, 0:200].indirect(T.oi[:]), d=[e_oi, e_tw, new0, new1])
    fin.append(dma("S", T.oc[:, 0:512], u8(T.t2[:]), [p1]))
    e_os = step(True)
    for k in range(2):
        dma("S", T.osc[4 * k:4 * k + 4, 0:128], T.t2s[32 * k:32 * k + 4, 0:128], [p2], e_os)
    y1 = cp(T.yw[:, 160:ye], T.ps[:, 1824 - ye:1664], [m4])
    e_yc = cp(T.ysb[:, 0:64], T.yw[:, 0:ye].indirect(T.oi[:, 0:4]), [y0, y1])
    act(T.ysb[:, 64:128], T.yw[:, 0:ye].indirect(T.oi[:, 4:8]), d=[y0, y1], s=e_yc)
    for k in range(2, 4):
        dma("A", T.osc[4 * k:4 * k + 4, 0:128], T.t2s[32 * k:32 * k + 4, 0:128], [p2], e_os)
    fin.append(dma("S", T.y[:, 0:128], T.ysb[:], [e_yc]))
    op("g", None, [(T.sem.sl, nsl["sl"]), fin, e_os])
    emit()
